import numpy as np
import ml_dtypes


def mxq(x, axis, fmt="e4m3"):
    dtype, down = {"e4m3": (ml_dtypes.float8_e4m3fn, 7), "e5m2": (ml_dtypes.float8_e5m2, 14)}[fmt]
    v = np.moveaxis(np.asarray(x, np.float32).astype(ml_dtypes.bfloat16).astype(np.float64), axis, -1)
    blocks = v.reshape(v.shape[:-1] + (-1, 32))
    amax = np.abs(blocks).max(-1, keepdims=True)
    byte = np.maximum(np.where(amax > 0, np.frexp(amax)[1] - 1 + 127, 0) - down, 1)
    scale = np.exp2(byte - 127.0)
    codes = (blocks / scale).astype(np.float32).astype(dtype).astype(np.float64)
    return np.moveaxis((codes * scale).reshape(v.shape), -1, axis)


WIDE = False


def mx_kscale(k):
    if not WIDE:
        return np.ones(k)
    levels = np.array([18, -18])
    if k % 512:
        return np.exp2(np.random.permutation(np.resize(levels, k // 32))).repeat(32)
    a = np.empty((k // 512, 16))
    for p in range(k // 512):
        a[p, :8] = np.random.permutation(np.resize(levels, 8))
        for g in range(8):
            far = levels[np.abs(levels - a[p, g]) >= 10]
            a[p, g + 8] = far[np.random.randint(len(far))]
    return np.exp2(a.ravel()).repeat(32)


def f64(x):
    return np.asarray(x).astype(np.float64)


def striped(idx):
    return np.tile(np.asarray(idx).reshape(-1, 16).T, (8, 1)).astype(np.uint16)


def unstriped(offs):
    return offs[:16].T.reshape(-1).astype(np.int64)


B, N, T, D, R = 2, 512, 2048, 512, 512


def setup_inputs():
    n = np.random.standard_normal
    idx = np.random.permutation(T)[:B * N]
    s = mx_kscale(D)[:, None]
    z = mx_kscale(R)[:, None]
    x = n((B, D, R))
    return {
        "xT": (x * s).astype(np.float32),
        "wT": (n((D, T)) * (1.00 / np.sqrt(D)) / s).astype(np.float32),
        "y": np.random.randint(0, 2, (B, R, N)).astype(np.float32),
        "wt": (np.random.uniform(0.5, 1.5, (B, R, 1)) * 1.0 / np.sqrt(R) * z).astype(np.float32),
        "xm": (x.transpose(0, 2, 1) / z).astype(np.float32),
        "offs": striped(idx),
    }


def reference(xT, wT, y, wt, xm, offs):
    idx = unstriped(offs)
    pick = lambda x: x[:, idx].reshape(x.shape[0], B, N).transpose(1, 0, 2)
    a = mxq(f64(xT), 1, "e4m3").transpose(0, 2, 1) @ mxq(pick(f64(wT)), 1, "e4m3")
    p = 1.0 / (1.0 + np.exp(-a))
    g = f64(wt) * (p - f64(y)) * p * (1.0 - p)
    dw = mxq(f64(xm), 1, "e4m3").transpose(0, 2, 1) @ mxq(g, 1, "e5m2")
    gw = np.zeros((D, T))
    gw[:, idx] = dw.transpose(1, 0, 2).reshape(D, B * N)
    return gw

@@ -1,0 +1,208 @@
+from contextlib import ExitStack
+
+import concourse.mybir as mybir
+
+B, N, T, D, R = 2, 512, 2048, 512, 512
+FLOPS = 2 * 2 * B * R * D * N
+
+F32 = mybir.dt.float32
+BF16 = mybir.dt.bfloat16
+U32 = mybir.dt.uint32
+U16 = mybir.dt.uint16
+U8 = mybir.dt.uint8
+E4M3 = mybir.dt.float8_e4m3fn_x4
+E5M2 = mybir.dt.float8_e5m2_x4
+ACT = mybir.ActivationFunctionType
+ALU = mybir.AluOpType
+
+P = 128
+PACK = 4
+HALF = N // 2
+LIST_COLS = N // 16
+
+
+def tile_attend_gsl2_w_kernel(tc, xT, wT, y, wt, xm, offs, out):
+    nc = tc.nc
+    with ExitStack() as ctx:
+        keep = ctx.enter_context(tc.tile_pool(name="keep", bufs=1))
+        psum = ctx.enter_context(tc.psum_pool(name="psum", bufs=1))
+
+        def tile(shape, dtype, name):
+            return keep.tile(shape, dtype, name=name, align_bytes=64)
+
+        offsets = keep.tile([P, B * LIST_COLS], U16, name="offsets")
+        nc.sync.dma_start(offsets[:], offs)
+
+        planes = [tile([P, T], F32, f"plane{j}") for j in range(PACK)]
+        xT_raw = [tile([P, PACK, R], F32, f"xT_raw{b}") for b in range(B)]
+        xm_raw = [tile([P, PACK, D], F32, f"xm_raw{b}") for b in range(B)]
+        y_sb = [tile([P, PACK, N], F32, f"y{b}") for b in range(B)]
+        wt_sb = tile([P, B, PACK], F32, "wt_sb")
+        w_rows = wT.rearrange("(p j) c -> p j c", j=PACK)
+
+        def load(dst, src):
+            nc.sync.dma_start(out=dst[:], in_=src.rearrange("(p j) w -> p j w", j=PACK))
+
+        nc.sync.dma_start(out=planes[0][:], in_=w_rows[:, 0, :])
+        nc.sync.dma_start(out=wt_sb[:], in_=wt.rearrange("b (p t) o -> p b (t o)", t=PACK))
+        nc.sync.dma_start(out=planes[1][:], in_=w_rows[:, 1, :])
+        nc.sync.dma_start(out=planes[2][:], in_=w_rows[:, 2, :])
+        load(xT_raw[0], xT[0])
+        nc.sync.dma_start(out=planes[3][:], in_=w_rows[:, 3, :])
+        load(y_sb[0], y[0])
+        load(xm_raw[0], xm[0])
+        load(xT_raw[1], xT[1])
+        load(y_sb[1], y[1])
+        load(xm_raw[1], xm[1])
+
+        warm_in = tile([P, 1], F32, "warm_in")
+        warm_out = tile([P, 1], F32, "warm_out")
+        nc.gpsimd.memset(warm_in[:], 0.0)
+        nc.scalar.activation(warm_out[:], warm_in[:], ACT.Sigmoid)
+
+        windows = [tile([P, T], F32, f"window{c}") for c in range(D // P)]
+        for window in windows:
+            nc.vector.memset(window[:], 0.0)
+
+        picked = [tile([P, PACK, N], F32, f"picked{b}") for b in range(B)]
+        w_bf = [tile([P, N, PACK], BF16, f"w_bf{b}") for b in range(B)]
+        x_bf = [tile([P, R * PACK], BF16, f"x_bf{b}") for b in range(B)]
+        xm_bf = [tile([P, D, PACK], BF16, f"xm_bf{b}") for b in range(B)]
+        g_bf = [tile([P, N, PACK], BF16, f"g_bf{b}") for b in range(B)]
+        prob = [tile([P, PACK, N], F32, f"prob{b}") for b in range(B)]
+        sq = [tile([P, PACK, N], F32, f"sq{b}") for b in range(B)]
+        slope, err = sq, y_sb
+        codes, scales = {}, {}
+        for kind in ("w", "x", "xm", "g"):
+            for b in range(B):
+                codes[kind, b] = tile([P, 512], U32, f"{kind}_codes{b}")
+                scales[kind, b] = tile([P, 512], U8, f"{kind}_scales{b}")
+
+        def slots(b, lo, hi):
+            return offsets[:, (b * N + lo) // 16 : (b * N + hi) // 16]
+
+        def gather(b, j, lo, hi):
+            nc.vector.tensor_copy(picked[b][:, j, lo:hi], planes[j][:].indirect(slots(b, lo, hi)))
+
+        def by_fours_src(ap):
+            return ap.rearrange("p j (c i) -> p c j i", i=4)
+
+        def by_fours_dst(ap):
+            return ap.rearrange("p (c i) j -> p c j i", i=4)
+
+        def quantise(kind, b, src, lo, hi, fmt):
+            nc.vector.quantize_mx(out=codes[kind, b][:, lo:hi].bitcast(fmt), scales=scales[kind, b][:, lo:hi], in_=src)
+
+        def flat(ap):
+            return ap.rearrange("p c j -> p (c j)")
+
+        def cast_x(b):
+            nc.scalar.copy(
+                x_bf[b][:].rearrange("p (t m j) -> p m t j", t=PACK, j=PACK),
+                xT_raw[b][:].rearrange("p j (m t) -> p m t j", t=PACK),
+            )
+
+        def scores(b, h):
+            lo, hi = h * HALF, (h + 1) * HALF
+            for u in range(2):
+                bank = psum.tile([P, 2, HALF], F32, name=f"score{h}{u}")
+                for e in range(2):
+                    t = 2 * u + e
+                    nc.tensor.matmul_mx(
+                        out=bank[:, e, :],
+                        lhsT=codes["x", b][:, t * P : (t + 1) * P].bitcast(E4M3),
+                        lhsT_scale=scales["x", b][:, t * P : (t + 1) * P],
+                        rhs=codes["w", b][:, lo:hi].bitcast(E4M3),
+                        rhs_scale=scales["w", b][:, lo:hi],
+                        start=True,
+                        stop=True,
+                    )
+                pair = slice(2 * u, 2 * u + 2)
+                nc.scalar.activation(prob[b][:, pair, lo:hi], bank[:], ACT.Sigmoid)
+                nc.scalar.activation(sq[b][:, pair, lo:hi], prob[b][:, pair, lo:hi], ACT.Square, bias=-0.5)
+
+        def gradient(b, h):
+            lo, hi = h * HALF, (h + 1) * HALF
+            nc.vector.tensor_tensor(err[b][:, :, lo:hi], y_sb[b][:, :, lo:hi], prob[b][:, :, lo:hi], ALU.subtract)
+            for t in range(PACK):
+                nc.vector.tensor_scalar(
+                    slope[b][:, t, lo:hi], sq[b][:, t, lo:hi], -0.25, wt_sb[:, b, t : t + 1], ALU.add, ALU.mult
+                )
+            nc.vector.tensor_tensor(
+                by_fours_dst(g_bf[b][:, lo:hi, :]),
+                by_fours_src(slope[b][:, :, lo:hi]),
+                by_fours_src(err[b][:, :, lo:hi]),
+                ALU.mult,
+            )
+
+        def quantise_g(b, h):
+            lo, hi = h * HALF, (h + 1) * HALF
+            quantise("g", b, flat(g_bf[b][:, lo:hi, :]), lo, hi, E5M2)
+
+        def cast_xm(b, lo, hi):
+            nc.scalar.copy(by_fours_dst(xm_bf[b][:, lo:hi, :]), by_fours_src(xm_raw[b][:, :, lo:hi]))
+
+        def product(b, c):
+            bank = psum.tile([P, N], F32, name=f"grad{c}")
+            nc.tensor.matmul_mx(
+                out=bank[:],
+                lhsT=codes["xm", b][:, c * P : (c + 1) * P].bitcast(E4M3),
+                lhsT_scale=scales["xm", b][:, c * P : (c + 1) * P],
+                rhs=codes["g", b][:].bitcast(E5M2),
+                rhs_scale=scales["g", b][:],
+                start=True,
+                stop=True,
+            )
+            dense = tile([P, N], F32, f"dense{b}{c}")
+            nc.scalar.copy(dense[:], bank[:])
+            return dense
+
+        def scatter(b, c, dense):
+            nc.vector.tensor_copy(windows[c][:].indirect(slots(b, 0, N)), dense[:])
+
+        for j in range(PACK - 1):
+            for b in range(B):
+                gather(b, j, 0, N)
+        cast_x(0)
+        quantise("x", 0, x_bf[0][:], 0, R, E4M3)
+        for h in range(2):
+            gather(0, PACK - 1, h * HALF, (h + 1) * HALF)
+        for h in range(2):
+            lo, hi = h * HALF, (h + 1) * HALF
+            nc.vector.tensor_copy(by_fours_dst(w_bf[0][:, lo:hi, :]), by_fours_src(picked[0][:, :, lo:hi]))
+        for h in range(2):
+            lo, hi = h * HALF, (h + 1) * HALF
+            quantise("w", 0, flat(w_bf[0][:, lo:hi, :]), lo, hi, E4M3)
+            scores(0, h)
+        gather(1, PACK - 1, 0, N)
+        for h in range(2):
+            gradient(0, h)
+        cast_xm(0, 0, P)
+        quantise("xm", 0, flat(xm_bf[0][:, 0:P, :]), 0, P, E4M3)
+        for h in range(2):
+            quantise_g(0, h)
+        scatter(0, 0, product(0, 0))
+        cast_xm(0, P, 2 * P)
+        cast_xm(0, 2 * P, D)
+        quantise("xm", 0, flat(xm_bf[0][:, P : 2 * P, :]), P, 2 * P, E4M3)
+        quantise("xm", 0, flat(xm_bf[0][:, 2 * P : D, :]), 2 * P, D, E4M3)
+        rest = [product(0, c) for c in range(1, D // P)]
+        nc.scalar.copy(by_fours_dst(w_bf[1][:]), by_fours_src(picked[1][:]))
+        cast_x(1)
+        scatter(0, 1, rest[0])
+        quantise("w", 1, flat(w_bf[1][:]), 0, N, E4M3)
+        quantise("x", 1, x_bf[1][:], 0, R, E4M3)
+        for h in range(2):
+            scores(1, h)
+        cast_xm(1, 0, D)
+        scatter(0, 2, rest[1])
+        for h in range(2):
+            gradient(1, h)
+        quantise("xm", 1, flat(xm_bf[1][:]), 0, D, E4M3)
+        for h in range(2):
+            quantise_g(1, h)
+        last = [product(1, c) for c in range(D // P)]
+        scatter(0, 3, rest[2])
+        for c in range(D // P):
+            scatter(1, c, last[c])
+            nc.sync.dma_start(out=out[c * P : (c + 1) * P, :], in_=windows[c][:])

@@ -30,10 +30,15 @@ def tile_attend_gsl2_w_kernel(tc, xT, wT, y, wt, xm, offs, out):
         def tile(shape, dtype, name):
             return keep.tile(shape, dtype, name=name, align_bytes=64)
 
+        def flat(ap):
+            return ap.rearrange("p c j -> p (c j)")
+
         offsets = keep.tile([P, B * LIST_COLS], U16, name="offsets")
         nc.sync.dma_start(offsets[:], offs)
 
-        planes = [tile([P, T], F32, f"plane{j}") for j in range(PACK)]
+        pairs = [tile([P, T], U32, f"pair{u}") for u in range(2)]
+        chunks = [(0, 0, 1024), (0, 1024, 2048), (1, 0, 1024), (1, 1024, 1536), (1, 1536, 2048)]
+        w_raw = [tile([P, 2, hi - lo], F32, f"w_raw{u}_{lo}") for u, lo, hi in chunks]
         xT_raw = [tile([P, PACK, R], F32, f"xT_raw{b}") for b in range(B)]
         xm_raw = [tile([P, PACK, D], F32, f"xm_raw{b}") for b in range(B)]
         y_sb = [tile([P, PACK, N], F32, f"y{b}") for b in range(B)]
@@ -43,16 +48,19 @@ def tile_attend_gsl2_w_kernel(tc, xT, wT, y, wt, xm, offs, out):
         def load(dst, src):
             nc.sync.dma_start(out=dst[:], in_=src.rearrange("(p j) w -> p j w", j=PACK))
 
-        nc.sync.dma_start(out=planes[0][:], in_=w_rows[:, 0, :])
+        for k, (u, lo, hi) in enumerate(chunks):
+            nc.sync.dma_start(out=w_raw[k][:], in_=w_rows[:, 2 * u : 2 * u + 2, lo:hi])
+        xT_rows = xT[0].rearrange("(p j) w -> p j w", j=PACK)
+        for h in range(2):
+            cols = slice(h * R // 2, (h + 1) * R // 2)
+            nc.sync.dma_start(out=xT_raw[0][:, :, cols], in_=xT_rows[:, :, cols])
         nc.sync.dma_start(out=wt_sb[:], in_=wt.rearrange("b (p t) o -> p b (t o)", t=PACK))
-        nc.sync.dma_start(out=planes[1][:], in_=w_rows[:, 1, :])
-        nc.sync.dma_start(out=planes[2][:], in_=w_rows[:, 2, :])
-        load(xT_raw[0], xT[0])
-        nc.sync.dma_start(out=planes[3][:], in_=w_rows[:, 3, :])
         load(y_sb[0], y[0])
-        load(xm_raw[0], xm[0])
-        load(xT_raw[1], xT[1])
+        xm_rows = xm[0].rearrange("(p j) w -> p j w", j=PACK)
+        nc.sync.dma_start(out=xm_raw[0][:, :, : D // 2], in_=xm_rows[:, :, : D // 2])
         load(y_sb[1], y[1])
+        load(xT_raw[1], xT[1])
+        nc.sync.dma_start(out=xm_raw[0][:, :, D // 2 :], in_=xm_rows[:, :, D // 2 :])
         load(xm_raw[1], xm[1])
 
         warm_in = tile([P, 1], F32, "warm_in")
@@ -64,9 +72,10 @@ def tile_attend_gsl2_w_kernel(tc, xT, wT, y, wt, xm, offs, out):
         for window in windows:
             nc.vector.memset(window[:], 0.0)
 
-        picked = [tile([P, PACK, N], F32, f"picked{b}") for b in range(B)]
-        w_bf = [tile([P, N, PACK], BF16, f"w_bf{b}") for b in range(B)]
-        x_bf = [tile([P, R * PACK], BF16, f"x_bf{b}") for b in range(B)]
+        picked = [tile([P, N, 2], U32, f"picked{b}") for b in range(B)]
+        bias_sb = tile([P, PACK], F32, "bias_sb")
+        shared = tile([P, 3, N], U32, "shared")
+        x_bf = [flat(shared[:, 1:3, :]).bitcast(BF16), tile([P, R * PACK], BF16, "x_bf1")[:]]
         xm_bf = [tile([P, D, PACK], BF16, f"xm_bf{b}") for b in range(B)]
         g_bf = [tile([P, N, PACK], BF16, f"g_bf{b}") for b in range(B)]
         prob = [tile([P, PACK, N], F32, f"prob{b}") for b in range(B)]
@@ -81,8 +90,16 @@ def tile_attend_gsl2_w_kernel(tc, xT, wT, y, wt, xm, offs, out):
         def slots(b, lo, hi):
             return offsets[:, (b * N + lo) // 16 : (b * N + hi) // 16]
 
-        def gather(b, j, lo, hi):
-            nc.vector.tensor_copy(picked[b][:, j, lo:hi], planes[j][:].indirect(slots(b, lo, hi)))
+        def gather(b, u):
+            dst = picked[0][:, :, u] if b == 0 else shared[:, u, :]
+            nc.vector.tensor_copy(dst, pairs[u][:].indirect(slots(b, 0, N)))
+
+        def cast_w(k, copy):
+            u, lo, hi = chunks[k]
+            copy(
+                pairs[u][:, lo:hi].bitcast(BF16).rearrange("p (c i e) -> p c e i", i=4, e=2),
+                w_raw[k][:].rearrange("p e (c i) -> p c e i", i=4),
+            )
 
         def by_fours_src(ap):
             return ap.rearrange("p j (c i) -> p c j i", i=4)
@@ -93,13 +110,10 @@ def tile_attend_gsl2_w_kernel(tc, xT, wT, y, wt, xm, offs, out):
         def quantise(kind, b, src, lo, hi, fmt):
             nc.vector.quantize_mx(out=codes[kind, b][:, lo:hi].bitcast(fmt), scales=scales[kind, b][:, lo:hi], in_=src)
 
-        def flat(ap):
-            return ap.rearrange("p c j -> p (c j)")
-
-        def cast_x(b):
-            nc.scalar.copy(
-                x_bf[b][:].rearrange("p (t m j) -> p m t j", t=PACK, j=PACK),
-                xT_raw[b][:].rearrange("p j (m t) -> p m t j", t=PACK),
+        def cast_x(b, lo, hi, copy):
+            copy(
+                x_bf[b].rearrange("p (t m j) -> p m t j", t=PACK, j=PACK)[:, lo:hi],
+                xT_raw[b][:].rearrange("p j (m t) -> p m t j", t=PACK)[:, lo:hi],
             )
 
         def scores(b, h):
@@ -123,11 +137,23 @@ def tile_attend_gsl2_w_kernel(tc, xT, wT, y, wt, xm, offs, out):
 
         def gradient(b, h):
             lo, hi = h * HALF, (h + 1) * HALF
-            nc.vector.tensor_tensor(err[b][:, :, lo:hi], y_sb[b][:, :, lo:hi], prob[b][:, :, lo:hi], ALU.subtract)
-            for t in range(PACK):
-                nc.vector.tensor_scalar(
-                    slope[b][:, t, lo:hi], sq[b][:, t, lo:hi], -0.25, wt_sb[:, b, t : t + 1], ALU.add, ALU.mult
-                )
+            if b == 0:
+                nc.vector.tensor_tensor(err[b][:, :, lo:hi], y_sb[b][:, :, lo:hi], prob[b][:, :, lo:hi], ALU.subtract)
+                for t in range(PACK):
+                    nc.vector.tensor_scalar(
+                        slope[b][:, t, lo:hi], sq[b][:, t, lo:hi], -0.25, wt_sb[:, b, t : t + 1], ALU.add, ALU.mult
+                    )
+            else:
+                for u in range(2):
+                    pair = slice(2 * u, 2 * u + 2)
+                    nc.gpsimd.tensor_tensor(
+                        err[b][:, pair, lo:hi], y_sb[b][:, pair, lo:hi], prob[b][:, pair, lo:hi], ALU.subtract
+                    )
+                for t in range(PACK):
+                    nc.scalar.activation(
+                        slope[b][:, t, lo:hi], sq[b][:, t, lo:hi], ACT.Identity,
+                        bias=bias_sb[:, t : t + 1], scale=wt_sb[:, b, t : t + 1],
+                    )
             nc.vector.tensor_tensor(
                 by_fours_dst(g_bf[b][:, lo:hi, :]),
                 by_fours_src(slope[b][:, :, lo:hi]),
@@ -142,7 +168,7 @@ def tile_attend_gsl2_w_kernel(tc, xT, wT, y, wt, xm, offs, out):
         def cast_xm(b, lo, hi):
             nc.scalar.copy(by_fours_dst(xm_bf[b][:, lo:hi, :]), by_fours_src(xm_raw[b][:, :, lo:hi]))
 
-        def product(b, c):
+        def product(b, c, copy):
             bank = psum.tile([P, N], F32, name=f"grad{c}")
             nc.tensor.matmul_mx(
                 out=bank[:],
@@ -153,56 +179,66 @@ def tile_attend_gsl2_w_kernel(tc, xT, wT, y, wt, xm, offs, out):
                 start=True,
                 stop=True,
             )
-            dense = tile([P, N], F32, f"dense{b}{c}")
-            nc.scalar.copy(dense[:], bank[:])
-            return dense
+            if (b, c) == (0, 0):
+                halves = [x_bf[1].bitcast(F32)[:, :HALF], flat(xm_bf[0][:, D // 2 :, :]).bitcast(F32)[:, :HALF]]
+                for h in range(2):
+                    copy(halves[h], bank[:, h * HALF : (h + 1) * HALF])
+                return halves
+            if (b, c) == (0, D // P - 1):
+                staged = sq[1][:, PACK - 1, :]
+            else:
+                staged = tile([P, N], F32, f"dense{b}{c}")[:]
+            copy(staged, bank[:])
+            return [staged[:, :HALF], staged[:, HALF:]]
 
-        def scatter(b, c, dense):
-            nc.vector.tensor_copy(windows[c][:].indirect(slots(b, 0, N)), dense[:])
+        def scatter(b, c, halves):
+            for h in range(2):
+                nc.vector.tensor_copy(windows[c][:].indirect(slots(b, h * HALF, (h + 1) * HALF)), halves[h])
 
-        for j in range(PACK - 1):
-            for b in range(B):
-                gather(b, j, 0, N)
-        cast_x(0)
-        quantise("x", 0, x_bf[0][:], 0, R, E4M3)
+        for k in range(len(chunks) - 1):
+            cast_w(k, nc.scalar.copy)
+        for b in range(B):
+            gather(b, 0)
+        cast_w(len(chunks) - 1, nc.vector.tensor_copy)
+        gather(0, 1)
+        quantise("w", 0, flat(picked[0][:]).bitcast(BF16), 0, N, E4M3)
+        cast_x(0, 0, 64, nc.scalar.copy)
+        cast_x(0, 64, 96, nc.scalar.copy)
+        cast_x(0, 96, P, nc.vector.tensor_copy)
+        for u in range(2):
+            quantise("x", 0, x_bf[0][:, u * 1024 : (u + 1) * 1024], u * 256, (u + 1) * 256, E4M3)
+        gather(1, 1)
+        nc.vector.tensor_copy(
+            flat(picked[1][:]).bitcast(BF16).rearrange("p (i u e) -> p i u e", u=2, e=2),
+            flat(shared[:, 0:2, :]).bitcast(BF16).rearrange("p (u i e) -> p i u e", u=2, e=2),
+        )
         for h in range(2):
-            gather(0, PACK - 1, h * HALF, (h + 1) * HALF)
-        for h in range(2):
-            lo, hi = h * HALF, (h + 1) * HALF
-            nc.vector.tensor_copy(by_fours_dst(w_bf[0][:, lo:hi, :]), by_fours_src(picked[0][:, :, lo:hi]))
-        for h in range(2):
-            lo, hi = h * HALF, (h + 1) * HALF
-            quantise("w", 0, flat(w_bf[0][:, lo:hi, :]), lo, hi, E4M3)
             scores(0, h)
-        gather(1, PACK - 1, 0, N)
         for h in range(2):
             gradient(0, h)
-        cast_xm(0, 0, P)
-        quantise("xm", 0, flat(xm_bf[0][:, 0:P, :]), 0, P, E4M3)
+        quantise("w", 1, flat(picked[1][:]).bitcast(BF16), 0, N, E4M3)
+        cast_xm(0, 0, D // 2)
+        quantise("xm", 0, flat(xm_bf[0][:, : D // 2, :]), 0, D // 2, E4M3)
         for h in range(2):
             quantise_g(0, h)
-        scatter(0, 0, product(0, 0))
-        cast_xm(0, P, 2 * P)
-        cast_xm(0, 2 * P, D)
-        quantise("xm", 0, flat(xm_bf[0][:, P : 2 * P, :]), P, 2 * P, E4M3)
-        quantise("xm", 0, flat(xm_bf[0][:, 2 * P : D, :]), 2 * P, D, E4M3)
-        rest = [product(0, c) for c in range(1, D // P)]
-        nc.scalar.copy(by_fours_dst(w_bf[1][:]), by_fours_src(picked[1][:]))
-        cast_x(1)
-        scatter(0, 1, rest[0])
-        quantise("w", 1, flat(w_bf[1][:]), 0, N, E4M3)
-        quantise("x", 1, x_bf[1][:], 0, R, E4M3)
+        cast_x(1, 0, P, nc.scalar.copy)
+        quantise("x", 1, x_bf[1], 0, R, E4M3)
+        cast_xm(0, D // 2, D)
+        quantise("xm", 0, flat(xm_bf[0][:, D // 2 :, :]), D // 2, D, E4M3)
+        dense = {(0, 0): product(0, 0, nc.vector.tensor_copy), (0, 1): product(0, 1, nc.scalar.copy)}
+        dense[0, 2] = product(0, 2, nc.scalar.copy)
+        nc.gpsimd.tensor_scalar(bias_sb[:], wt_sb[:, 1, :], -0.25, 0.0, ALU.mult, ALU.add)
         for h in range(2):
             scores(1, h)
-        cast_xm(1, 0, D)
-        scatter(0, 2, rest[1])
-        for h in range(2):
             gradient(1, h)
+        dense[0, 3] = product(0, 3, nc.scalar.copy)
+        cast_xm(1, 0, D)
         quantise("xm", 1, flat(xm_bf[1][:]), 0, D, E4M3)
         for h in range(2):
             quantise_g(1, h)
-        last = [product(1, c) for c in range(D // P)]
-        scatter(0, 3, rest[2])
         for c in range(D // P):
-            scatter(1, c, last[c])
+            dense[1, c] = product(1, c, nc.scalar.copy)
+        for c in range(D // P):
+            for b in range(B):
+                scatter(b, c, dense[b, c])
             nc.sync.dma_start(out=out[c * P : (c + 1) * P, :], in_=windows[c][:])

@@ -34,7 +34,6 @@ def tile_attend_gsl2_w_kernel(tc, xT, wT, y, wt, xm, offs, out):
             return ap.rearrange("p c j -> p (c j)")
 
         offsets = keep.tile([P, B * LIST_COLS], U16, name="offsets")
-        nc.sync.dma_start(offsets[:], offs)
 
         pairs = [tile([P, T], U32, f"pair{u}") for u in range(2)]
         chunks = [(0, 0, 1024), (0, 1024, 2048), (1, 0, 1024), (1, 1024, 1536), (1, 1536, 2048)]
@@ -50,6 +49,8 @@ def tile_attend_gsl2_w_kernel(tc, xT, wT, y, wt, xm, offs, out):
 
         for k, (u, lo, hi) in enumerate(chunks):
             nc.sync.dma_start(out=w_raw[k][:], in_=w_rows[:, 2 * u : 2 * u + 2, lo:hi])
+            if k == 0:
+                nc.sync.dma_start(offsets[:], offs)
         xT_rows = xT[0].rearrange("(p j) w -> p j w", j=PACK)
         for h in range(2):
             cols = slice(h * R // 2, (h + 1) * R // 2)
@@ -69,18 +70,21 @@ def tile_attend_gsl2_w_kernel(tc, xT, wT, y, wt, xm, offs, out):
         nc.scalar.activation(warm_out[:], warm_in[:], ACT.Sigmoid)
 
         windows = [tile([P, T], F32, f"window{c}") for c in range(D // P)]
-        for window in windows:
-            nc.vector.memset(window[:], 0.0)
+        for c, window in enumerate(windows):
+            (nc.vector if c < 2 else nc.gpsimd).memset(window[:], 0.0)
 
         picked = [tile([P, N, 2], U32, f"picked{b}") for b in range(B)]
         bias_sb = tile([P, PACK], F32, "bias_sb")
         shared = tile([P, 3, N], U32, "shared")
         x_bf = [flat(shared[:, 1:3, :]).bitcast(BF16), tile([P, R * PACK], BF16, "x_bf1")[:]]
-        xm_bf = [tile([P, D, PACK], BF16, f"xm_bf{b}") for b in range(B)]
         g_bf = [tile([P, N, PACK], BF16, f"g_bf{b}") for b in range(B)]
         prob = [tile([P, PACK, N], F32, f"prob{b}") for b in range(B)]
         sq = [tile([P, PACK, N], F32, f"sq{b}") for b in range(B)]
         slope, err = sq, y_sb
+        xm_bf = [
+            tile([P, D, PACK], BF16, "xm_bf0"),
+            flat(prob[1][:, 2:4, :]).bitcast(BF16).rearrange("p (c j) -> p c j", j=PACK),
+        ]
         codes, scales = {}, {}
         for kind in ("w", "x", "xm", "g"):
             for b in range(B):
@@ -154,12 +158,21 @@ def tile_attend_gsl2_w_kernel(tc, xT, wT, y, wt, xm, offs, out):
                         slope[b][:, t, lo:hi], sq[b][:, t, lo:hi], ACT.Identity,
                         bias=bias_sb[:, t : t + 1], scale=wt_sb[:, b, t : t + 1],
                     )
-            nc.vector.tensor_tensor(
-                by_fours_dst(g_bf[b][:, lo:hi, :]),
-                by_fours_src(slope[b][:, :, lo:hi]),
-                by_fours_src(err[b][:, :, lo:hi]),
-                ALU.mult,
-            )
+            if (b, h) != (1, 0):
+                nc.vector.tensor_tensor(
+                    by_fours_dst(g_bf[b][:, lo:hi, :]),
+                    by_fours_src(slope[b][:, :, lo:hi]),
+                    by_fours_src(err[b][:, :, lo:hi]),
+                    ALU.mult,
+                )
+            else:
+                for q in range(lo, hi, P):
+                    nc.gpsimd.tensor_tensor(
+                        g_bf[b][:, q : q + P, :],
+                        slope[b][:, :, q : q + P].rearrange("p t i -> p i t"),
+                        err[b][:, :, q : q + P].rearrange("p t i -> p i t"),
+                        ALU.mult,
+                    )
 
         def quantise_g(b, h):
             lo, hi = h * HALF, (h + 1) * HALF
@@ -185,21 +198,26 @@ def tile_attend_gsl2_w_kernel(tc, xT, wT, y, wt, xm, offs, out):
                     copy(halves[h], bank[:, h * HALF : (h + 1) * HALF])
                 return halves
             if (b, c) == (0, D // P - 1):
-                staged = sq[1][:, PACK - 1, :]
-            else:
-                staged = tile([P, N], F32, f"dense{b}{c}")[:]
+                halves = [tile([P, HALF], F32, "dense03")[:], sq[1][:, PACK - 1, HALF:]]
+                for h in range(2):
+                    copy(halves[h], bank[:, h * HALF : (h + 1) * HALF])
+                return halves
+            staged = tile([P, N], F32, f"dense{b}{c}")[:]
             copy(staged, bank[:])
-            return [staged[:, :HALF], staged[:, HALF:]]
+            return [staged]
 
         def scatter(b, c, halves):
-            for h in range(2):
-                nc.vector.tensor_copy(windows[c][:].indirect(slots(b, h * HALF, (h + 1) * HALF)), halves[h])
+            width = N // len(halves)
+            for h, piece in enumerate(halves):
+                nc.vector.tensor_copy(windows[c][:].indirect(slots(b, h * width, (h + 1) * width)), piece)
 
-        for k in range(len(chunks) - 1):
-            cast_w(k, nc.scalar.copy)
+        cast_w(0, nc.scalar.copy)
+        cast_w(1, nc.vector.tensor_copy)
         for b in range(B):
             gather(b, 0)
-        cast_w(len(chunks) - 1, nc.vector.tensor_copy)
+        cast_w(2, nc.scalar.copy)
+        cast_w(3, nc.vector.tensor_copy)
+        cast_w(4, nc.vector.tensor_copy)
         gather(0, 1)
         quantise("w", 0, flat(picked[0][:]).bitcast(BF16), 0, N, E4M3)
         cast_x(0, 0, 64, nc.scalar.copy)
@@ -232,8 +250,9 @@ def tile_attend_gsl2_w_kernel(tc, xT, wT, y, wt, xm, offs, out):
             scores(1, h)
             gradient(1, h)
         dense[0, 3] = product(0, 3, nc.scalar.copy)
-        cast_xm(1, 0, D)
-        quantise("xm", 1, flat(xm_bf[1][:]), 0, D, E4M3)
+        for lo in (0, D // 2):
+            cast_xm(1, lo, lo + D // 2)
+            quantise("xm", 1, flat(xm_bf[1][:, lo : lo + D // 2, :]), lo, lo + D // 2, E4M3)
         for h in range(2):
             quantise_g(1, h)
         for c in range(D // P):

@@ -56,9 +56,9 @@ def tile_attend_gsl2_w_kernel(tc, xT, wT, y, wt, xm, offs, out):
             cols = slice(h * R // 2, (h + 1) * R // 2)
             nc.sync.dma_start(out=xT_raw[0][:, :, cols], in_=xT_rows[:, :, cols])
         nc.sync.dma_start(out=wt_sb[:], in_=wt.rearrange("b (p t) o -> p b (t o)", t=PACK))
-        load(y_sb[0], y[0])
         xm_rows = xm[0].rearrange("(p j) w -> p j w", j=PACK)
         nc.sync.dma_start(out=xm_raw[0][:, :, : D // 2], in_=xm_rows[:, :, : D // 2])
+        load(y_sb[0], y[0])
         load(y_sb[1], y[1])
         load(xT_raw[1], xT[1])
         nc.sync.dma_start(out=xm_raw[0][:, :, D // 2 :], in_=xm_rows[:, :, D // 2 :])
@@ -77,12 +77,16 @@ def tile_attend_gsl2_w_kernel(tc, xT, wT, y, wt, xm, offs, out):
         bias_sb = tile([P, PACK], F32, "bias_sb")
         shared = tile([P, 3, N], U32, "shared")
         x_bf = [flat(shared[:, 1:3, :]).bitcast(BF16), tile([P, R * PACK], BF16, "x_bf1")[:]]
-        g_bf = [tile([P, N, PACK], BF16, f"g_bf{b}") for b in range(B)]
+        err = [y_sb[0], tile([P, PACK, N], F32, "err1")]
+        g_bf = [
+            flat(err[1][:, 0:2, :]).bitcast(BF16).rearrange("p (c j) -> p c j", j=PACK),
+            tile([P, N, PACK], BF16, "g_bf1"),
+        ]
         prob = [tile([P, PACK, N], F32, f"prob{b}") for b in range(B)]
         sq = [tile([P, PACK, N], F32, f"sq{b}") for b in range(B)]
-        slope, err = sq, y_sb
+        slope = sq
         xm_bf = [
-            tile([P, D, PACK], BF16, "xm_bf0"),
+            flat(err[1][:, 2:4, :]).bitcast(BF16).rearrange("p (c j) -> p c j", j=PACK),
             flat(prob[1][:, 2:4, :]).bitcast(BF16).rearrange("p (c j) -> p c j", j=PACK),
         ]
         codes, scales = {}, {}
@@ -116,8 +120,8 @@ def tile_attend_gsl2_w_kernel(tc, xT, wT, y, wt, xm, offs, out):
 
         def cast_x(b, lo, hi, copy):
             copy(
-                x_bf[b].rearrange("p (t m j) -> p m t j", t=PACK, j=PACK)[:, lo:hi],
-                xT_raw[b][:].rearrange("p j (m t) -> p m t j", t=PACK)[:, lo:hi],
+                x_bf[b].rearrange("p (t m j) -> p m j t", t=PACK, j=PACK)[:, lo:hi],
+                xT_raw[b][:].rearrange("p j (m t) -> p m j t", t=PACK)[:, lo:hi],
             )
 
         def scores(b, h):
@@ -148,31 +152,27 @@ def tile_attend_gsl2_w_kernel(tc, xT, wT, y, wt, xm, offs, out):
                         slope[b][:, t, lo:hi], sq[b][:, t, lo:hi], -0.25, wt_sb[:, b, t : t + 1], ALU.add, ALU.mult
                     )
             else:
-                for u in range(2):
-                    pair = slice(2 * u, 2 * u + 2)
-                    nc.gpsimd.tensor_tensor(
-                        err[b][:, pair, lo:hi], y_sb[b][:, pair, lo:hi], prob[b][:, pair, lo:hi], ALU.subtract
-                    )
+                nc.gpsimd.tensor_tensor(err[b][:, :, lo:hi], y_sb[b][:, :, lo:hi], prob[b][:, :, lo:hi], ALU.subtract)
                 for t in range(PACK):
                     nc.scalar.activation(
                         slope[b][:, t, lo:hi], sq[b][:, t, lo:hi], ACT.Identity,
                         bias=bias_sb[:, t : t + 1], scale=wt_sb[:, b, t : t + 1],
                     )
-            if (b, h) != (1, 0):
-                nc.vector.tensor_tensor(
-                    by_fours_dst(g_bf[b][:, lo:hi, :]),
-                    by_fours_src(slope[b][:, :, lo:hi]),
-                    by_fours_src(err[b][:, :, lo:hi]),
+            cut = lo if b == 0 else min(hi, N - P)
+            if cut > lo:
+                nc.gpsimd.tensor_tensor(
+                    g_bf[b][:, lo:cut, :],
+                    slope[b][:, :, lo:cut].rearrange("p t i -> p i t"),
+                    err[b][:, :, lo:cut].rearrange("p t i -> p i t"),
                     ALU.mult,
                 )
-            else:
-                for q in range(lo, hi, P):
-                    nc.gpsimd.tensor_tensor(
-                        g_bf[b][:, q : q + P, :],
-                        slope[b][:, :, q : q + P].rearrange("p t i -> p i t"),
-                        err[b][:, :, q : q + P].rearrange("p t i -> p i t"),
-                        ALU.mult,
-                    )
+            if cut < hi:
+                nc.vector.tensor_tensor(
+                    by_fours_dst(g_bf[b][:, cut:hi, :]),
+                    by_fours_src(slope[b][:, :, cut:hi]),
+                    by_fours_src(err[b][:, :, cut:hi]),
+                    ALU.mult,
+                )
 
         def quantise_g(b, h):
             lo, hi = h * HALF, (h + 1) * HALF
@@ -192,17 +192,15 @@ def tile_attend_gsl2_w_kernel(tc, xT, wT, y, wt, xm, offs, out):
                 start=True,
                 stop=True,
             )
-            if (b, c) == (0, 0):
-                halves = [x_bf[1].bitcast(F32)[:, :HALF], flat(xm_bf[0][:, D // 2 :, :]).bitcast(F32)[:, :HALF]]
-                for h in range(2):
-                    copy(halves[h], bank[:, h * HALF : (h + 1) * HALF])
-                return halves
             if (b, c) == (0, D // P - 1):
                 halves = [tile([P, HALF], F32, "dense03")[:], sq[1][:, PACK - 1, HALF:]]
                 for h in range(2):
                     copy(halves[h], bank[:, h * HALF : (h + 1) * HALF])
                 return halves
-            staged = tile([P, N], F32, f"dense{b}{c}")[:]
+            if (b, c) == (0, 0):
+                staged = x_bf[1].bitcast(F32)[:, :N]
+            else:
+                staged = tile([P, N], F32, f"dense{b}{c}")[:]
             copy(staged, bank[:])
             return [staged]
 
@@ -232,15 +230,15 @@ def tile_attend_gsl2_w_kernel(tc, xT, wT, y, wt, xm, offs, out):
         )
         for h in range(2):
             scores(0, h)
-        for h in range(2):
-            gradient(0, h)
+        gradient(0, 0)
         quantise("w", 1, flat(picked[1][:]).bitcast(BF16), 0, N, E4M3)
-        cast_xm(0, 0, D // 2)
-        quantise("xm", 0, flat(xm_bf[0][:, : D // 2, :]), 0, D // 2, E4M3)
-        for h in range(2):
-            quantise_g(0, h)
         cast_x(1, 0, P, nc.scalar.copy)
         quantise("x", 1, x_bf[1], 0, R, E4M3)
+        cast_xm(0, 0, D // 2)
+        quantise("xm", 0, flat(xm_bf[0][:, : D // 2, :]), 0, D // 2, E4M3)
+        gradient(0, 1)
+        for h in range(2):
+            quantise_g(0, h)
         cast_xm(0, D // 2, D)
         quantise("xm", 0, flat(xm_bf[0][:, D // 2 :, :]), D // 2, D, E4M3)
         dense = {(0, 0): product(0, 0, nc.vector.tensor_copy), (0, 1): product(0, 1, nc.scalar.copy)}
@@ -260,4 +258,8 @@ def tile_attend_gsl2_w_kernel(tc, xT, wT, y, wt, xm, offs, out):
         for c in range(D // P):
             for b in range(B):
                 scatter(b, c, dense[b, c])
-            nc.sync.dma_start(out=out[c * P : (c + 1) * P, :], in_=windows[c][:])
+            if c < D // P - 1:
+                nc.sync.dma_start(out=out[c * P : (c + 1) * P, :], in_=windows[c][:])
+            else:
+                nc.sync.dma_start(out=out[c * P : (c + 1) * P, : T // 2], in_=windows[c][:, : T // 2])
+                nc.scalar.dma_start(out=out[c * P : (c + 1) * P, T // 2 :], in_=windows[c][:, T // 2 :])

@@ -120,8 +120,8 @@ def tile_attend_gsl2_w_kernel(tc, xT, wT, y, wt, xm, offs, out):
 
         def cast_x(b, lo, hi, copy):
             copy(
-                x_bf[b].rearrange("p (t m j) -> p m j t", t=PACK, j=PACK)[:, lo:hi],
-                xT_raw[b][:].rearrange("p j (m t) -> p m j t", t=PACK)[:, lo:hi],
+                x_bf[b].rearrange("p (t m j) -> p m t j", t=PACK, j=PACK)[:, lo:hi],
+                xT_raw[b][:].rearrange("p j (m t) -> p m t j", t=PACK)[:, lo:hi],
             )
 
         def scores(b, h):
@@ -158,19 +158,15 @@ def tile_attend_gsl2_w_kernel(tc, xT, wT, y, wt, xm, offs, out):
                         slope[b][:, t, lo:hi], sq[b][:, t, lo:hi], ACT.Identity,
                         bias=bias_sb[:, t : t + 1], scale=wt_sb[:, b, t : t + 1],
                     )
-            cut = lo if b == 0 else min(hi, N - P)
-            if cut > lo:
-                nc.gpsimd.tensor_tensor(
-                    g_bf[b][:, lo:cut, :],
-                    slope[b][:, :, lo:cut].rearrange("p t i -> p i t"),
-                    err[b][:, :, lo:cut].rearrange("p t i -> p i t"),
-                    ALU.mult,
-                )
-            if cut < hi:
+            if (b, h) == (1, 0):
+                g_rows = tile([P, PACK, HALF], BF16, f"g_rows{h}")
+                nc.gpsimd.tensor_tensor(g_rows[:], slope[b][:, :, lo:hi], err[b][:, :, lo:hi], ALU.mult)
+                nc.scalar.copy(g_bf[b][:, lo:hi, :], g_rows[:].rearrange("p t i -> p i t"))
+            else:
                 nc.vector.tensor_tensor(
-                    by_fours_dst(g_bf[b][:, cut:hi, :]),
-                    by_fours_src(slope[b][:, :, cut:hi]),
-                    by_fours_src(err[b][:, :, cut:hi]),
+                    by_fours_dst(g_bf[b][:, lo:hi, :]),
+                    by_fours_src(slope[b][:, :, lo:hi]),
+                    by_fours_src(err[b][:, :, lo:hi]),
                     ALU.mult,
                 )
 
@@ -258,8 +254,4 @@ def tile_attend_gsl2_w_kernel(tc, xT, wT, y, wt, xm, offs, out):
         for c in range(D // P):
             for b in range(B):
                 scatter(b, c, dense[b, c])
-            if c < D // P - 1:
-                nc.sync.dma_start(out=out[c * P : (c + 1) * P, :], in_=windows[c][:])
-            else:
-                nc.sync.dma_start(out=out[c * P : (c + 1) * P, : T // 2], in_=windows[c][:, : T // 2])
-                nc.scalar.dma_start(out=out[c * P : (c + 1) * P, T // 2 :], in_=windows[c][:, T // 2 :])
+            nc.sync.dma_start(out=out[c * P : (c + 1) * P, :], in_=windows[c][:])

@@ -25,75 +25,95 @@ def tile_attend_gsl2_w_kernel(tc, xT, wT, y, wt, xm, offs, out):
     nc = tc.nc
     with ExitStack() as ctx:
         keep = ctx.enter_context(tc.tile_pool(name="keep", bufs=1))
+        reuse = ctx.enter_context(tc.tile_pool(name="reuse", bufs=1))
         psum = ctx.enter_context(tc.psum_pool(name="psum", bufs=1))
 
         def tile(shape, dtype, name):
             return keep.tile(shape, dtype, name=name, align_bytes=64)
 
+        def tile_at(shape, dtype, name, kib):
+            return reuse.tile(shape, dtype, name=name, align_bytes=64, offset=int(1024 * kib))[:]
+
         def flat(ap):
             return ap.rearrange("p c j -> p (c j)")
+
+        def rows(src):
+            return src.rearrange("(p j) w -> p j w", j=PACK)
+
+        def half(h):
+            return slice(h * HALF, (h + 1) * HALF)
 
         offsets = keep.tile([P, B * LIST_COLS], U16, name="offsets")
 
         pairs = [tile([P, T], U32, f"pair{u}") for u in range(2)]
         chunks = [(0, 0, 1024), (0, 1024, 2048), (1, 0, 1024), (1, 1024, 1536), (1, 1536, 2048)]
         w_raw = [tile([P, 2, hi - lo], F32, f"w_raw{u}_{lo}") for u, lo, hi in chunks]
-        xT_raw = [tile([P, PACK, R], F32, f"xT_raw{b}") for b in range(B)]
-        xm_raw = [tile([P, PACK, D], F32, f"xm_raw{b}") for b in range(B)]
-        y_sb = [tile([P, PACK, N], F32, f"y{b}") for b in range(B)]
+        x0_raw = [tile([P, PACK, HALF], F32, f"x0_raw{h}") for h in range(2)]
+        x1_raw = tile_at([P, PACK, R], F32, "x1_raw", 12)
+        xm1_raw = tile([P, PACK, D], F32, "xm1_raw")
+        y1_raw = tile([P, PACK, N], F32, "y1_raw")
+        xm_raw = {(0, h): tile([P, PACK, HALF], F32, f"xm0_raw{h}")[:] for h in range(2)}
+        y_sb = {(0, h): tile([P, PACK, HALF], F32, f"y0_raw{h}")[:] for h in range(2)}
+        for h in range(2):
+            xm_raw[1, h] = xm1_raw[:, :, half(h)]
+            y_sb[1, h] = y1_raw[:, :, half(h)]
         wt_sb = tile([P, B, PACK], F32, "wt_sb")
-        w_rows = wT.rearrange("(p j) c -> p j c", j=PACK)
-
-        def load(dst, src):
-            nc.sync.dma_start(out=dst[:], in_=src.rearrange("(p j) w -> p j w", j=PACK))
 
         for k, (u, lo, hi) in enumerate(chunks):
-            nc.sync.dma_start(out=w_raw[k][:], in_=w_rows[:, 2 * u : 2 * u + 2, lo:hi])
+            nc.sync.dma_start(out=w_raw[k][:], in_=rows(wT)[:, 2 * u : 2 * u + 2, lo:hi])
             if k == 0:
                 nc.sync.dma_start(offsets[:], offs)
-        xT_rows = xT[0].rearrange("(p j) w -> p j w", j=PACK)
         for h in range(2):
-            cols = slice(h * R // 2, (h + 1) * R // 2)
-            nc.sync.dma_start(out=xT_raw[0][:, :, cols], in_=xT_rows[:, :, cols])
+            nc.sync.dma_start(out=x0_raw[h][:], in_=rows(xT[0])[:, :, half(h)])
         nc.sync.dma_start(out=wt_sb[:], in_=wt.rearrange("b (p t) o -> p b (t o)", t=PACK))
-        xm_rows = xm[0].rearrange("(p j) w -> p j w", j=PACK)
-        nc.sync.dma_start(out=xm_raw[0][:, :, : D // 2], in_=xm_rows[:, :, : D // 2])
-        load(y_sb[0], y[0])
-        load(y_sb[1], y[1])
-        load(xT_raw[1], xT[1])
-        nc.sync.dma_start(out=xm_raw[0][:, :, D // 2 :], in_=xm_rows[:, :, D // 2 :])
-        load(xm_raw[1], xm[1])
+        nc.sync.dma_start(out=xm_raw[0, 0], in_=rows(xm[0])[:, :, half(0)])
+        for h in range(2):
+            nc.sync.dma_start(out=y_sb[0, h], in_=rows(y[0])[:, :, half(h)])
+        nc.sync.dma_start(out=x1_raw, in_=rows(xT[1]))
+        nc.sync.dma_start(out=xm_raw[0, 1], in_=rows(xm[0])[:, :, half(1)])
+        nc.sync.dma_start(out=xm1_raw[:], in_=rows(xm[1]))
+        nc.sync.dma_start(out=y1_raw[:], in_=rows(y[1]))
 
         warm_in = tile([P, 1], F32, "warm_in")
         warm_out = tile([P, 1], F32, "warm_out")
         nc.gpsimd.memset(warm_in[:], 0.0)
         nc.scalar.activation(warm_out[:], warm_in[:], ACT.Sigmoid)
 
-        windows = [tile([P, T], F32, f"window{c}") for c in range(D // P)]
-        for c, window in enumerate(windows):
-            (nc.vector if c < 2 else nc.gpsimd).memset(window[:], 0.0)
-
-        picked = [tile([P, N, 2], U32, f"picked{b}") for b in range(B)]
-        bias_sb = tile([P, PACK], F32, "bias_sb")
-        shared = tile([P, 3, N], U32, "shared")
-        x_bf = [flat(shared[:, 1:3, :]).bitcast(BF16), tile([P, R * PACK], BF16, "x_bf1")[:]]
-        err = [y_sb[0], tile([P, PACK, N], F32, "err1")]
-        g_bf = [
-            flat(err[1][:, 0:2, :]).bitcast(BF16).rearrange("p (c j) -> p c j", j=PACK),
-            tile([P, N, PACK], BF16, "g_bf1"),
-        ]
-        prob = [tile([P, PACK, N], F32, f"prob{b}") for b in range(B)]
-        sq = [tile([P, PACK, N], F32, f"sq{b}") for b in range(B)]
-        slope = sq
-        xm_bf = [
-            flat(err[1][:, 2:4, :]).bitcast(BF16).rearrange("p (c j) -> p c j", j=PACK),
-            flat(prob[1][:, 2:4, :]).bitcast(BF16).rearrange("p (c j) -> p c j", j=PACK),
-        ]
         codes, scales = {}, {}
         for kind in ("w", "x", "xm", "g"):
             for b in range(B):
                 codes[kind, b] = tile([P, 512], U32, f"{kind}_codes{b}")
                 scales[kind, b] = tile([P, 512], U8, f"{kind}_scales{b}")
+
+        windows = [tile([P, T], F32, f"window{c}") for c in range(D // P)]
+        for c, window in enumerate(windows):
+            (nc.vector if c < 3 else nc.gpsimd).memset(window[:], 0.0)
+        nc.gpsimd.memset(codes["g", 0][:, HALF:], 0)
+        nc.gpsimd.memset(scales["g", 0][:, HALF:], 0)
+
+        picked = {0: tile([P, N, 2], U32, "picked0")[:]}
+        shared = tile([P, 3, N], U32, "shared")
+        bias_sb = tile([P, B, PACK], F32, "bias_sb")
+        x_bf = [flat(shared[:, 1:3, :]).bitcast(BF16), tile_at([P, R * PACK], BF16, "x_bf1", 4)]
+        xm_bf = {(b, h): tile([P, HALF, PACK], BF16, f"xm_bf{b}{h}")[:] for b, h in ((0, 0), (1, 0), (1, 1))}
+        prob = {(b, h): tile([P, PACK, HALF], F32, f"prob{b}{h}") for b in range(B) for h in range(2)}
+        sq = {(b, 0): tile([P, PACK, HALF], F32, f"sq{b}0")[:] for b in range(B)}
+        sq[0, 1] = tile_at([P, PACK, HALF], F32, "sq01", 12)
+        sq[1, 1] = tile_at([P, PACK, HALF], F32, "sq11", 20)
+        err = dict(y_sb)
+        g_bf = {(b, h): tile([P, HALF, PACK], BF16, f"g_bf{b}{h}")[:] for b, h in ((1, 0), (1, 1))}
+        g_bf[0, 0] = tile_at([P, HALF, PACK], BF16, "g_bf00", 0)
+        picked[1] = tile_at([P, N, 2], U32, "picked1", 0)
+        err[0, 1] = tile_at([P, PACK, HALF], F32, "err01", 2)
+        g_bf[0, 1] = tile_at([P, HALF, PACK], BF16, "g_bf01", 8)
+        xm_bf[0, 1] = tile_at([P, HALF, PACK], BF16, "xm_bf01", 10)
+        err[1, 0] = tile_at([P, PACK, HALF], F32, "err10", 8)
+        dense = {(b, c): tile([P, N], F32, f"dense{b}{c}")[:] for b in range(B) for c in range(D // P) if b == 1 or c > 2}
+        dense[0, 2] = tile_at([P, N], F32, "dense02", 2)
+        dense[0, 0] = tile_at([P, N], F32, "dense00", 16)
+        dense[0, 1] = tile_at([P, N], F32, "dense01", 18)
+        g_rows = tile_at([P, PACK, HALF], BF16, "g_rows", 24)
+        late = tile_at([P, HALF], F32, "late", 23.5)
 
         def slots(b, lo, hi):
             return offsets[:, (b * N + lo) // 16 : (b * N + hi) // 16]
@@ -102,11 +122,11 @@ def tile_attend_gsl2_w_kernel(tc, xT, wT, y, wt, xm, offs, out):
             dst = picked[0][:, :, u] if b == 0 else shared[:, u, :]
             nc.vector.tensor_copy(dst, pairs[u][:].indirect(slots(b, 0, N)))
 
-        def cast_w(k, copy):
-            u, lo, hi = chunks[k]
+        def cast_w(k, lo, hi, copy):
+            u, first, last = chunks[k]
             copy(
-                pairs[u][:, lo:hi].bitcast(BF16).rearrange("p (c i e) -> p c e i", i=4, e=2),
-                w_raw[k][:].rearrange("p e (c i) -> p c e i", i=4),
+                pairs[u][:, first + lo : first + hi].bitcast(BF16).rearrange("p (c i e) -> p c e i", i=4, e=2),
+                w_raw[k][:, :, lo:hi].rearrange("p e (c i) -> p c e i", i=4),
             )
 
         def by_fours_src(ap):
@@ -118,67 +138,66 @@ def tile_attend_gsl2_w_kernel(tc, xT, wT, y, wt, xm, offs, out):
         def quantise(kind, b, src, lo, hi, fmt):
             nc.vector.quantize_mx(out=codes[kind, b][:, lo:hi].bitcast(fmt), scales=scales[kind, b][:, lo:hi], in_=src)
 
-        def cast_x(b, lo, hi, copy):
+        def cast_x(b, raw, lo, hi, copy):
             copy(
                 x_bf[b].rearrange("p (t m j) -> p m t j", t=PACK, j=PACK)[:, lo:hi],
-                xT_raw[b][:].rearrange("p j (m t) -> p m t j", t=PACK)[:, lo:hi],
+                raw.rearrange("p j (m t) -> p m t j", t=PACK),
             )
 
-        def scores(b, h):
-            lo, hi = h * HALF, (h + 1) * HALF
-            for u in range(2):
-                bank = psum.tile([P, 2, HALF], F32, name=f"score{h}{u}")
-                for e in range(2):
-                    t = 2 * u + e
-                    nc.tensor.matmul_mx(
-                        out=bank[:, e, :],
-                        lhsT=codes["x", b][:, t * P : (t + 1) * P].bitcast(E4M3),
-                        lhsT_scale=scales["x", b][:, t * P : (t + 1) * P],
-                        rhs=codes["w", b][:, lo:hi].bitcast(E4M3),
-                        rhs_scale=scales["w", b][:, lo:hi],
-                        start=True,
-                        stop=True,
-                    )
-                pair = slice(2 * u, 2 * u + 2)
-                nc.scalar.activation(prob[b][:, pair, lo:hi], bank[:], ACT.Sigmoid)
-                nc.scalar.activation(sq[b][:, pair, lo:hi], prob[b][:, pair, lo:hi], ACT.Square, bias=-0.5)
+        def cast_xm(b, h):
+            nc.scalar.copy(by_fours_dst(xm_bf[b, h]), by_fours_src(xm_raw[b, h]))
 
-        def gradient(b, h):
-            lo, hi = h * HALF, (h + 1) * HALF
-            if b == 0:
-                nc.vector.tensor_tensor(err[b][:, :, lo:hi], y_sb[b][:, :, lo:hi], prob[b][:, :, lo:hi], ALU.subtract)
-                for t in range(PACK):
-                    nc.vector.tensor_scalar(
-                        slope[b][:, t, lo:hi], sq[b][:, t, lo:hi], -0.25, wt_sb[:, b, t : t + 1], ALU.add, ALU.mult
-                    )
-            else:
-                nc.gpsimd.tensor_tensor(err[b][:, :, lo:hi], y_sb[b][:, :, lo:hi], prob[b][:, :, lo:hi], ALU.subtract)
-                for t in range(PACK):
-                    nc.scalar.activation(
-                        slope[b][:, t, lo:hi], sq[b][:, t, lo:hi], ACT.Identity,
-                        bias=bias_sb[:, t : t + 1], scale=wt_sb[:, b, t : t + 1],
-                    )
-            if (b, h) == (1, 0):
-                g_rows = tile([P, PACK, HALF], BF16, f"g_rows{h}")
-                nc.gpsimd.tensor_tensor(g_rows[:], slope[b][:, :, lo:hi], err[b][:, :, lo:hi], ALU.mult)
-                nc.scalar.copy(g_bf[b][:, lo:hi, :], g_rows[:].rearrange("p t i -> p i t"))
-            else:
-                nc.vector.tensor_tensor(
-                    by_fours_dst(g_bf[b][:, lo:hi, :]),
-                    by_fours_src(slope[b][:, :, lo:hi]),
-                    by_fours_src(err[b][:, :, lo:hi]),
-                    ALU.mult,
-                )
+        def quantise_xm(b, h):
+            quantise("xm", b, flat(xm_bf[b, h]), h * HALF, (h + 1) * HALF, E4M3)
 
         def quantise_g(b, h):
-            lo, hi = h * HALF, (h + 1) * HALF
-            quantise("g", b, flat(g_bf[b][:, lo:hi, :]), lo, hi, E5M2)
+            quantise("g", b, flat(g_bf[b, h]), h * HALF, (h + 1) * HALF, E5M2)
 
-        def cast_xm(b, lo, hi):
-            nc.scalar.copy(by_fours_dst(xm_bf[b][:, lo:hi, :]), by_fours_src(xm_raw[b][:, :, lo:hi]))
+        def scores(b, h, q):
+            bank = psum.tile([P, PACK, P], F32, name=f"score{h}{q}")
+            cols = slice(h * HALF + q * P, h * HALF + (q + 1) * P)
+            for t in range(PACK):
+                nc.tensor.matmul_mx(
+                    out=bank[:, t, :],
+                    lhsT=codes["x", b][:, t * P : (t + 1) * P].bitcast(E4M3),
+                    lhsT_scale=scales["x", b][:, t * P : (t + 1) * P],
+                    rhs=codes["w", b][:, cols].bitcast(E4M3),
+                    rhs_scale=scales["w", b][:, cols],
+                    start=True,
+                    stop=True,
+                )
+            nc.scalar.activation(prob[b, h][:, :, q * P : (q + 1) * P], bank[:], ACT.Sigmoid)
 
-        def product(b, c, copy):
-            bank = psum.tile([P, N], F32, name=f"grad{c}")
+        def square(b, h, lo, hi):
+            nc.scalar.activation(sq[b, h][:, :, lo:hi], prob[b, h][:, :, lo:hi], ACT.Square, bias=-0.5)
+
+        def error(b, h, lo, hi, engine):
+            engine.tensor_tensor(err[b, h][:, :, lo:hi], y_sb[b, h][:, :, lo:hi], prob[b, h][:, :, lo:hi], ALU.subtract)
+
+        def slope_alu(b, h, lo, hi, engine):
+            for t in range(PACK):
+                engine.tensor_scalar(
+                    sq[b, h][:, t, lo:hi], sq[b, h][:, t, lo:hi], wt_sb[:, b, t : t + 1], bias_sb[:, b, t : t + 1],
+                    ALU.mult, ALU.add,
+                )
+
+        def slope_act(b, h):
+            for t in range(PACK):
+                nc.scalar.activation(
+                    sq[b, h][:, t, :], sq[b, h][:, t, :], ACT.Identity,
+                    bias=bias_sb[:, b, t : t + 1], scale=wt_sb[:, b, t : t + 1],
+                )
+
+        def gradient(b, h, lo, hi):
+            nc.vector.tensor_tensor(
+                by_fours_dst(g_bf[b, h][:, lo:hi, :]),
+                by_fours_src(sq[b, h][:, :, lo:hi]),
+                by_fours_src(err[b, h][:, :, lo:hi]),
+                ALU.mult,
+            )
+
+        def product(b, c, bank_name, lo, hi):
+            bank = psum.tile([P, N], F32, name=bank_name)
             nc.tensor.matmul_mx(
                 out=bank[:],
                 lhsT=codes["xm", b][:, c * P : (c + 1) * P].bitcast(E4M3),
@@ -188,70 +207,87 @@ def tile_attend_gsl2_w_kernel(tc, xT, wT, y, wt, xm, offs, out):
                 start=True,
                 stop=True,
             )
-            if (b, c) == (0, D // P - 1):
-                halves = [tile([P, HALF], F32, "dense03")[:], sq[1][:, PACK - 1, HALF:]]
-                for h in range(2):
-                    copy(halves[h], bank[:, h * HALF : (h + 1) * HALF])
-                return halves
-            if (b, c) == (0, 0):
-                staged = x_bf[1].bitcast(F32)[:, :N]
-            else:
-                staged = tile([P, N], F32, f"dense{b}{c}")[:]
-            copy(staged, bank[:])
-            return [staged]
+            nc.scalar.copy(dense[b, c][:, lo:hi], bank[:, lo:hi])
+            return bank
 
-        def scatter(b, c, halves):
-            width = N // len(halves)
-            for h, piece in enumerate(halves):
-                nc.vector.tensor_copy(windows[c][:].indirect(slots(b, h * width, (h + 1) * width)), piece)
+        def scatter(b, c, lo, hi):
+            nc.vector.tensor_copy(windows[c][:].indirect(slots(b, lo, hi)), dense[b, c][:, lo:hi])
+            if b == B - 1:
+                nc.sync.dma_start(out=out[c * P : (c + 1) * P, :], in_=windows[c][:])
 
-        cast_w(0, nc.scalar.copy)
-        cast_w(1, nc.vector.tensor_copy)
+        cast_w(0, 0, 1024, nc.scalar.copy)
+        cast_w(1, 0, 1024, nc.vector.tensor_copy)
         for b in range(B):
             gather(b, 0)
-        cast_w(2, nc.scalar.copy)
-        cast_w(3, nc.vector.tensor_copy)
-        cast_w(4, nc.vector.tensor_copy)
+        cast_w(2, 0, 1024, nc.scalar.copy)
+        cast_w(3, 0, 512, nc.vector.tensor_copy)
+        cast_w(4, 0, 320, nc.vector.tensor_copy)
+        cast_w(4, 320, 512, nc.scalar.copy)
         gather(0, 1)
-        quantise("w", 0, flat(picked[0][:]).bitcast(BF16), 0, N, E4M3)
-        cast_x(0, 0, 64, nc.scalar.copy)
-        cast_x(0, 64, 96, nc.scalar.copy)
-        cast_x(0, 96, P, nc.vector.tensor_copy)
+        quantise("w", 0, flat(picked[0]).bitcast(BF16), 0, N, E4M3)
+        cast_x(0, x0_raw[0][:], 0, 64, nc.scalar.copy)
+        cast_x(0, x0_raw[1][:, :, :128], 64, 96, nc.scalar.copy)
+        cast_x(0, x0_raw[1][:, :, 128:], 96, 128, nc.vector.tensor_copy)
         for u in range(2):
             quantise("x", 0, x_bf[0][:, u * 1024 : (u + 1) * 1024], u * 256, (u + 1) * 256, E4M3)
         gather(1, 1)
-        nc.vector.tensor_copy(
-            flat(picked[1][:]).bitcast(BF16).rearrange("p (i u e) -> p i u e", u=2, e=2),
-            flat(shared[:, 0:2, :]).bitcast(BF16).rearrange("p (u i e) -> p i u e", u=2, e=2),
-        )
-        for h in range(2):
-            scores(0, h)
-        gradient(0, 0)
-        quantise("w", 1, flat(picked[1][:]).bitcast(BF16), 0, N, E4M3)
-        cast_x(1, 0, P, nc.scalar.copy)
+        nc.gpsimd.tensor_scalar(bias_sb[:], wt_sb[:], -0.25, 0.0, ALU.mult, ALU.add)
+        for q in range(2):
+            scores(0, 0, q)
+            square(0, 0, q * P, (q + 1) * P)
+            error(0, 0, q * P, (q + 1) * P, nc.vector)
+            slope_alu(0, 0, q * P, (q + 1) * P, nc.vector)
+            gradient(0, 0, q * P, (q + 1) * P)
+        for q in range(2):
+            nc.scalar.copy(
+                by_fours_dst(xm_bf[0, 0][:, q * P : (q + 1) * P, :]), by_fours_src(xm_raw[0, 0][:, :, q * P : (q + 1) * P])
+            )
+        quantise_xm(0, 0)
+        quantise_g(0, 0)
+        nc.vector.tensor_copy(picked[1], shared[:, 0:2, :].rearrange("p u i -> p i u"))
+        quantise("w", 1, flat(picked[1]).bitcast(BF16), 0, N, E4M3)
+        for q in range(2):
+            scores(0, 1, q)
+        cast_x(1, x1_raw, 0, P, nc.scalar.copy)
         quantise("x", 1, x_bf[1], 0, R, E4M3)
-        cast_xm(0, 0, D // 2)
-        quantise("xm", 0, flat(xm_bf[0][:, : D // 2, :]), 0, D // 2, E4M3)
-        gradient(0, 1)
+        for c in range(2):
+            product(0, c, f"grad{c}", 0, HALF)
+            scatter(0, c, 0, HALF)
+        error(0, 1, 0, HALF, nc.gpsimd)
+        square(0, 1, 0, HALF)
+        slope_act(0, 1)
+        cast_xm(0, 1)
+        quantise_xm(0, 1)
+        gradient(0, 1, 0, HALF)
+        product(0, 2, "grad2", 0, HALF)
+        quantise_g(0, 1)
+        scatter(0, 2, 0, HALF)
         for h in range(2):
-            quantise_g(0, h)
-        cast_xm(0, D // 2, D)
-        quantise("xm", 0, flat(xm_bf[0][:, D // 2 :, :]), D // 2, D, E4M3)
-        dense = {(0, 0): product(0, 0, nc.vector.tensor_copy), (0, 1): product(0, 1, nc.scalar.copy)}
-        dense[0, 2] = product(0, 2, nc.scalar.copy)
-        nc.gpsimd.tensor_scalar(bias_sb[:], wt_sb[:, 1, :], -0.25, 0.0, ALU.mult, ALU.add)
-        for h in range(2):
-            scores(1, h)
-            gradient(1, h)
-        dense[0, 3] = product(0, 3, nc.scalar.copy)
-        for lo in (0, D // 2):
-            cast_xm(1, lo, lo + D // 2)
-            quantise("xm", 1, flat(xm_bf[1][:, lo : lo + D // 2, :]), lo, lo + D // 2, E4M3)
+            for q in range(2):
+                scores(1, h, q)
+        error(1, 0, 0, HALF, nc.gpsimd)
+        error(1, 1, 0, HALF, nc.gpsimd)
+        for c in range(3):
+            product(0, c, f"grad{(c + 3) % 4}", HALF, N)
+            scatter(0, c, HALF, N)
+        for q in range(2):
+            square(1, 0, q * P, (q + 1) * P)
+        slope_act(1, 0)
+        nc.gpsimd.tensor_tensor(g_rows, sq[1, 0], err[1, 0], ALU.mult)
+        square(1, 1, 0, HALF)
+        slope_act(1, 1)
+        last_bank = product(0, 3, "grad2", 0, HALF)
+        scatter(0, 3, 0, HALF)
+        gradient(1, 1, 0, HALF)
+        nc.scalar.copy(by_fours_dst(g_bf[1, 0]), by_fours_src(g_rows))
+        cast_xm(1, 0)
+        quantise_xm(1, 0)
         for h in range(2):
             quantise_g(1, h)
+        nc.scalar.copy(late, last_bank[:, HALF:])
+        nc.vector.tensor_copy(windows[3][:].indirect(slots(0, HALF, N)), late)
+        cast_xm(1, 1)
+        quantise_xm(1, 1)
         for c in range(D // P):
-            dense[1, c] = product(1, c, nc.scalar.copy)
-        for c in range(D // P):
-            for b in range(B):
-                scatter(b, c, dense[b, c])
-            nc.sync.dma_start(out=out[c * P : (c + 1) * P, :], in_=windows[c][:])
+            product(1, c, f"grad{(c + 3) % 4}", 0, N)
+            scatter(1, c, 0, N)

@@ -67,12 +67,12 @@ def tile_attend_gsl2_w_kernel(tc, xT, wT, y, wt, xm, offs, out):
             nc.sync.dma_start(out=x0_raw[h][:], in_=rows(xT[0])[:, :, half(h)])
         nc.sync.dma_start(out=wt_sb[:], in_=wt.rearrange("b (p t) o -> p b (t o)", t=PACK))
         nc.sync.dma_start(out=xm_raw[0, 0], in_=rows(xm[0])[:, :, half(0)])
-        for h in range(2):
-            nc.sync.dma_start(out=y_sb[0, h], in_=rows(y[0])[:, :, half(h)])
+        nc.sync.dma_start(out=y_sb[0, 0], in_=rows(y[0])[:, :, half(0)])
         nc.sync.dma_start(out=x1_raw, in_=rows(xT[1]))
+        nc.sync.dma_start(out=y_sb[0, 1], in_=rows(y[0])[:, :, half(1)])
         nc.sync.dma_start(out=xm_raw[0, 1], in_=rows(xm[0])[:, :, half(1)])
-        nc.sync.dma_start(out=xm1_raw[:], in_=rows(xm[1]))
         nc.sync.dma_start(out=y1_raw[:], in_=rows(y[1]))
+        nc.sync.dma_start(out=xm1_raw[:], in_=rows(xm[1]))
 
         warm_in = tile([P, 1], F32, "warm_in")
         warm_out = tile([P, 1], F32, "warm_out")
@@ -80,10 +80,12 @@ def tile_attend_gsl2_w_kernel(tc, xT, wT, y, wt, xm, offs, out):
         nc.scalar.activation(warm_out[:], warm_in[:], ACT.Sigmoid)
 
         codes, scales = {}, {}
-        for kind in ("w", "x", "xm", "g"):
-            for b in range(B):
-                codes[kind, b] = tile([P, 512], U32, f"{kind}_codes{b}")
-                scales[kind, b] = tile([P, 512], U8, f"{kind}_scales{b}")
+        for b in range(B):
+            for kind in ("x", "g"):
+                codes[kind, b] = tile([P, 512], U32, f"{kind}_codes{b}")[:]
+            for kind in ("w", "x", "xm", "g"):
+                scales[kind, b] = tile([P, 512], U8, f"{kind}_scales{b}")[:]
+        xm_codes = {(0, 0): tile([P, HALF], U32, "xm_codes00")[:]}
 
         windows = [tile([P, T], F32, f"window{c}") for c in range(D // P)]
         for c, window in enumerate(windows):
@@ -92,35 +94,44 @@ def tile_attend_gsl2_w_kernel(tc, xT, wT, y, wt, xm, offs, out):
         nc.gpsimd.memset(scales["g", 0][:, HALF:], 0)
 
         picked = {0: tile([P, N, 2], U32, "picked0")[:]}
-        shared = tile([P, 3, N], U32, "shared")
         bias_sb = tile([P, B, PACK], F32, "bias_sb")
-        x_bf = [flat(shared[:, 1:3, :]).bitcast(BF16), tile_at([P, R * PACK], BF16, "x_bf1", 4)]
+        x_bf = [tile([P, R * PACK], BF16, "x_bf0")[:], tile_at([P, R * PACK], BF16, "x_bf1", 4)]
         xm_bf = {(b, h): tile([P, HALF, PACK], BF16, f"xm_bf{b}{h}")[:] for b, h in ((0, 0), (1, 0), (1, 1))}
-        prob = {(b, h): tile([P, PACK, HALF], F32, f"prob{b}{h}") for b in range(B) for h in range(2)}
+        prob = {(b, h): tile([P, PACK, HALF], F32, f"prob{b}{h}")[:] for b, h in ((0, 0), (0, 1), (1, 0))}
+        prob[1, 1] = tile_at([P, PACK, HALF], F32, "prob11", 26)
         sq = {(b, 0): tile([P, PACK, HALF], F32, f"sq{b}0")[:] for b in range(B)}
         sq[0, 1] = tile_at([P, PACK, HALF], F32, "sq01", 12)
         sq[1, 1] = tile_at([P, PACK, HALF], F32, "sq11", 20)
         err = dict(y_sb)
-        g_bf = {(b, h): tile([P, HALF, PACK], BF16, f"g_bf{b}{h}")[:] for b, h in ((1, 0), (1, 1))}
-        g_bf[0, 0] = tile_at([P, HALF, PACK], BF16, "g_bf00", 0)
+        g_bf = {(1, 1): tile([P, HALF, PACK], BF16, "g_bf11")[:]}
+        g_bf[1, 0] = tile([P, HALF, PACK], BF16, "g_bf10")[:]
+        for h in range(2):
+            xm_codes[1, h] = tile_at([P, HALF], U32, f"xm_codes1{h}", 28 + h)
+        g_bf[0, 0] = tile_at([P, HALF, PACK], BF16, "g_bf00", 30)
+        codes["w", 0] = tile([P, N], U32, "w_codes0")[:]
+        codes["w", 1] = tile_at([P, N], U32, "w_codes1", 30)
+        g_rows = tile_at([P, PACK, HALF], BF16, "g_rows", 24)
         picked[1] = tile_at([P, N, 2], U32, "picked1", 0)
         err[0, 1] = tile_at([P, PACK, HALF], F32, "err01", 2)
         g_bf[0, 1] = tile_at([P, HALF, PACK], BF16, "g_bf01", 8)
         xm_bf[0, 1] = tile_at([P, HALF, PACK], BF16, "xm_bf01", 10)
         err[1, 0] = tile_at([P, PACK, HALF], F32, "err10", 8)
-        dense = {(b, c): tile([P, N], F32, f"dense{b}{c}")[:] for b in range(B) for c in range(D // P) if b == 1 or c > 2}
-        dense[0, 2] = tile_at([P, N], F32, "dense02", 2)
-        dense[0, 0] = tile_at([P, N], F32, "dense00", 16)
-        dense[0, 1] = tile_at([P, N], F32, "dense01", 18)
-        g_rows = tile_at([P, PACK, HALF], BF16, "g_rows", 24)
-        late = tile_at([P, HALF], F32, "late", 23.5)
+        err[1, 1] = tile_at([P, PACK, HALF], F32, "err11", 8)
+        dense = {(1, c, 0): tile([P, N], F32, f"dense1{c}")[:] for c in range(D // P)}
+        dense[0, 0, 0] = tile_at([P, HALF], F32, "dense00a", 16)
+        dense[0, 1, 0] = tile_at([P, HALF], F32, "dense01a", 17)
+        xm_codes[0, 1] = tile_at([P, HALF], U32, "xm_codes01", 17)
+        dense[0, 2, 0] = tile_at([P, HALF], F32, "dense02a", 2)
+        dense[0, 3, 0] = tile([P, HALF], F32, "dense03a")[:]
+        for c in range(3):
+            dense[0, c, HALF] = tile([P, HALF], F32, f"dense0{c}b")[:]
+        dense[0, 3, HALF] = tile_at([P, HALF], F32, "dense03b", 23.5)
 
         def slots(b, lo, hi):
             return offsets[:, (b * N + lo) // 16 : (b * N + hi) // 16]
 
         def gather(b, u):
-            dst = picked[0][:, :, u] if b == 0 else shared[:, u, :]
-            nc.vector.tensor_copy(dst, pairs[u][:].indirect(slots(b, 0, N)))
+            nc.vector.tensor_copy(picked[b][:, :, u], pairs[u][:].indirect(slots(b, 0, N)))
 
         def cast_w(k, lo, hi, copy):
             u, first, last = chunks[k]
@@ -148,7 +159,9 @@ def tile_attend_gsl2_w_kernel(tc, xT, wT, y, wt, xm, offs, out):
             nc.scalar.copy(by_fours_dst(xm_bf[b, h]), by_fours_src(xm_raw[b, h]))
 
         def quantise_xm(b, h):
-            quantise("xm", b, flat(xm_bf[b, h]), h * HALF, (h + 1) * HALF, E4M3)
+            nc.vector.quantize_mx(
+                out=xm_codes[b, h].bitcast(E4M3), scales=scales["xm", b][:, half(h)], in_=flat(xm_bf[b, h])
+            )
 
         def quantise_g(b, h):
             quantise("g", b, flat(g_bf[b, h]), h * HALF, (h + 1) * HALF, E5M2)
@@ -200,23 +213,24 @@ def tile_attend_gsl2_w_kernel(tc, xT, wT, y, wt, xm, offs, out):
             bank = psum.tile([P, N], F32, name=bank_name)
             nc.tensor.matmul_mx(
                 out=bank[:],
-                lhsT=codes["xm", b][:, c * P : (c + 1) * P].bitcast(E4M3),
+                lhsT=xm_codes[b, c // 2][:, (c % 2) * P : (c % 2 + 1) * P].bitcast(E4M3),
                 lhsT_scale=scales["xm", b][:, c * P : (c + 1) * P],
-                rhs=codes["g", b][:].bitcast(E5M2),
-                rhs_scale=scales["g", b][:],
+                rhs=codes["g", b].bitcast(E5M2),
+                rhs_scale=scales["g", b],
                 start=True,
                 stop=True,
             )
-            nc.scalar.copy(dense[b, c][:, lo:hi], bank[:, lo:hi])
+            nc.scalar.copy(dense[b, c, lo], bank[:, lo:hi])
             return bank
 
         def scatter(b, c, lo, hi):
-            nc.vector.tensor_copy(windows[c][:].indirect(slots(b, lo, hi)), dense[b, c][:, lo:hi])
+            nc.vector.tensor_copy(windows[c][:].indirect(slots(b, lo, hi)), dense[b, c, lo])
             if b == B - 1:
                 nc.sync.dma_start(out=out[c * P : (c + 1) * P, :], in_=windows[c][:])
 
         cast_w(0, 0, 1024, nc.scalar.copy)
-        cast_w(1, 0, 1024, nc.vector.tensor_copy)
+        cast_w(1, 0, 704, nc.vector.tensor_copy)
+        cast_w(1, 704, 1024, nc.scalar.copy)
         for b in range(B):
             gather(b, 0)
         cast_w(2, 0, 1024, nc.scalar.copy)
@@ -225,26 +239,21 @@ def tile_attend_gsl2_w_kernel(tc, xT, wT, y, wt, xm, offs, out):
         cast_w(4, 320, 512, nc.scalar.copy)
         gather(0, 1)
         quantise("w", 0, flat(picked[0]).bitcast(BF16), 0, N, E4M3)
-        cast_x(0, x0_raw[0][:], 0, 64, nc.scalar.copy)
-        cast_x(0, x0_raw[1][:, :, :128], 64, 96, nc.scalar.copy)
-        cast_x(0, x0_raw[1][:, :, 128:], 96, 128, nc.vector.tensor_copy)
+        for h in range(2):
+            cast_x(0, x0_raw[h][:], 64 * h, 64 * (h + 1), nc.scalar.copy)
         for u in range(2):
             quantise("x", 0, x_bf[0][:, u * 1024 : (u + 1) * 1024], u * 256, (u + 1) * 256, E4M3)
         gather(1, 1)
         nc.gpsimd.tensor_scalar(bias_sb[:], wt_sb[:], -0.25, 0.0, ALU.mult, ALU.add)
+        nc.vector.tensor_copy(by_fours_dst(xm_bf[0, 0]), by_fours_src(xm_raw[0, 0]))
         for q in range(2):
             scores(0, 0, q)
             square(0, 0, q * P, (q + 1) * P)
             error(0, 0, q * P, (q + 1) * P, nc.vector)
             slope_alu(0, 0, q * P, (q + 1) * P, nc.vector)
             gradient(0, 0, q * P, (q + 1) * P)
-        for q in range(2):
-            nc.scalar.copy(
-                by_fours_dst(xm_bf[0, 0][:, q * P : (q + 1) * P, :]), by_fours_src(xm_raw[0, 0][:, :, q * P : (q + 1) * P])
-            )
         quantise_xm(0, 0)
         quantise_g(0, 0)
-        nc.vector.tensor_copy(picked[1], shared[:, 0:2, :].rearrange("p u i -> p i u"))
         quantise("w", 1, flat(picked[1]).bitcast(BF16), 0, N, E4M3)
         for q in range(2):
             scores(0, 1, q)
@@ -259,33 +268,36 @@ def tile_attend_gsl2_w_kernel(tc, xT, wT, y, wt, xm, offs, out):
         cast_xm(0, 1)
         quantise_xm(0, 1)
         gradient(0, 1, 0, HALF)
+        for q in range(2):
+            scores(1, 0, q)
+        square(1, 0, 0, HALF)
         product(0, 2, "grad2", 0, HALF)
         quantise_g(0, 1)
         scatter(0, 2, 0, HALF)
-        for h in range(2):
-            for q in range(2):
-                scores(1, h, q)
         error(1, 0, 0, HALF, nc.gpsimd)
-        error(1, 1, 0, HALF, nc.gpsimd)
-        for c in range(3):
-            product(0, c, f"grad{(c + 3) % 4}", HALF, N)
-            scatter(0, c, HALF, N)
-        for q in range(2):
-            square(1, 0, q * P, (q + 1) * P)
+        product(0, 0, "grad3", HALF, N)
+        scatter(0, 0, HALF, N)
         slope_act(1, 0)
         nc.gpsimd.tensor_tensor(g_rows, sq[1, 0], err[1, 0], ALU.mult)
+        product(0, 1, "grad0", HALF, N)
+        scatter(0, 1, HALF, N)
+        for q in range(2):
+            scores(1, 1, q)
+        error(1, 1, 0, HALF, nc.gpsimd)
+        product(0, 2, "grad1", HALF, N)
+        scatter(0, 2, HALF, N)
         square(1, 1, 0, HALF)
-        slope_act(1, 1)
         last_bank = product(0, 3, "grad2", 0, HALF)
         scatter(0, 3, 0, HALF)
-        gradient(1, 1, 0, HALF)
-        nc.scalar.copy(by_fours_dst(g_bf[1, 0]), by_fours_src(g_rows))
+        slope_act(1, 1)
         cast_xm(1, 0)
+        nc.scalar.copy(by_fours_dst(g_bf[1, 0]), by_fours_src(g_rows))
+        gradient(1, 1, 0, HALF)
         quantise_xm(1, 0)
-        for h in range(2):
+        for h in (1, 0):
             quantise_g(1, h)
-        nc.scalar.copy(late, last_bank[:, HALF:])
-        nc.vector.tensor_copy(windows[3][:].indirect(slots(0, HALF, N)), late)
+        nc.scalar.copy(dense[0, 3, HALF], last_bank[:, HALF:])
+        scatter(0, 3, HALF, N)
         cast_xm(1, 1)
         quantise_xm(1, 1)
         for c in range(D // P):

@@ -187,15 +187,15 @@ def tile_attend_gsl2_w_kernel(tc, xT, wT, y, wt, xm, offs, out):
         def error(b, h, lo, hi, engine):
             engine.tensor_tensor(err[b, h][:, :, lo:hi], y_sb[b, h][:, :, lo:hi], prob[b, h][:, :, lo:hi], ALU.subtract)
 
-        def slope_alu(b, h, lo, hi, engine):
-            for t in range(PACK):
+        def slope_alu(b, h, lo, hi, engine, places=range(PACK)):
+            for t in places:
                 engine.tensor_scalar(
                     sq[b, h][:, t, lo:hi], sq[b, h][:, t, lo:hi], wt_sb[:, b, t : t + 1], bias_sb[:, b, t : t + 1],
                     ALU.mult, ALU.add,
                 )
 
-        def slope_act(b, h):
-            for t in range(PACK):
+        def slope_act(b, h, places=range(PACK)):
+            for t in places:
                 nc.scalar.activation(
                     sq[b, h][:, t, :], sq[b, h][:, t, :], ACT.Identity,
                     bias=bias_sb[:, b, t : t + 1], scale=wt_sb[:, b, t : t + 1],
@@ -257,14 +257,16 @@ def tile_attend_gsl2_w_kernel(tc, xT, wT, y, wt, xm, offs, out):
         quantise("w", 1, flat(picked[1]).bitcast(BF16), 0, N, E4M3)
         for q in range(2):
             scores(0, 1, q)
-        cast_x(1, x1_raw, 0, P, nc.scalar.copy)
+        cast_x(1, x1_raw[:, :, :384], 0, 96, nc.scalar.copy)
+        cast_x(1, x1_raw[:, :, 384:], 96, P, nc.vector.tensor_copy)
         quantise("x", 1, x_bf[1], 0, R, E4M3)
         for c in range(2):
             product(0, c, f"grad{c}", 0, HALF)
             scatter(0, c, 0, HALF)
         error(0, 1, 0, HALF, nc.gpsimd)
         square(0, 1, 0, HALF)
-        slope_act(0, 1)
+        slope_act(0, 1, range(2))
+        slope_alu(0, 1, 0, HALF, nc.gpsimd, range(2, 4))
         cast_xm(0, 1)
         quantise_xm(0, 1)
         gradient(0, 1, 0, HALF)

@@ -74,10 +74,10 @@ def tile_attend_gsl2_w_kernel(tc, xT, wT, y, wt, xm, offs, out):
         nc.sync.dma_start(out=y1_raw[:], in_=rows(y[1]))
         nc.sync.dma_start(out=xm1_raw[:], in_=rows(xm[1]))
 
-        warm_in = tile([P, 1], F32, "warm_in")
-        warm_out = tile([P, 1], F32, "warm_out")
-        nc.gpsimd.memset(warm_in[:], 0.0)
-        nc.scalar.activation(warm_out[:], warm_in[:], ACT.Sigmoid)
+        zero = tile([P, 1], F32, "zero")
+        centre = tile([P, 1], F32, "centre")
+        nc.gpsimd.memset(zero[:], 0.0)
+        nc.scalar.activation(centre[:], zero[:], ACT.Sigmoid)
 
         codes, scales = {}, {}
         for b in range(B):
@@ -98,25 +98,26 @@ def tile_attend_gsl2_w_kernel(tc, xT, wT, y, wt, xm, offs, out):
         x_bf = [tile([P, R * PACK], BF16, "x_bf0")[:], tile_at([P, R * PACK], BF16, "x_bf1", 4)]
         xm_bf = {(b, h): tile([P, HALF, PACK], BF16, f"xm_bf{b}{h}")[:] for b, h in ((0, 0), (1, 0), (1, 1))}
         prob = {(b, h): tile([P, PACK, HALF], F32, f"prob{b}{h}")[:] for b, h in ((0, 0), (0, 1), (1, 0))}
-        prob[1, 1] = tile_at([P, PACK, HALF], F32, "prob11", 26)
+        prob[1, 1] = tile([P, PACK, HALF], F32, "prob11")[:]
         sq = {(b, 0): tile([P, PACK, HALF], F32, f"sq{b}0")[:] for b in range(B)}
         sq[0, 1] = tile_at([P, PACK, HALF], F32, "sq01", 12)
         sq[1, 1] = tile_at([P, PACK, HALF], F32, "sq11", 20)
         err = dict(y_sb)
-        g_bf = {(1, 1): tile([P, HALF, PACK], BF16, "g_bf11")[:]}
+        g_bf = {}
         g_bf[1, 0] = tile([P, HALF, PACK], BF16, "g_bf10")[:]
         for h in range(2):
-            xm_codes[1, h] = tile_at([P, HALF], U32, f"xm_codes1{h}", 28 + h)
+            xm_codes[1, h] = tile_at([P, HALF], U32, f"xm_codes1{h}", 34 + h)
         g_bf[0, 0] = tile_at([P, HALF, PACK], BF16, "g_bf00", 30)
         codes["w", 0] = tile([P, N], U32, "w_codes0")[:]
         codes["w", 1] = tile_at([P, N], U32, "w_codes1", 30)
         g_rows = tile_at([P, PACK, HALF], BF16, "g_rows", 24)
         picked[1] = tile_at([P, N, 2], U32, "picked1", 0)
         err[0, 1] = tile_at([P, PACK, HALF], F32, "err01", 2)
-        g_bf[0, 1] = tile_at([P, HALF, PACK], BF16, "g_bf01", 8)
-        xm_bf[0, 1] = tile_at([P, HALF, PACK], BF16, "xm_bf01", 10)
-        err[1, 0] = tile_at([P, PACK, HALF], F32, "err10", 8)
-        err[1, 1] = tile_at([P, PACK, HALF], F32, "err11", 8)
+        g_bf[0, 1] = tile_at([P, HALF, PACK], BF16, "g_bf01", 35)
+        xm_bf[0, 1] = tile([P, HALF, PACK], BF16, "xm_bf01")[:]
+        err[1, 0] = tile_at([P, PACK, HALF], F32, "err10", 32)
+        err[1, 1] = tile_at([P, PACK, HALF], F32, "err11", 36)
+        g_bf[1, 1] = tile_at([P, HALF, PACK], BF16, "g_bf11", 32)
         dense = {(1, c, 0): tile([P, N], F32, f"dense1{c}")[:] for c in range(D // P)}
         dense[0, 0, 0] = tile_at([P, HALF], F32, "dense00a", 16)
         dense[0, 1, 0] = tile_at([P, HALF], F32, "dense01a", 17)
@@ -151,16 +152,18 @@ def tile_attend_gsl2_w_kernel(tc, xT, wT, y, wt, xm, offs, out):
 
         def cast_x(b, raw, lo, hi, copy):
             copy(
-                x_bf[b].rearrange("p (t m j) -> p m t j", t=PACK, j=PACK)[:, lo:hi],
-                raw.rearrange("p j (m t) -> p m t j", t=PACK),
+                x_bf[b].rearrange("p (u e m j) -> p u m j e", u=2, e=2, j=PACK)[:, :, lo:hi],
+                raw.rearrange("p j (m u e) -> p u m j e", u=2, e=2),
             )
 
-        def cast_xm(b, h):
-            nc.scalar.copy(by_fours_dst(xm_bf[b, h]), by_fours_src(xm_raw[b, h]))
+        def cast_xm(b, h, lo=0, hi=HALF):
+            nc.scalar.copy(by_fours_dst(xm_bf[b, h][:, lo:hi, :]), by_fours_src(xm_raw[b, h][:, :, lo:hi]))
 
-        def quantise_xm(b, h):
+        def quantise_xm(b, h, lo=0, hi=HALF):
             nc.vector.quantize_mx(
-                out=xm_codes[b, h].bitcast(E4M3), scales=scales["xm", b][:, half(h)], in_=flat(xm_bf[b, h])
+                out=xm_codes[b, h][:, lo:hi].bitcast(E4M3),
+                scales=scales["xm", b][:, h * HALF + lo : h * HALF + hi],
+                in_=flat(xm_bf[b, h][:, lo:hi, :]),
             )
 
         def quantise_g(b, h):
@@ -182,7 +185,7 @@ def tile_attend_gsl2_w_kernel(tc, xT, wT, y, wt, xm, offs, out):
             nc.scalar.activation(prob[b, h][:, :, q * P : (q + 1) * P], bank[:], ACT.Sigmoid)
 
         def square(b, h, lo, hi):
-            nc.scalar.activation(sq[b, h][:, :, lo:hi], prob[b, h][:, :, lo:hi], ACT.Square, bias=-0.5)
+            nc.scalar.activation(sq[b, h][:, :, lo:hi], prob[b, h][:, :, lo:hi], ACT.Square, bias=centre[:], scale=-1.0)
 
         def error(b, h, lo, hi, engine):
             engine.tensor_tensor(err[b, h][:, :, lo:hi], y_sb[b, h][:, :, lo:hi], prob[b, h][:, :, lo:hi], ALU.subtract)
@@ -277,29 +280,31 @@ def tile_attend_gsl2_w_kernel(tc, xT, wT, y, wt, xm, offs, out):
         quantise_g(0, 1)
         scatter(0, 2, 0, HALF)
         error(1, 0, 0, HALF, nc.gpsimd)
+        scores(1, 1, 0)
         product(0, 0, "grad3", HALF, N)
         scatter(0, 0, HALF, N)
-        slope_act(1, 0)
-        nc.gpsimd.tensor_tensor(g_rows, sq[1, 0], err[1, 0], ALU.mult)
+        scores(1, 1, 1)
+        error(1, 1, 0, HALF, nc.gpsimd)
         product(0, 1, "grad0", HALF, N)
         scatter(0, 1, HALF, N)
-        for q in range(2):
-            scores(1, 1, q)
-        error(1, 1, 0, HALF, nc.gpsimd)
+        slope_act(1, 0)
+        nc.gpsimd.tensor_tensor(g_rows, sq[1, 0], err[1, 0], ALU.mult)
         product(0, 2, "grad1", HALF, N)
         scatter(0, 2, HALF, N)
         square(1, 1, 0, HALF)
         last_bank = product(0, 3, "grad2", 0, HALF)
         scatter(0, 3, 0, HALF)
         slope_act(1, 1)
-        cast_xm(1, 0)
+        cast_xm(1, 0, 0, P)
         nc.scalar.copy(by_fours_dst(g_bf[1, 0]), by_fours_src(g_rows))
         gradient(1, 1, 0, HALF)
-        quantise_xm(1, 0)
+        quantise_xm(1, 0, 0, P)
         for h in (1, 0):
             quantise_g(1, h)
         nc.scalar.copy(dense[0, 3, HALF], last_bank[:, HALF:])
         scatter(0, 3, HALF, N)
+        cast_xm(1, 0, P, HALF)
+        quantise_xm(1, 0, P, HALF)
         cast_xm(1, 1)
         quantise_xm(1, 1)
         for c in range(D // P):

@@ -48,7 +48,7 @@ def tile_attend_gsl2_w_kernel(tc, xT, wT, y, wt, xm, offs, out):
         pairs = [tile([P, T], U32, f"pair{u}") for u in range(2)]
         chunks = [(0, 0, 1024), (0, 1024, 2048), (1, 0, 1024), (1, 1024, 1536), (1, 1536, 2048)]
         w_raw = [tile([P, 2, hi - lo], F32, f"w_raw{u}_{lo}") for u, lo, hi in chunks]
-        x0_raw = [tile([P, PACK, HALF], F32, f"x0_raw{h}") for h in range(2)]
+        x0_raw = [tile([P, PACK, HALF], F32, "x0_raw0")[:], tile_at([P, PACK, HALF], F32, "x0_raw1", 0)]
         x1_raw = tile_at([P, PACK, R], F32, "x1_raw", 12)
         xm1_raw = tile([P, PACK, D], F32, "xm1_raw")
         y1_raw = tile([P, PACK, N], F32, "y1_raw")
@@ -64,7 +64,7 @@ def tile_attend_gsl2_w_kernel(tc, xT, wT, y, wt, xm, offs, out):
             if k == 0:
                 nc.sync.dma_start(offsets[:], offs)
         for h in range(2):
-            nc.sync.dma_start(out=x0_raw[h][:], in_=rows(xT[0])[:, :, half(h)])
+            nc.sync.dma_start(out=x0_raw[h], in_=rows(xT[0])[:, :, half(h)])
         nc.sync.dma_start(out=wt_sb[:], in_=wt.rearrange("b (p t) o -> p b (t o)", t=PACK))
         nc.sync.dma_start(out=xm_raw[0, 0], in_=rows(xm[0])[:, :, half(0)])
         nc.sync.dma_start(out=y_sb[0, 0], in_=rows(y[0])[:, :, half(0)])
@@ -94,6 +94,7 @@ def tile_attend_gsl2_w_kernel(tc, xT, wT, y, wt, xm, offs, out):
         nc.gpsimd.memset(scales["g", 0][:, HALF:], 0)
 
         picked = {0: tile([P, N, 2], U32, "picked0")[:]}
+        planes = tile([P, 2, N], U32, "planes")
         bias_sb = tile([P, B, PACK], F32, "bias_sb")
         x_bf = [tile([P, R * PACK], BF16, "x_bf0")[:], tile_at([P, R * PACK], BF16, "x_bf1", 4)]
         xm_bf = {(b, h): tile([P, HALF, PACK], BF16, f"xm_bf{b}{h}")[:] for b, h in ((0, 0), (1, 0), (1, 1))}
@@ -132,7 +133,8 @@ def tile_attend_gsl2_w_kernel(tc, xT, wT, y, wt, xm, offs, out):
             return offsets[:, (b * N + lo) // 16 : (b * N + hi) // 16]
 
         def gather(b, u):
-            nc.vector.tensor_copy(picked[b][:, :, u], pairs[u][:].indirect(slots(b, 0, N)))
+            dst = picked[0][:, :, u] if b == 0 else planes[:, u, :]
+            nc.vector.tensor_copy(dst, pairs[u][:].indirect(slots(b, 0, N)))
 
         def cast_w(k, lo, hi, copy):
             u, first, last = chunks[k]
@@ -242,11 +244,12 @@ def tile_attend_gsl2_w_kernel(tc, xT, wT, y, wt, xm, offs, out):
         cast_w(4, 320, 512, nc.scalar.copy)
         gather(0, 1)
         quantise("w", 0, flat(picked[0]).bitcast(BF16), 0, N, E4M3)
+        gather(1, 1)
         for h in range(2):
-            cast_x(0, x0_raw[h][:], 64 * h, 64 * (h + 1), nc.scalar.copy)
+            cast_x(0, x0_raw[h], 64 * h, 64 * (h + 1), nc.scalar.copy)
         for u in range(2):
             quantise("x", 0, x_bf[0][:, u * 1024 : (u + 1) * 1024], u * 256, (u + 1) * 256, E4M3)
-        gather(1, 1)
+        nc.scalar.copy(picked[1], planes[:].rearrange("p u i -> p i u"))
         nc.gpsimd.tensor_scalar(bias_sb[:], wt_sb[:], -0.25, 0.0, ALU.mult, ALU.add)
         nc.vector.tensor_copy(by_fours_dst(xm_bf[0, 0]), by_fours_src(xm_raw[0, 0]))
         for q in range(2):

@@ -92,6 +92,8 @@ def tile_attend_gsl2_w_kernel(tc, xT, wT, y, wt, xm, offs, out):
             (nc.vector if c < 3 else nc.gpsimd).memset(window[:], 0.0)
         nc.gpsimd.memset(codes["g", 0][:, HALF:], 0)
         nc.gpsimd.memset(scales["g", 0][:, HALF:], 0)
+        nc.gpsimd.memset(codes["g", 1][:, HALF:], 0)
+        nc.gpsimd.memset(scales["g", 1][:, HALF:], 0)
 
         picked = {0: tile([P, N, 2], U32, "picked0")[:]}
         planes = tile([P, 2, N], U32, "planes")
@@ -105,21 +107,23 @@ def tile_attend_gsl2_w_kernel(tc, xT, wT, y, wt, xm, offs, out):
         sq[1, 1] = tile_at([P, PACK, HALF], F32, "sq11", 20)
         err = dict(y_sb)
         g_bf = {}
-        g_bf[1, 0] = tile([P, HALF, PACK], BF16, "g_bf10")[:]
-        for h in range(2):
-            xm_codes[1, h] = tile_at([P, HALF], U32, f"xm_codes1{h}", 34 + h)
+        g_bf[1, 0] = tile_at([P, HALF, PACK], BF16, "g_bf10", 40)
+        xm1_first = tile_at([P, P], U32, "xm1_first", 34)
         g_bf[0, 0] = tile_at([P, HALF, PACK], BF16, "g_bf00", 30)
         codes["w", 0] = tile([P, N], U32, "w_codes0")[:]
         codes["w", 1] = tile_at([P, N], U32, "w_codes1", 30)
-        g_rows = tile_at([P, PACK, HALF], BF16, "g_rows", 24)
         picked[1] = tile_at([P, N, 2], U32, "picked1", 0)
         err[0, 1] = tile_at([P, PACK, HALF], F32, "err01", 2)
         g_bf[0, 1] = tile_at([P, HALF, PACK], BF16, "g_bf01", 35)
         xm_bf[0, 1] = tile([P, HALF, PACK], BF16, "xm_bf01")[:]
         err[1, 0] = tile_at([P, PACK, HALF], F32, "err10", 32)
         err[1, 1] = tile_at([P, PACK, HALF], F32, "err11", 36)
-        g_bf[1, 1] = tile_at([P, HALF, PACK], BF16, "g_bf11", 32)
-        dense = {(1, c, 0): tile([P, N], F32, f"dense1{c}")[:] for c in range(D // P)}
+        g_late = [tile([P, P, PACK], BF16, "g_late0")[:], tile_at([P, P, PACK], BF16, "g_late1", 41)]
+        xm1_second = tile_at([P, P], U32, "xm1_second", 37)
+        xm_codes[1, 1] = tile_at([P, HALF], U32, "xm_codes11", 38)
+        dense = {(1, c, 0): tile([P, N], F32, f"dense1{c}")[:] for c in range(1, D // P)}
+        dense[1, 0, 0] = tile_at([P, HALF], F32, "dense10a", 36)
+        dense[1, 0, HALF] = tile([P, HALF], F32, "dense10b")[:]
         dense[0, 0, 0] = tile_at([P, HALF], F32, "dense00a", 16)
         dense[0, 1, 0] = tile_at([P, HALF], F32, "dense01a", 17)
         xm_codes[0, 1] = tile_at([P, HALF], U32, "xm_codes01", 17)
@@ -127,7 +131,7 @@ def tile_attend_gsl2_w_kernel(tc, xT, wT, y, wt, xm, offs, out):
         dense[0, 3, 0] = tile([P, HALF], F32, "dense03a")[:]
         for c in range(3):
             dense[0, c, HALF] = tile([P, HALF], F32, f"dense0{c}b")[:]
-        dense[0, 3, HALF] = tile_at([P, HALF], F32, "dense03b", 23.5)
+        dense[0, 3, HALF] = tile_at([P, HALF], F32, "dense03b", 32)
 
         def slots(b, lo, hi):
             return offsets[:, (b * N + lo) // 16 : (b * N + hi) // 16]
@@ -199,10 +203,10 @@ def tile_attend_gsl2_w_kernel(tc, xT, wT, y, wt, xm, offs, out):
                     ALU.mult, ALU.add,
                 )
 
-        def slope_act(b, h, places=range(PACK)):
+        def slope_act(b, h, places=range(PACK), lo=0, hi=HALF):
             for t in places:
                 nc.scalar.activation(
-                    sq[b, h][:, t, :], sq[b, h][:, t, :], ACT.Identity,
+                    sq[b, h][:, t, lo:hi], sq[b, h][:, t, lo:hi], ACT.Identity,
                     bias=bias_sb[:, b, t : t + 1], scale=wt_sb[:, b, t : t + 1],
                 )
 
@@ -214,11 +218,31 @@ def tile_attend_gsl2_w_kernel(tc, xT, wT, y, wt, xm, offs, out):
                 ALU.mult,
             )
 
+        def gradient_pool(b, h, lo, hi, dst):
+            nc.gpsimd.tensor_tensor(
+                dst.rearrange("p (c i) j -> p c j i", i=2),
+                sq[b, h][:, :, lo:hi].rearrange("p j (c i) -> p c j i", i=2),
+                err[b, h][:, :, lo:hi].rearrange("p j (c i) -> p c j i", i=2),
+                ALU.mult,
+            )
+
+        def xm_block(b, c):
+            if b == 1 and c < 2:
+                return (xm1_first, xm1_second)[c]
+            return xm_codes[b, c // 2][:, (c % 2) * P : (c % 2 + 1) * P]
+
+        def quantise_xm_block(b, c):
+            nc.vector.quantize_mx(
+                out=xm_block(b, c).bitcast(E4M3),
+                scales=scales["xm", b][:, c * P : (c + 1) * P],
+                in_=flat(xm_bf[b, c // 2][:, (c % 2) * P : (c % 2 + 1) * P, :]),
+            )
+
         def product(b, c, bank_name, lo, hi):
             bank = psum.tile([P, N], F32, name=bank_name)
             nc.tensor.matmul_mx(
                 out=bank[:],
-                lhsT=xm_codes[b, c // 2][:, (c % 2) * P : (c % 2 + 1) * P].bitcast(E4M3),
+                lhsT=xm_block(b, c).bitcast(E4M3),
                 lhsT_scale=scales["xm", b][:, c * P : (c + 1) * P],
                 rhs=codes["g", b].bitcast(E5M2),
                 rhs_scale=scales["g", b],
@@ -230,7 +254,7 @@ def tile_attend_gsl2_w_kernel(tc, xT, wT, y, wt, xm, offs, out):
 
         def scatter(b, c, lo, hi):
             nc.vector.tensor_copy(windows[c][:].indirect(slots(b, lo, hi)), dense[b, c, lo])
-            if b == B - 1:
+            if b == B - 1 and hi == N:
                 nc.sync.dma_start(out=out[c * P : (c + 1) * P, :], in_=windows[c][:])
 
         cast_w(0, 0, 1024, nc.scalar.copy)
@@ -291,25 +315,32 @@ def tile_attend_gsl2_w_kernel(tc, xT, wT, y, wt, xm, offs, out):
         product(0, 1, "grad0", HALF, N)
         scatter(0, 1, HALF, N)
         slope_act(1, 0)
-        nc.gpsimd.tensor_tensor(g_rows, sq[1, 0], err[1, 0], ALU.mult)
+        gradient_pool(1, 0, 0, HALF, g_bf[1, 0])
         product(0, 2, "grad1", HALF, N)
         scatter(0, 2, HALF, N)
-        square(1, 1, 0, HALF)
+        square(1, 1, 0, P)
         last_bank = product(0, 3, "grad2", 0, HALF)
         scatter(0, 3, 0, HALF)
-        slope_act(1, 1)
+        slope_act(1, 1, range(PACK), 0, P)
+        gradient_pool(1, 1, 0, P, g_late[0])
+        square(1, 1, P, HALF)
+        slope_act(1, 1, range(PACK), P, HALF)
         cast_xm(1, 0, 0, P)
-        nc.scalar.copy(by_fours_dst(g_bf[1, 0]), by_fours_src(g_rows))
-        gradient(1, 1, 0, HALF)
-        quantise_xm(1, 0, 0, P)
-        for h in (1, 0):
-            quantise_g(1, h)
+        quantise_g(1, 0)
+        quantise_xm_block(1, 0)
         nc.scalar.copy(dense[0, 3, HALF], last_bank[:, HALF:])
         scatter(0, 3, HALF, N)
+        gradient_pool(1, 1, P, HALF, g_late[1])
+        product(1, 0, "grad3", 0, HALF)
+        for q in range(2):
+            quantise("g", 1, flat(g_late[q]), HALF + q * P, HALF + (q + 1) * P, E5M2)
         cast_xm(1, 0, P, HALF)
-        quantise_xm(1, 0, P, HALF)
+        quantise_xm_block(1, 1)
+        scatter(1, 0, 0, HALF)
         cast_xm(1, 1)
         quantise_xm(1, 1)
-        for c in range(D // P):
-            product(1, c, f"grad{(c + 3) % 4}", 0, N)
+        product(1, 0, "grad0", HALF, N)
+        scatter(1, 0, HALF, N)
+        for c in range(1, D // P):
+            product(1, c, ("grad1", "grad3", "grad2")[c - 1], 0, N)
             scatter(1, c, 0, N)

@@ -19,6 +19,7 @@ P = 128
 PACK = 4
 HALF = N // 2
 LIST_COLS = N // 16
+EARLY = 96
 
 
 def tile_attend_gsl2_w_kernel(tc, xT, wT, y, wt, xm, offs, out):
@@ -47,7 +48,7 @@ def tile_attend_gsl2_w_kernel(tc, xT, wT, y, wt, xm, offs, out):
 
         pairs = [tile([P, T], U32, f"pair{u}") for u in range(2)]
         chunks = [(0, 0, 1024), (0, 1024, 2048), (1, 0, 1024), (1, 1024, 1536), (1, 1536, 2048)]
-        w_raw = [tile([P, 2, hi - lo], F32, f"w_raw{u}_{lo}") for u, lo, hi in chunks]
+        w_raw = [tile_at([P, 2, hi - lo], F32, f"w_raw{u}_{lo}", 44 + 16 * u + lo // 128) for u, lo, hi in chunks]
         x0_raw = [tile([P, PACK, HALF], F32, "x0_raw0")[:], tile_at([P, PACK, HALF], F32, "x0_raw1", 0)]
         x1_raw = tile_at([P, PACK, R], F32, "x1_raw", 12)
         xm1_raw = tile([P, PACK, D], F32, "xm1_raw")
@@ -60,7 +61,7 @@ def tile_attend_gsl2_w_kernel(tc, xT, wT, y, wt, xm, offs, out):
         wt_sb = tile([P, B, PACK], F32, "wt_sb")
 
         for k, (u, lo, hi) in enumerate(chunks):
-            nc.sync.dma_start(out=w_raw[k][:], in_=rows(wT)[:, 2 * u : 2 * u + 2, lo:hi])
+            nc.sync.dma_start(out=w_raw[k], in_=rows(wT)[:, 2 * u : 2 * u + 2, lo:hi])
             if k == 0:
                 nc.sync.dma_start(offsets[:], offs)
         for h in range(2):
@@ -87,9 +88,10 @@ def tile_attend_gsl2_w_kernel(tc, xT, wT, y, wt, xm, offs, out):
                 scales[kind, b] = tile([P, 512], U8, f"{kind}_scales{b}")[:]
         xm_codes = {(0, 0): tile([P, HALF], U32, "xm_codes00")[:]}
 
-        windows = [tile([P, T], F32, f"window{c}") for c in range(D // P)]
+        windows = [tile([P, T], F32, f"window{c}") for c in range(3)]
         for c, window in enumerate(windows):
-            (nc.vector if c < 3 else nc.gpsimd).memset(window[:], 0.0)
+            (nc.vector if c < 2 else nc.gpsimd).memset(window[:], 0.0)
+        windows.append(reuse.tile([P, T], F32, name="window3", align_bytes=64, offset=52 * 1024))
         nc.gpsimd.memset(codes["g", 0][:, HALF:], 0)
         nc.gpsimd.memset(scales["g", 0][:, HALF:], 0)
         nc.gpsimd.memset(codes["g", 1][:, HALF:], 0)
@@ -107,7 +109,9 @@ def tile_attend_gsl2_w_kernel(tc, xT, wT, y, wt, xm, offs, out):
         sq[1, 1] = tile_at([P, PACK, HALF], F32, "sq11", 20)
         err = dict(y_sb)
         g_bf = {}
-        g_bf[1, 0] = tile_at([P, HALF, PACK], BF16, "g_bf10", 40)
+        g_both = tile([P, HALF + EARLY, PACK], BF16, "g_both")
+        g_bf[1, 0] = g_both[:, EARLY:, :]
+        g_bf[1, 1] = g_both[:, :HALF, :]
         xm1_first = tile_at([P, P], U32, "xm1_first", 34)
         g_bf[0, 0] = tile_at([P, HALF, PACK], BF16, "g_bf00", 30)
         codes["w", 0] = tile([P, N], U32, "w_codes0")[:]
@@ -118,7 +122,6 @@ def tile_attend_gsl2_w_kernel(tc, xT, wT, y, wt, xm, offs, out):
         xm_bf[0, 1] = tile([P, HALF, PACK], BF16, "xm_bf01")[:]
         err[1, 0] = tile_at([P, PACK, HALF], F32, "err10", 32)
         err[1, 1] = tile_at([P, PACK, HALF], F32, "err11", 36)
-        g_late = [tile([P, P, PACK], BF16, "g_late0")[:], tile_at([P, P, PACK], BF16, "g_late1", 41)]
         xm1_second = tile_at([P, P], U32, "xm1_second", 37)
         xm_codes[1, 1] = tile_at([P, HALF], U32, "xm_codes11", 38)
         dense = {(1, c, 0): tile([P, N], F32, f"dense1{c}")[:] for c in range(1, D // P)}
@@ -126,7 +129,7 @@ def tile_attend_gsl2_w_kernel(tc, xT, wT, y, wt, xm, offs, out):
         dense[1, 0, HALF] = tile([P, HALF], F32, "dense10b")[:]
         dense[0, 0, 0] = tile_at([P, HALF], F32, "dense00a", 16)
         dense[0, 1, 0] = tile_at([P, HALF], F32, "dense01a", 17)
-        xm_codes[0, 1] = tile_at([P, HALF], U32, "xm_codes01", 17)
+        xm0_late = [tile_at([P, P], U32, "xm0_third", 17), tile_at([P, P], U32, "xm0_fourth", 3)]
         dense[0, 2, 0] = tile_at([P, HALF], F32, "dense02a", 2)
         dense[0, 3, 0] = tile([P, HALF], F32, "dense03a")[:]
         for c in range(3):
@@ -229,6 +232,8 @@ def tile_attend_gsl2_w_kernel(tc, xT, wT, y, wt, xm, offs, out):
         def xm_block(b, c):
             if b == 1 and c < 2:
                 return (xm1_first, xm1_second)[c]
+            if b == 0 and c >= 2:
+                return xm0_late[c - 2]
             return xm_codes[b, c // 2][:, (c % 2) * P : (c % 2 + 1) * P]
 
         def quantise_xm_block(b, c):
@@ -257,9 +262,11 @@ def tile_attend_gsl2_w_kernel(tc, xT, wT, y, wt, xm, offs, out):
             if b == B - 1 and hi == N:
                 nc.sync.dma_start(out=out[c * P : (c + 1) * P, :], in_=windows[c][:])
 
-        cast_w(0, 0, 1024, nc.scalar.copy)
+        cast_w(0, 0, 768, nc.scalar.copy)
+        cast_w(0, 768, 1024, nc.vector.tensor_copy)
         cast_w(1, 0, 704, nc.vector.tensor_copy)
         cast_w(1, 704, 1024, nc.scalar.copy)
+        nc.gpsimd.memset(windows[3][:], 0.0)
         for b in range(B):
             gather(b, 0)
         cast_w(2, 0, 1024, nc.scalar.copy)
@@ -297,9 +304,11 @@ def tile_attend_gsl2_w_kernel(tc, xT, wT, y, wt, xm, offs, out):
         square(0, 1, 0, HALF)
         slope_act(0, 1, range(2))
         slope_alu(0, 1, 0, HALF, nc.gpsimd, range(2, 4))
-        cast_xm(0, 1)
-        quantise_xm(0, 1)
+        cast_xm(0, 1, 0, P)
+        quantise_xm_block(0, 2)
+        cast_xm(0, 1, P, HALF)
         gradient(0, 1, 0, HALF)
+        quantise_xm_block(0, 3)
         for q in range(2):
             scores(1, 0, q)
         square(1, 0, 0, HALF)
@@ -322,7 +331,7 @@ def tile_attend_gsl2_w_kernel(tc, xT, wT, y, wt, xm, offs, out):
         last_bank = product(0, 3, "grad2", 0, HALF)
         scatter(0, 3, 0, HALF)
         slope_act(1, 1, range(PACK), 0, P)
-        gradient_pool(1, 1, 0, P, g_late[0])
+        gradient_pool(1, 1, 0, EARLY, g_bf[1, 1][:, :EARLY, :])
         square(1, 1, P, HALF)
         slope_act(1, 1, range(PACK), P, HALF)
         cast_xm(1, 0, 0, P)
@@ -330,17 +339,18 @@ def tile_attend_gsl2_w_kernel(tc, xT, wT, y, wt, xm, offs, out):
         quantise_xm_block(1, 0)
         nc.scalar.copy(dense[0, 3, HALF], last_bank[:, HALF:])
         scatter(0, 3, HALF, N)
-        gradient_pool(1, 1, P, HALF, g_late[1])
+        gradient_pool(1, 1, EARLY, HALF, g_bf[1, 1][:, EARLY:, :])
         product(1, 0, "grad3", 0, HALF)
-        for q in range(2):
-            quantise("g", 1, flat(g_late[q]), HALF + q * P, HALF + (q + 1) * P, E5M2)
+        quantise_g(1, 1)
         cast_xm(1, 0, P, HALF)
         quantise_xm_block(1, 1)
         scatter(1, 0, 0, HALF)
         cast_xm(1, 1)
         quantise_xm(1, 1)
+        product(1, 1, "grad1", 0, N)
+        scatter(1, 1, 0, N)
         product(1, 0, "grad0", HALF, N)
         scatter(1, 0, HALF, N)
-        for c in range(1, D // P):
-            product(1, c, ("grad1", "grad3", "grad2")[c - 1], 0, N)
+        for c in range(2, D // P):
+            product(1, c, ("grad3", "grad2")[c - 2], 0, N)
             scatter(1, c, 0, N)

@@ -19,7 +19,7 @@ P = 128
 PACK = 4
 HALF = N // 2
 LIST_COLS = N // 16
-EARLY = 96
+EARLY = 80
 
 
 def tile_attend_gsl2_w_kernel(tc, xT, wT, y, wt, xm, offs, out):
@@ -223,9 +223,9 @@ def tile_attend_gsl2_w_kernel(tc, xT, wT, y, wt, xm, offs, out):
 
         def gradient_pool(b, h, lo, hi, dst):
             nc.gpsimd.tensor_tensor(
-                dst.rearrange("p (c i) j -> p c j i", i=2),
-                sq[b, h][:, :, lo:hi].rearrange("p j (c i) -> p c j i", i=2),
-                err[b, h][:, :, lo:hi].rearrange("p j (c i) -> p c j i", i=2),
+                dst.rearrange("p (c i) j -> p c j i", i=4),
+                sq[b, h][:, :, lo:hi].rearrange("p j (c i) -> p c j i", i=4),
+                err[b, h][:, :, lo:hi].rearrange("p j (c i) -> p c j i", i=4),
                 ALU.mult,
             )
 

@@ -19,7 +19,6 @@ P = 128
 PACK = 4
 HALF = N // 2
 LIST_COLS = N // 16
-EARLY = 80
 
 
 def tile_attend_gsl2_w_kernel(tc, xT, wT, y, wt, xm, offs, out):
@@ -44,25 +43,19 @@ def tile_attend_gsl2_w_kernel(tc, xT, wT, y, wt, xm, offs, out):
         def half(h):
             return slice(h * HALF, (h + 1) * HALF)
 
+        pieces = [(b, h) for b in range(B) for h in range(2)]
         offsets = keep.tile([P, B * LIST_COLS], U16, name="offsets")
-
-        pairs = [tile([P, T], U32, f"pair{u}") for u in range(2)]
-        chunks = [(0, 0, 1024), (0, 1024, 2048), (1, 0, 1024), (1, 1024, 1536), (1, 1536, 2048)]
-        w_raw = [tile_at([P, 2, hi - lo], F32, f"w_raw{u}_{lo}", 44 + 16 * u + lo // 128) for u, lo, hi in chunks]
-        x0_raw = [tile([P, PACK, HALF], F32, "x0_raw0")[:], tile_at([P, PACK, HALF], F32, "x0_raw1", 0)]
-        x1_raw = tile_at([P, PACK, R], F32, "x1_raw", 12)
-        xm1_raw = tile([P, PACK, D], F32, "xm1_raw")
-        y1_raw = tile([P, PACK, N], F32, "y1_raw")
-        xm_raw = {(0, h): tile([P, PACK, HALF], F32, f"xm0_raw{h}")[:] for h in range(2)}
-        y_sb = {(0, h): tile([P, PACK, HALF], F32, f"y0_raw{h}")[:] for h in range(2)}
-        for h in range(2):
-            xm_raw[1, h] = xm1_raw[:, :, half(h)]
-            y_sb[1, h] = y1_raw[:, :, half(h)]
+        planes = [tile([P, T], F32, f"plane{t}") for t in range(PACK)]
+        x0_raw = [tile_at([P, PACK, HALF], F32, "x0_raw0", 0), tile([P, PACK, HALF], F32, "x0_raw1")[:]]
+        x1_raw = tile([P, PACK, R], F32, "x1_raw")[:]
+        xm_raw = {bh: tile([P, PACK, HALF], F32, f"xm_raw{bh[0]}{bh[1]}")[:] for bh in pieces}
+        y_sb = {bh: tile([P, PACK, HALF], F32, f"y{bh[0]}{bh[1]}")[:] for bh in pieces[:3]}
+        y_sb[1, 1] = tile_at([P, PACK, HALF], F32, "y11", 4)
         wt_sb = tile([P, B, PACK], F32, "wt_sb")
 
-        for k, (u, lo, hi) in enumerate(chunks):
-            nc.sync.dma_start(out=w_raw[k], in_=rows(wT)[:, 2 * u : 2 * u + 2, lo:hi])
-            if k == 0:
+        for t in range(PACK):
+            nc.sync.dma_start(out=planes[t][:], in_=rows(wT)[:, t, :])
+            if t == 0:
                 nc.sync.dma_start(offsets[:], offs)
         for h in range(2):
             nc.sync.dma_start(out=x0_raw[h], in_=rows(xT[0])[:, :, half(h)])
@@ -71,84 +64,41 @@ def tile_attend_gsl2_w_kernel(tc, xT, wT, y, wt, xm, offs, out):
         nc.sync.dma_start(out=y_sb[0, 0], in_=rows(y[0])[:, :, half(0)])
         nc.sync.dma_start(out=x1_raw, in_=rows(xT[1]))
         nc.sync.dma_start(out=y_sb[0, 1], in_=rows(y[0])[:, :, half(1)])
+        nc.sync.dma_start(out=y_sb[1, 0], in_=rows(y[1])[:, :, half(0)])
+        nc.sync.dma_start(out=xm_raw[1, 0], in_=rows(xm[1])[:, :, half(0)])
+        nc.sync.dma_start(out=y_sb[1, 1], in_=rows(y[1])[:, :, half(1)])
         nc.sync.dma_start(out=xm_raw[0, 1], in_=rows(xm[0])[:, :, half(1)])
-        nc.sync.dma_start(out=y1_raw[:], in_=rows(y[1]))
-        nc.sync.dma_start(out=xm1_raw[:], in_=rows(xm[1]))
+        nc.sync.dma_start(out=xm_raw[1, 1], in_=rows(xm[1])[:, :, half(1)])
 
         zero = tile([P, 1], F32, "zero")
         centre = tile([P, 1], F32, "centre")
         nc.gpsimd.memset(zero[:], 0.0)
         nc.scalar.activation(centre[:], zero[:], ACT.Sigmoid)
 
+        windows = [tile([P, T], F32, f"window{c}") for c in range(D // P)]
+        for window in windows:
+            nc.gpsimd.memset(window[:], 0.0)
+
         codes, scales = {}, {}
         for b in range(B):
-            for kind in ("x", "g"):
-                codes[kind, b] = tile([P, 512], U32, f"{kind}_codes{b}")[:]
             for kind in ("w", "x", "xm", "g"):
+                codes[kind, b] = tile([P, 512], U32, f"{kind}_codes{b}")[:]
                 scales[kind, b] = tile([P, 512], U8, f"{kind}_scales{b}")[:]
-        xm_codes = {(0, 0): tile([P, HALF], U32, "xm_codes00")[:]}
 
-        windows = [tile([P, T], F32, f"window{c}") for c in range(3)]
-        for c, window in enumerate(windows):
-            (nc.vector if c < 2 else nc.gpsimd).memset(window[:], 0.0)
-        windows.append(reuse.tile([P, T], F32, name="window3", align_bytes=64, offset=52 * 1024))
-        nc.gpsimd.memset(codes["g", 0][:, HALF:], 0)
-        nc.gpsimd.memset(scales["g", 0][:, HALF:], 0)
-        nc.gpsimd.memset(codes["g", 1][:, HALF:], 0)
-        nc.gpsimd.memset(scales["g", 1][:, HALF:], 0)
+        picked = [tile([P, N, PACK], BF16, "picked0")[:], tile_at([P, N, PACK], BF16, "picked1", 0)]
+        plain = tile([P, PACK, N], BF16, "plain")
+        x_bf = [tile([P, R * PACK], BF16, f"x_bf{b}")[:] for b in range(B)]
+        xm_bf = {bh: tile([P, HALF, PACK], BF16, f"xm_bf{bh[0]}{bh[1]}")[:] for bh in pieces}
+        prob = {bh: tile([P, PACK, HALF], F32, f"prob{bh[0]}{bh[1]}")[:] for bh in pieces}
+        sq = {bh: tile([P, PACK, HALF], F32, f"sq{bh[0]}{bh[1]}")[:] for bh in pieces}
+        g_bf = {bh: tile([P, HALF, PACK], BF16, f"g_bf{bh[0]}{bh[1]}")[:] for bh in pieces}
+        early = {bh: tile([P, 2, HALF], F32, f"early{bh[0]}{bh[1]}")[:] for bh in pieces}
+        late30 = tile_at([P, N], F32, "late30", 4)
+        late31 = tile([P, N], F32, "late31")[:]
+        late2 = tile([P, B * N], F32, "late2")[:]
 
-        picked = {0: tile([P, N, 2], U32, "picked0")[:]}
-        planes = tile([P, 2, N], U32, "planes")
-        bias_sb = tile([P, B, PACK], F32, "bias_sb")
-        x_bf = [tile([P, R * PACK], BF16, "x_bf0")[:], tile_at([P, R * PACK], BF16, "x_bf1", 4)]
-        xm_bf = {(b, h): tile([P, HALF, PACK], BF16, f"xm_bf{b}{h}")[:] for b, h in ((0, 0), (1, 0), (1, 1))}
-        prob = {(b, h): tile([P, PACK, HALF], F32, f"prob{b}{h}")[:] for b, h in ((0, 0), (0, 1), (1, 0))}
-        prob[1, 1] = tile([P, PACK, HALF], F32, "prob11")[:]
-        sq = {(b, 0): tile([P, PACK, HALF], F32, f"sq{b}0")[:] for b in range(B)}
-        sq[0, 1] = tile_at([P, PACK, HALF], F32, "sq01", 12)
-        sq[1, 1] = tile_at([P, PACK, HALF], F32, "sq11", 20)
-        err = dict(y_sb)
-        g_bf = {}
-        g_both = tile([P, HALF + EARLY, PACK], BF16, "g_both")
-        g_bf[1, 0] = g_both[:, EARLY:, :]
-        g_bf[1, 1] = g_both[:, :HALF, :]
-        xm1_first = tile_at([P, P], U32, "xm1_first", 34)
-        g_bf[0, 0] = tile_at([P, HALF, PACK], BF16, "g_bf00", 30)
-        codes["w", 0] = tile([P, N], U32, "w_codes0")[:]
-        codes["w", 1] = tile_at([P, N], U32, "w_codes1", 30)
-        picked[1] = tile_at([P, N, 2], U32, "picked1", 0)
-        err[0, 1] = tile_at([P, PACK, HALF], F32, "err01", 2)
-        g_bf[0, 1] = tile_at([P, HALF, PACK], BF16, "g_bf01", 35)
-        xm_bf[0, 1] = tile([P, HALF, PACK], BF16, "xm_bf01")[:]
-        err[1, 0] = tile_at([P, PACK, HALF], F32, "err10", 32)
-        err[1, 1] = tile_at([P, PACK, HALF], F32, "err11", 36)
-        xm1_second = tile_at([P, P], U32, "xm1_second", 37)
-        xm_codes[1, 1] = tile_at([P, HALF], U32, "xm_codes11", 38)
-        dense = {(1, c, 0): tile([P, N], F32, f"dense1{c}")[:] for c in range(1, D // P)}
-        dense[1, 0, 0] = tile_at([P, HALF], F32, "dense10a", 36)
-        dense[1, 0, HALF] = tile([P, HALF], F32, "dense10b")[:]
-        dense[0, 0, 0] = tile_at([P, HALF], F32, "dense00a", 16)
-        dense[0, 1, 0] = tile_at([P, HALF], F32, "dense01a", 17)
-        xm0_late = [tile_at([P, P], U32, "xm0_third", 17), tile_at([P, P], U32, "xm0_fourth", 3)]
-        dense[0, 2, 0] = tile_at([P, HALF], F32, "dense02a", 2)
-        dense[0, 3, 0] = tile([P, HALF], F32, "dense03a")[:]
-        for c in range(3):
-            dense[0, c, HALF] = tile([P, HALF], F32, f"dense0{c}b")[:]
-        dense[0, 3, HALF] = tile_at([P, HALF], F32, "dense03b", 32)
-
-        def slots(b, lo, hi):
-            return offsets[:, (b * N + lo) // 16 : (b * N + hi) // 16]
-
-        def gather(b, u):
-            dst = picked[0][:, :, u] if b == 0 else planes[:, u, :]
-            nc.vector.tensor_copy(dst, pairs[u][:].indirect(slots(b, 0, N)))
-
-        def cast_w(k, lo, hi, copy):
-            u, first, last = chunks[k]
-            copy(
-                pairs[u][:, first + lo : first + hi].bitcast(BF16).rearrange("p (c i e) -> p c e i", i=4, e=2),
-                w_raw[k][:, :, lo:hi].rearrange("p e (c i) -> p c e i", i=4),
-            )
+        def slots(lo, hi):
+            return offsets[:, lo // 16 : hi // 16]
 
         def by_fours_src(ap):
             return ap.rearrange("p j (c i) -> p c j i", i=4)
@@ -165,18 +115,9 @@ def tile_attend_gsl2_w_kernel(tc, xT, wT, y, wt, xm, offs, out):
                 raw.rearrange("p j (m u e) -> p u m j e", u=2, e=2),
             )
 
-        def cast_xm(b, h, lo=0, hi=HALF):
-            nc.scalar.copy(by_fours_dst(xm_bf[b, h][:, lo:hi, :]), by_fours_src(xm_raw[b, h][:, :, lo:hi]))
-
-        def quantise_xm(b, h, lo=0, hi=HALF):
-            nc.vector.quantize_mx(
-                out=xm_codes[b, h][:, lo:hi].bitcast(E4M3),
-                scales=scales["xm", b][:, h * HALF + lo : h * HALF + hi],
-                in_=flat(xm_bf[b, h][:, lo:hi, :]),
-            )
-
-        def quantise_g(b, h):
-            quantise("g", b, flat(g_bf[b, h]), h * HALF, (h + 1) * HALF, E5M2)
+        def prepare_xm(b, h):
+            nc.vector.tensor_copy(by_fours_dst(xm_bf[b, h]), by_fours_src(xm_raw[b, h]))
+            quantise("xm", b, flat(xm_bf[b, h]), h * HALF, (h + 1) * HALF, E4M3)
 
         def scores(b, h, q):
             bank = psum.tile([P, PACK, P], F32, name=f"score{h}{q}")
@@ -196,161 +137,110 @@ def tile_attend_gsl2_w_kernel(tc, xT, wT, y, wt, xm, offs, out):
         def square(b, h, lo, hi):
             nc.scalar.activation(sq[b, h][:, :, lo:hi], prob[b, h][:, :, lo:hi], ACT.Square, bias=centre[:], scale=-1.0)
 
-        def error(b, h, lo, hi, engine):
-            engine.tensor_tensor(err[b, h][:, :, lo:hi], y_sb[b, h][:, :, lo:hi], prob[b, h][:, :, lo:hi], ALU.subtract)
+        def error(b, h, lo, hi):
+            nc.vector.tensor_tensor(y_sb[b, h][:, :, lo:hi], y_sb[b, h][:, :, lo:hi], prob[b, h][:, :, lo:hi], ALU.subtract)
 
-        def slope_alu(b, h, lo, hi, engine, places=range(PACK)):
-            for t in places:
-                engine.tensor_scalar(
-                    sq[b, h][:, t, lo:hi], sq[b, h][:, t, lo:hi], wt_sb[:, b, t : t + 1], bias_sb[:, b, t : t + 1],
-                    ALU.mult, ALU.add,
-                )
-
-        def slope_act(b, h, places=range(PACK), lo=0, hi=HALF):
-            for t in places:
-                nc.scalar.activation(
-                    sq[b, h][:, t, lo:hi], sq[b, h][:, t, lo:hi], ACT.Identity,
-                    bias=bias_sb[:, b, t : t + 1], scale=wt_sb[:, b, t : t + 1],
+        def slope(b, h, lo, hi):
+            for t in range(PACK):
+                nc.vector.tensor_scalar(
+                    sq[b, h][:, t, lo:hi], sq[b, h][:, t, lo:hi], 0.25, wt_sb[:, b, t : t + 1], ALU.subtract, ALU.mult
                 )
 
         def gradient(b, h, lo, hi):
             nc.vector.tensor_tensor(
                 by_fours_dst(g_bf[b, h][:, lo:hi, :]),
                 by_fours_src(sq[b, h][:, :, lo:hi]),
-                by_fours_src(err[b, h][:, :, lo:hi]),
+                by_fours_src(y_sb[b, h][:, :, lo:hi]),
                 ALU.mult,
             )
 
-        def gradient_pool(b, h, lo, hi, dst):
-            nc.gpsimd.tensor_tensor(
-                dst.rearrange("p (c i) j -> p c j i", i=4),
-                sq[b, h][:, :, lo:hi].rearrange("p j (c i) -> p c j i", i=4),
-                err[b, h][:, :, lo:hi].rearrange("p j (c i) -> p c j i", i=4),
-                ALU.mult,
-            )
+        def quantise_g(b, h):
+            quantise("g", b, flat(g_bf[b, h]), h * HALF, (h + 1) * HALF, E5M2)
 
-        def xm_block(b, c):
-            if b == 1 and c < 2:
-                return (xm1_first, xm1_second)[c]
-            if b == 0 and c >= 2:
-                return xm0_late[c - 2]
-            return xm_codes[b, c // 2][:, (c % 2) * P : (c % 2 + 1) * P]
-
-        def quantise_xm_block(b, c):
-            nc.vector.quantize_mx(
-                out=xm_block(b, c).bitcast(E4M3),
-                scales=scales["xm", b][:, c * P : (c + 1) * P],
-                in_=flat(xm_bf[b, c // 2][:, (c % 2) * P : (c % 2 + 1) * P, :]),
-            )
-
-        def product(b, c, bank_name, lo, hi):
-            bank = psum.tile([P, N], F32, name=bank_name)
+        def product(dst, b, c, lo, hi):
             nc.tensor.matmul_mx(
-                out=bank[:],
-                lhsT=xm_block(b, c).bitcast(E4M3),
+                out=dst,
+                lhsT=codes["xm", b][:, c * P : (c + 1) * P].bitcast(E4M3),
                 lhsT_scale=scales["xm", b][:, c * P : (c + 1) * P],
-                rhs=codes["g", b].bitcast(E5M2),
-                rhs_scale=scales["g", b],
+                rhs=codes["g", b][:, lo:hi].bitcast(E5M2),
+                rhs_scale=scales["g", b][:, lo:hi],
                 start=True,
                 stop=True,
             )
-            nc.scalar.copy(dense[b, c, lo], bank[:, lo:hi])
-            return bank
 
-        def scatter(b, c, lo, hi):
-            nc.vector.tensor_copy(windows[c][:].indirect(slots(b, lo, hi)), dense[b, c, lo])
-            if b == B - 1 and hi == N:
-                nc.sync.dma_start(out=out[c * P : (c + 1) * P, :], in_=windows[c][:])
+        def scatter_act(c, lo, hi, src):
+            nc.scalar.activation(windows[c][:].indirect(slots(lo, hi)), src, ACT.Copy)
 
-        cast_w(0, 0, 768, nc.scalar.copy)
-        cast_w(0, 768, 1024, nc.vector.tensor_copy)
-        cast_w(1, 0, 704, nc.vector.tensor_copy)
-        cast_w(1, 704, 1024, nc.scalar.copy)
-        nc.gpsimd.memset(windows[3][:], 0.0)
-        for b in range(B):
-            gather(b, 0)
-        cast_w(2, 0, 1024, nc.scalar.copy)
-        cast_w(3, 0, 512, nc.vector.tensor_copy)
-        cast_w(4, 0, 320, nc.vector.tensor_copy)
-        cast_w(4, 320, 512, nc.scalar.copy)
-        gather(0, 1)
-        quantise("w", 0, flat(picked[0]).bitcast(BF16), 0, N, E4M3)
-        gather(1, 1)
-        for h in range(2):
-            cast_x(0, x0_raw[h], 64 * h, 64 * (h + 1), nc.scalar.copy)
+        def scatter_vec(c, lo, hi, src):
+            nc.vector.tensor_copy(windows[c][:].indirect(slots(lo, hi)), src)
+
+        def store(c):
+            nc.sync.dma_start(out=out[c * P : (c + 1) * P, :], in_=windows[c][:])
+
+        def early_blocks(b, h):
+            bank = psum.tile([P, 2, HALF], F32, name=f"grad{h}")
+            for c in range(2):
+                product(bank[:, c, :], b, c, h * HALF, (h + 1) * HALF)
+            nc.scalar.copy(early[b, h], bank[:])
+            for c in range(2):
+                scatter_act(c, b * N + h * HALF, b * N + (h + 1) * HALF, early[b, h][:, c, :])
+                if (b, h) == pieces[-1]:
+                    store(c)
+
+        def late_block(b, c, name, dst, copy):
+            bank = psum.tile([P, N], F32, name=name)
+            product(bank[:], b, c, 0, N)
+            copy(dst, bank[:])
+
+        for t in range(PACK):
+            nc.vector.tensor_copy(picked[0][:, :, t], planes[t][:].indirect(slots(0, N)))
+            nc.scalar.activation(plain[:, t, :], planes[t][:].indirect(slots(N, 2 * N)), ACT.Copy)
+        quantise("w", 0, flat(picked[0]), 0, N, E4M3)
+        cast_x(0, x0_raw[0], 0, 64, nc.scalar.copy)
+        cast_x(0, x0_raw[1], 64, 128, nc.vector.tensor_copy)
         for u in range(2):
             quantise("x", 0, x_bf[0][:, u * 1024 : (u + 1) * 1024], u * 256, (u + 1) * 256, E4M3)
-        nc.scalar.copy(picked[1], planes[:].rearrange("p u i -> p i u"))
-        nc.gpsimd.tensor_scalar(bias_sb[:], wt_sb[:], -0.25, 0.0, ALU.mult, ALU.add)
-        nc.vector.tensor_copy(by_fours_dst(xm_bf[0, 0]), by_fours_src(xm_raw[0, 0]))
+        nc.scalar.copy(by_fours_dst(picked[1]), by_fours_src(plain[:]))
+        prepare_xm(0, 0)
         for q in range(2):
             scores(0, 0, q)
             square(0, 0, q * P, (q + 1) * P)
-            error(0, 0, q * P, (q + 1) * P, nc.vector)
-            slope_alu(0, 0, q * P, (q + 1) * P, nc.vector)
+            error(0, 0, q * P, (q + 1) * P)
+            slope(0, 0, q * P, (q + 1) * P)
             gradient(0, 0, q * P, (q + 1) * P)
-        quantise_xm(0, 0)
-        quantise_g(0, 0)
-        quantise("w", 1, flat(picked[1]).bitcast(BF16), 0, N, E4M3)
         for q in range(2):
             scores(0, 1, q)
-        cast_x(1, x1_raw[:, :, :384], 0, 96, nc.scalar.copy)
-        cast_x(1, x1_raw[:, :, 384:], 96, P, nc.vector.tensor_copy)
-        quantise("x", 1, x_bf[1], 0, R, E4M3)
-        for c in range(2):
-            product(0, c, f"grad{c}", 0, HALF)
-            scatter(0, c, 0, HALF)
-        error(0, 1, 0, HALF, nc.gpsimd)
         square(0, 1, 0, HALF)
-        slope_act(0, 1, range(2))
-        slope_alu(0, 1, 0, HALF, nc.gpsimd, range(2, 4))
-        cast_xm(0, 1, 0, P)
-        quantise_xm_block(0, 2)
-        cast_xm(0, 1, P, HALF)
+        quantise("w", 1, flat(picked[1]), 0, N, E4M3)
+        quantise_g(0, 0)
+        cast_x(1, x1_raw, 0, P, nc.vector.tensor_copy)
+        early_blocks(0, 0)
+        error(0, 1, 0, HALF)
+        quantise("x", 1, x_bf[1], 0, R, E4M3)
+        for h in range(2):
+            for q in range(2):
+                scores(1, h, q)
+            square(1, h, 0, HALF)
+        slope(0, 1, 0, HALF)
         gradient(0, 1, 0, HALF)
-        quantise_xm_block(0, 3)
-        for q in range(2):
-            scores(1, 0, q)
-        square(1, 0, 0, HALF)
-        product(0, 2, "grad2", 0, HALF)
         quantise_g(0, 1)
-        scatter(0, 2, 0, HALF)
-        error(1, 0, 0, HALF, nc.gpsimd)
-        scores(1, 1, 0)
-        product(0, 0, "grad3", HALF, N)
-        scatter(0, 0, HALF, N)
-        scores(1, 1, 1)
-        error(1, 1, 0, HALF, nc.gpsimd)
-        product(0, 1, "grad0", HALF, N)
-        scatter(0, 1, HALF, N)
-        slope_act(1, 0)
-        gradient_pool(1, 0, 0, HALF, g_bf[1, 0])
-        product(0, 2, "grad1", HALF, N)
-        scatter(0, 2, HALF, N)
-        square(1, 1, 0, P)
-        last_bank = product(0, 3, "grad2", 0, HALF)
-        scatter(0, 3, 0, HALF)
-        slope_act(1, 1, range(PACK), 0, P)
-        gradient_pool(1, 1, 0, EARLY, g_bf[1, 1][:, :EARLY, :])
-        square(1, 1, P, HALF)
-        slope_act(1, 1, range(PACK), P, HALF)
-        cast_xm(1, 0, 0, P)
-        quantise_g(1, 0)
-        quantise_xm_block(1, 0)
-        nc.scalar.copy(dense[0, 3, HALF], last_bank[:, HALF:])
-        scatter(0, 3, HALF, N)
-        gradient_pool(1, 1, EARLY, HALF, g_bf[1, 1][:, EARLY:, :])
-        product(1, 0, "grad3", 0, HALF)
-        quantise_g(1, 1)
-        cast_xm(1, 0, P, HALF)
-        quantise_xm_block(1, 1)
-        scatter(1, 0, 0, HALF)
-        cast_xm(1, 1)
-        quantise_xm(1, 1)
-        product(1, 1, "grad1", 0, N)
-        scatter(1, 1, 0, N)
-        product(1, 0, "grad0", HALF, N)
-        scatter(1, 0, HALF, N)
-        for c in range(2, D // P):
-            product(1, c, ("grad3", "grad2")[c - 2], 0, N)
-            scatter(1, c, 0, N)
+        early_blocks(0, 1)
+        prepare_xm(1, 0)
+        for h in range(2):
+            error(1, h, 0, HALF)
+            slope(1, h, 0, HALF)
+            gradient(1, h, 0, HALF)
+            quantise_g(1, h)
+            early_blocks(1, h)
+        prepare_xm(0, 1)
+        prepare_xm(1, 1)
+        late_block(0, 3, "grad2", late30, nc.vector.tensor_copy)
+        scatter_vec(3, 0, N, late30)
+        late_block(0, 2, "grad3", late2[:, :N], nc.vector.tensor_copy)
+        late_block(1, 2, "grad2", late2[:, N:], nc.vector.tensor_copy)
+        late_block(1, 3, "grad3", late31, nc.scalar.copy)
+        for h in range(2):
+            scatter_act(3, N + h * HALF, N + (h + 1) * HALF, late31[:, half(h)])
+        store(3)
+        scatter_vec(2, 0, 2 * N, late2)
+        store(2)

@@ -49,8 +49,7 @@ def tile_attend_gsl2_w_kernel(tc, xT, wT, y, wt, xm, offs, out):
         x0_raw = [tile_at([P, PACK, HALF], F32, "x0_raw0", 0), tile([P, PACK, HALF], F32, "x0_raw1")[:]]
         x1_raw = tile([P, PACK, R], F32, "x1_raw")[:]
         xm_raw = {bh: tile([P, PACK, HALF], F32, f"xm_raw{bh[0]}{bh[1]}")[:] for bh in pieces}
-        y_sb = {bh: tile([P, PACK, HALF], F32, f"y{bh[0]}{bh[1]}")[:] for bh in pieces[:3]}
-        y_sb[1, 1] = tile_at([P, PACK, HALF], F32, "y11", 4)
+        y_sb = {bh: tile([P, PACK, HALF], F32, f"y{bh[0]}{bh[1]}")[:] for bh in pieces}
         wt_sb = tile([P, B, PACK], F32, "wt_sb")
 
         for t in range(PACK):
@@ -65,9 +64,9 @@ def tile_attend_gsl2_w_kernel(tc, xT, wT, y, wt, xm, offs, out):
         nc.sync.dma_start(out=x1_raw, in_=rows(xT[1]))
         nc.sync.dma_start(out=y_sb[0, 1], in_=rows(y[0])[:, :, half(1)])
         nc.sync.dma_start(out=y_sb[1, 0], in_=rows(y[1])[:, :, half(0)])
-        nc.sync.dma_start(out=xm_raw[1, 0], in_=rows(xm[1])[:, :, half(0)])
-        nc.sync.dma_start(out=y_sb[1, 1], in_=rows(y[1])[:, :, half(1)])
         nc.sync.dma_start(out=xm_raw[0, 1], in_=rows(xm[0])[:, :, half(1)])
+        nc.sync.dma_start(out=y_sb[1, 1], in_=rows(y[1])[:, :, half(1)])
+        nc.sync.dma_start(out=xm_raw[1, 0], in_=rows(xm[1])[:, :, half(0)])
         nc.sync.dma_start(out=xm_raw[1, 1], in_=rows(xm[1])[:, :, half(1)])
 
         zero = tile([P, 1], F32, "zero")
@@ -85,17 +84,27 @@ def tile_attend_gsl2_w_kernel(tc, xT, wT, y, wt, xm, offs, out):
                 codes[kind, b] = tile([P, 512], U32, f"{kind}_codes{b}")[:]
                 scales[kind, b] = tile([P, 512], U8, f"{kind}_scales{b}")[:]
 
-        picked = [tile([P, N, PACK], BF16, "picked0")[:], tile_at([P, N, PACK], BF16, "picked1", 0)]
+        picked0 = tile([P, N, PACK], BF16, "picked0")[:]
+        picked1 = [tile_at([P, HALF, PACK], BF16, "picked10", 0), tile_at([P, HALF, PACK], BF16, "picked11", 16)]
         plain = tile([P, PACK, N], BF16, "plain")
-        x_bf = [tile([P, R * PACK], BF16, f"x_bf{b}")[:] for b in range(B)]
-        xm_bf = {bh: tile([P, HALF, PACK], BF16, f"xm_bf{bh[0]}{bh[1]}")[:] for bh in pieces}
-        prob = {bh: tile([P, PACK, HALF], F32, f"prob{bh[0]}{bh[1]}")[:] for bh in pieces}
+        x_bf = [tile([P, R * PACK], BF16, "x_bf0")[:], tile_at([P, R * PACK], BF16, "x_bf1", 8)]
+        xm_bf = {bh: tile([P, HALF, PACK], BF16, f"xm_bf{bh[0]}{bh[1]}")[:] for bh in pieces if bh != (0, 1)}
+        xm_bf[0, 1] = tile_at([P, HALF, PACK], BF16, "xm_bf01", 12)
+        prob = {bh: tile([P, PACK, HALF], F32, f"prob{bh[0]}{bh[1]}")[:] for bh in pieces[1:]}
+        prob[0, 0] = tile_at([P, PACK, HALF], F32, "prob00", 16)
         sq = {bh: tile([P, PACK, HALF], F32, f"sq{bh[0]}{bh[1]}")[:] for bh in pieces}
-        g_bf = {bh: tile([P, HALF, PACK], BF16, f"g_bf{bh[0]}{bh[1]}")[:] for bh in pieces}
-        early = {bh: tile([P, 2, HALF], F32, f"early{bh[0]}{bh[1]}")[:] for bh in pieces}
-        late30 = tile_at([P, N], F32, "late30", 4)
+        g_bf = {bh: tile([P, HALF, PACK], BF16, f"g_bf{bh[0]}{bh[1]}")[:] for bh in pieces[2:]}
+        g_bf[0, 1] = tile_at([P, HALF, PACK], BF16, "g_bf01", 14)
+        err = dict(y_sb)
+        err[1, 0] = tile_at([P, PACK, HALF], F32, "err10", 12)
+        g_bf[0, 0] = tile_at([P, HALF, PACK], BF16, "g_bf00", 8)
+        early = {bh: tile([P, HALF], F32, f"early{bh[0]}{bh[1]}")[:] for bh in pieces}
+        late30 = tile([P, N], F32, "late30")[:]
+        late20 = tile([P, HALF], F32, "late20")[:]
+        late10 = tile([P, N], F32, "late10")[:]
+        late11 = tile([P, N], F32, "late11")[:]
         late31 = tile([P, N], F32, "late31")[:]
-        late2 = tile([P, B * N], F32, "late2")[:]
+        late2 = tile([P, HALF + N], F32, "late2")[:]
 
         def slots(lo, hi):
             return offsets[:, lo // 16 : hi // 16]
@@ -137,8 +146,8 @@ def tile_attend_gsl2_w_kernel(tc, xT, wT, y, wt, xm, offs, out):
         def square(b, h, lo, hi):
             nc.scalar.activation(sq[b, h][:, :, lo:hi], prob[b, h][:, :, lo:hi], ACT.Square, bias=centre[:], scale=-1.0)
 
-        def error(b, h, lo, hi):
-            nc.vector.tensor_tensor(y_sb[b, h][:, :, lo:hi], y_sb[b, h][:, :, lo:hi], prob[b, h][:, :, lo:hi], ALU.subtract)
+        def error(b, h, lo, hi, engine=nc.vector):
+            engine.tensor_tensor(err[b, h][:, :, lo:hi], y_sb[b, h][:, :, lo:hi], prob[b, h][:, :, lo:hi], ALU.subtract)
 
         def slope(b, h, lo, hi):
             for t in range(PACK):
@@ -150,7 +159,7 @@ def tile_attend_gsl2_w_kernel(tc, xT, wT, y, wt, xm, offs, out):
             nc.vector.tensor_tensor(
                 by_fours_dst(g_bf[b, h][:, lo:hi, :]),
                 by_fours_src(sq[b, h][:, :, lo:hi]),
-                by_fours_src(y_sb[b, h][:, :, lo:hi]),
+                by_fours_src(err[b, h][:, :, lo:hi]),
                 ALU.mult,
             )
 
@@ -178,14 +187,10 @@ def tile_attend_gsl2_w_kernel(tc, xT, wT, y, wt, xm, offs, out):
             nc.sync.dma_start(out=out[c * P : (c + 1) * P, :], in_=windows[c][:])
 
         def early_blocks(b, h):
-            bank = psum.tile([P, 2, HALF], F32, name=f"grad{h}")
-            for c in range(2):
-                product(bank[:, c, :], b, c, h * HALF, (h + 1) * HALF)
+            bank = psum.tile([P, HALF], F32, name=f"grad{h}")
+            product(bank[:], b, 0, h * HALF, (h + 1) * HALF)
             nc.scalar.copy(early[b, h], bank[:])
-            for c in range(2):
-                scatter_act(c, b * N + h * HALF, b * N + (h + 1) * HALF, early[b, h][:, c, :])
-                if (b, h) == pieces[-1]:
-                    store(c)
+            scatter_act(0, b * N + h * HALF, b * N + (h + 1) * HALF, early[b, h])
 
         def late_block(b, c, name, dst, copy):
             bank = psum.tile([P, N], F32, name=name)
@@ -193,14 +198,14 @@ def tile_attend_gsl2_w_kernel(tc, xT, wT, y, wt, xm, offs, out):
             copy(dst, bank[:])
 
         for t in range(PACK):
-            nc.vector.tensor_copy(picked[0][:, :, t], planes[t][:].indirect(slots(0, N)))
+            nc.vector.tensor_copy(picked0[:, :, t], planes[t][:].indirect(slots(0, N)))
             nc.scalar.activation(plain[:, t, :], planes[t][:].indirect(slots(N, 2 * N)), ACT.Copy)
-        quantise("w", 0, flat(picked[0]), 0, N, E4M3)
+        quantise("w", 0, flat(picked0), 0, N, E4M3)
         cast_x(0, x0_raw[0], 0, 64, nc.scalar.copy)
         cast_x(0, x0_raw[1], 64, 128, nc.vector.tensor_copy)
         for u in range(2):
             quantise("x", 0, x_bf[0][:, u * 1024 : (u + 1) * 1024], u * 256, (u + 1) * 256, E4M3)
-        nc.scalar.copy(by_fours_dst(picked[1]), by_fours_src(plain[:]))
+        nc.scalar.copy(by_fours_dst(picked1[0]), by_fours_src(plain[:, :, half(0)]))
         prepare_xm(0, 0)
         for q in range(2):
             scores(0, 0, q)
@@ -211,9 +216,12 @@ def tile_attend_gsl2_w_kernel(tc, xT, wT, y, wt, xm, offs, out):
         for q in range(2):
             scores(0, 1, q)
         square(0, 1, 0, HALF)
-        quantise("w", 1, flat(picked[1]), 0, N, E4M3)
+        nc.scalar.copy(by_fours_dst(picked1[1]), by_fours_src(plain[:, :, half(1)]))
         quantise_g(0, 0)
-        cast_x(1, x1_raw, 0, P, nc.vector.tensor_copy)
+        for h in range(2):
+            quantise("w", 1, flat(picked1[h]), h * HALF, (h + 1) * HALF, E4M3)
+        for h in range(2):
+            cast_x(1, x1_raw[:, :, half(h)], 64 * h, 64 * (h + 1), nc.vector.tensor_copy)
         early_blocks(0, 0)
         error(0, 1, 0, HALF)
         quantise("x", 1, x_bf[1], 0, R, E4M3)
@@ -225,22 +233,35 @@ def tile_attend_gsl2_w_kernel(tc, xT, wT, y, wt, xm, offs, out):
         gradient(0, 1, 0, HALF)
         quantise_g(0, 1)
         early_blocks(0, 1)
-        prepare_xm(1, 0)
+        prepare_xm(0, 1)
+        late_block(0, 1, "grad2", late10, nc.vector.tensor_copy)
+        scatter_vec(1, 0, N, late10)
+        late_block(0, 3, "grad3", late30, nc.scalar.copy)
         for h in range(2):
-            error(1, h, 0, HALF)
+            scatter_act(3, h * HALF, (h + 1) * HALF, late30[:, half(h)])
+        bank20 = psum.tile([P, N], F32, name="score00")
+        product(bank20[:], 0, 2, 0, N)
+        nc.scalar.copy(late20, bank20[:, half(0)])
+        scatter_act(2, 0, HALF, late20)
+        error(1, 0, 0, HALF, nc.gpsimd)
+        error(1, 1, 0, 192, nc.gpsimd)
+        prepare_xm(1, 0)
+        error(1, 1, 192, HALF)
+        nc.vector.tensor_copy(late2[:, :HALF], bank20[:, half(1)])
+        for h in range(2):
             slope(1, h, 0, HALF)
             gradient(1, h, 0, HALF)
             quantise_g(1, h)
             early_blocks(1, h)
-        prepare_xm(0, 1)
+        store(0)
         prepare_xm(1, 1)
-        late_block(0, 3, "grad2", late30, nc.vector.tensor_copy)
-        scatter_vec(3, 0, N, late30)
-        late_block(0, 2, "grad3", late2[:, :N], nc.vector.tensor_copy)
-        late_block(1, 2, "grad2", late2[:, N:], nc.vector.tensor_copy)
+        late_block(1, 1, "grad2", late11, nc.vector.tensor_copy)
+        scatter_vec(1, N, 2 * N, late11)
+        store(1)
         late_block(1, 3, "grad3", late31, nc.scalar.copy)
         for h in range(2):
             scatter_act(3, N + h * HALF, N + (h + 1) * HALF, late31[:, half(h)])
         store(3)
-        scatter_vec(2, 0, 2 * N, late2)
+        late_block(1, 2, "score01", late2[:, HALF:], nc.vector.tensor_copy)
+        scatter_vec(2, HALF, 2 * N, late2)
         store(2)

@@ -85,26 +85,23 @@ def tile_attend_gsl2_w_kernel(tc, xT, wT, y, wt, xm, offs, out):
                 scales[kind, b] = tile([P, 512], U8, f"{kind}_scales{b}")[:]
 
         picked0 = tile([P, N, PACK], BF16, "picked0")[:]
-        picked1 = [tile_at([P, HALF, PACK], BF16, "picked10", 0), tile_at([P, HALF, PACK], BF16, "picked11", 16)]
+        picked1 = [tile_at([P, HALF, PACK], BF16, "picked10", 0), tile_at([P, HALF, PACK], BF16, "picked11", 20)]
         plain = tile([P, PACK, N], BF16, "plain")
         x_bf = [tile([P, R * PACK], BF16, "x_bf0")[:], tile_at([P, R * PACK], BF16, "x_bf1", 8)]
-        xm_bf = {bh: tile([P, HALF, PACK], BF16, f"xm_bf{bh[0]}{bh[1]}")[:] for bh in pieces if bh != (0, 1)}
-        xm_bf[0, 1] = tile_at([P, HALF, PACK], BF16, "xm_bf01", 12)
+        xm_bf = {bh: tile([P, HALF, PACK], BF16, f"xm_bf{bh[0]}{bh[1]}")[:] for bh in pieces}
         prob = {bh: tile([P, PACK, HALF], F32, f"prob{bh[0]}{bh[1]}")[:] for bh in pieces[1:]}
-        prob[0, 0] = tile_at([P, PACK, HALF], F32, "prob00", 16)
+        prob[0, 0] = tile_at([P, PACK, HALF], F32, "prob00", 20)
         sq = {bh: tile([P, PACK, HALF], F32, f"sq{bh[0]}{bh[1]}")[:] for bh in pieces}
-        g_bf = {bh: tile([P, HALF, PACK], BF16, f"g_bf{bh[0]}{bh[1]}")[:] for bh in pieces[2:]}
-        g_bf[0, 1] = tile_at([P, HALF, PACK], BF16, "g_bf01", 14)
+        g_bf = {bh: tile([P, HALF, PACK], BF16, f"g_bf{bh[0]}{bh[1]}")[:] for bh in pieces[1:3]}
+        g_bf[1, 1] = tile_at([P, HALF, PACK], BF16, "g_bf11", 14)
         err = dict(y_sb)
-        err[1, 0] = tile_at([P, PACK, HALF], F32, "err10", 12)
         g_bf[0, 0] = tile_at([P, HALF, PACK], BF16, "g_bf00", 8)
         early = {bh: tile([P, HALF], F32, f"early{bh[0]}{bh[1]}")[:] for bh in pieces}
-        late30 = tile([P, N], F32, "late30")[:]
-        late20 = tile([P, HALF], F32, "late20")[:]
+        late30 = tile_at([P, N + P], F32, "late30", 12)
         late10 = tile([P, N], F32, "late10")[:]
         late11 = tile([P, N], F32, "late11")[:]
-        late31 = tile([P, N], F32, "late31")[:]
-        late2 = tile([P, HALF + N], F32, "late2")[:]
+        late31 = tile([P, N - P], F32, "late31")[:]
+        late2 = tile_at([P, B * N], F32, "late2", 15)
 
         def slots(lo, hi):
             return offsets[:, lo // 16 : hi // 16]
@@ -233,35 +230,31 @@ def tile_attend_gsl2_w_kernel(tc, xT, wT, y, wt, xm, offs, out):
         gradient(0, 1, 0, HALF)
         quantise_g(0, 1)
         early_blocks(0, 1)
-        prepare_xm(0, 1)
-        late_block(0, 1, "grad2", late10, nc.vector.tensor_copy)
-        scatter_vec(1, 0, N, late10)
-        late_block(0, 3, "grad3", late30, nc.scalar.copy)
+        late_block(0, 1, "grad2", late10, nc.scalar.copy)
         for h in range(2):
-            scatter_act(3, h * HALF, (h + 1) * HALF, late30[:, half(h)])
-        bank20 = psum.tile([P, N], F32, name="score00")
-        product(bank20[:], 0, 2, 0, N)
-        nc.scalar.copy(late20, bank20[:, half(0)])
-        scatter_act(2, 0, HALF, late20)
-        error(1, 0, 0, HALF, nc.gpsimd)
-        error(1, 1, 0, 192, nc.gpsimd)
+            scatter_act(1, h * HALF, (h + 1) * HALF, late10[:, half(h)])
         prepare_xm(1, 0)
-        error(1, 1, 192, HALF)
-        nc.vector.tensor_copy(late2[:, :HALF], bank20[:, half(1)])
         for h in range(2):
+            error(1, h, 0, HALF)
             slope(1, h, 0, HALF)
             gradient(1, h, 0, HALF)
             quantise_g(1, h)
             early_blocks(1, h)
+            prepare_xm(h, 1)
         store(0)
-        prepare_xm(1, 1)
-        late_block(1, 1, "grad2", late11, nc.vector.tensor_copy)
-        scatter_vec(1, N, 2 * N, late11)
-        store(1)
-        late_block(1, 3, "grad3", late31, nc.scalar.copy)
+        late_block(1, 1, "grad2", late11, nc.scalar.copy)
         for h in range(2):
-            scatter_act(3, N + h * HALF, N + (h + 1) * HALF, late31[:, half(h)])
+            scatter_act(1, N + h * HALF, N + (h + 1) * HALF, late11[:, half(h)])
+        store(1)
+        late_block(0, 3, "grad3", late30[:, :N], nc.vector.tensor_copy)
+        bank31 = psum.tile([P, N], F32, name="score00")
+        product(bank31[:], 1, 3, 0, N)
+        nc.vector.tensor_copy(late30[:, N:], bank31[:, :P])
+        late_block(0, 2, "score01", late2[:, :N], nc.vector.tensor_copy)
+        scatter_vec(3, 0, N + P, late30)
+        late_block(1, 2, "score10", late2[:, N:], nc.vector.tensor_copy)
+        nc.scalar.copy(late31, bank31[:, P:])
+        scatter_act(3, N + P, 2 * N, late31)
         store(3)
-        late_block(1, 2, "score01", late2[:, HALF:], nc.vector.tensor_copy)
-        scatter_vec(2, HALF, 2 * N, late2)
+        scatter_vec(2, 0, 2 * N, late2)
         store(2)

@@ -46,7 +46,7 @@ def tile_attend_gsl2_w_kernel(tc, xT, wT, y, wt, xm, offs, out):
         pieces = [(b, h) for b in range(B) for h in range(2)]
         offsets = keep.tile([P, B * LIST_COLS], U16, name="offsets")
         planes = [tile([P, T], F32, f"plane{t}") for t in range(PACK)]
-        x0_raw = [tile_at([P, PACK, HALF], F32, "x0_raw0", 0), tile([P, PACK, HALF], F32, "x0_raw1")[:]]
+        x0_raw = [tile_at([P, PACK, HALF], F32, "x0_raw0", 0), tile_at([P, PACK, HALF], F32, "x0_raw1", 4)]
         x1_raw = tile([P, PACK, R], F32, "x1_raw")[:]
         xm_raw = {bh: tile([P, PACK, HALF], F32, f"xm_raw{bh[0]}{bh[1]}")[:] for bh in pieces}
         y_sb = {bh: tile([P, PACK, HALF], F32, f"y{bh[0]}{bh[1]}")[:] for bh in pieces}
@@ -58,9 +58,9 @@ def tile_attend_gsl2_w_kernel(tc, xT, wT, y, wt, xm, offs, out):
                 nc.sync.dma_start(offsets[:], offs)
         for h in range(2):
             nc.sync.dma_start(out=x0_raw[h], in_=rows(xT[0])[:, :, half(h)])
-        nc.sync.dma_start(out=wt_sb[:], in_=wt.rearrange("b (p t) o -> p b (t o)", t=PACK))
         nc.sync.dma_start(out=xm_raw[0, 0], in_=rows(xm[0])[:, :, half(0)])
         nc.sync.dma_start(out=y_sb[0, 0], in_=rows(y[0])[:, :, half(0)])
+        nc.sync.dma_start(out=wt_sb[:], in_=wt.rearrange("b (p t) o -> p b (t o)", t=PACK))
         nc.sync.dma_start(out=x1_raw, in_=rows(xT[1]))
         nc.sync.dma_start(out=y_sb[0, 1], in_=rows(y[0])[:, :, half(1)])
         nc.sync.dma_start(out=y_sb[1, 0], in_=rows(y[1])[:, :, half(0)])
@@ -81,10 +81,12 @@ def tile_attend_gsl2_w_kernel(tc, xT, wT, y, wt, xm, offs, out):
         codes, scales = {}, {}
         for b in range(B):
             for kind in ("w", "x", "xm", "g"):
-                codes[kind, b] = tile([P, 512], U32, f"{kind}_codes{b}")[:]
+                if (kind, b) != ("w", 0):
+                    codes[kind, b] = tile([P, 512], U32, f"{kind}_codes{b}")[:]
                 scales[kind, b] = tile([P, 512], U8, f"{kind}_scales{b}")[:]
 
-        picked0 = tile([P, N, PACK], BF16, "picked0")[:]
+        picked0 = [tile([P, HALF, PACK], BF16, f"picked0{h}")[:] for h in range(2)]
+        w0_codes = [tile([P, HALF], U32, "w0_codes0")[:], tile_at([P, HALF], U32, "w0_codes1", 4)]
         picked1 = [tile_at([P, HALF, PACK], BF16, "picked10", 0), tile_at([P, HALF, PACK], BF16, "picked11", 20)]
         plain = tile([P, PACK, N], BF16, "plain")
         x_bf = [tile([P, R * PACK], BF16, "x_bf0")[:], tile_at([P, R * PACK], BF16, "x_bf1", 8)]
@@ -133,7 +135,7 @@ def tile_attend_gsl2_w_kernel(tc, xT, wT, y, wt, xm, offs, out):
                     out=bank[:, t, :],
                     lhsT=codes["x", b][:, t * P : (t + 1) * P].bitcast(E4M3),
                     lhsT_scale=scales["x", b][:, t * P : (t + 1) * P],
-                    rhs=codes["w", b][:, cols].bitcast(E4M3),
+                    rhs=(w0_codes[h][:, q * P : (q + 1) * P] if b == 0 else codes["w", b][:, cols]).bitcast(E4M3),
                     rhs_scale=scales["w", b][:, cols],
                     start=True,
                     stop=True,
@@ -195,14 +197,16 @@ def tile_attend_gsl2_w_kernel(tc, xT, wT, y, wt, xm, offs, out):
             copy(dst, bank[:])
 
         for t in range(PACK):
-            nc.vector.tensor_copy(picked0[:, :, t], planes[t][:].indirect(slots(0, N)))
+            for h in range(2):
+                nc.vector.tensor_copy(picked0[h][:, :, t], planes[t][:].indirect(slots(h * HALF, (h + 1) * HALF)))
             nc.scalar.activation(plain[:, t, :], planes[t][:].indirect(slots(N, 2 * N)), ACT.Copy)
-        quantise("w", 0, flat(picked0), 0, N, E4M3)
+        nc.vector.quantize_mx(out=w0_codes[0].bitcast(E4M3), scales=scales["w", 0][:, half(0)], in_=flat(picked0[0]))
         cast_x(0, x0_raw[0], 0, 64, nc.scalar.copy)
         cast_x(0, x0_raw[1], 64, 128, nc.vector.tensor_copy)
         for u in range(2):
             quantise("x", 0, x_bf[0][:, u * 1024 : (u + 1) * 1024], u * 256, (u + 1) * 256, E4M3)
         nc.scalar.copy(by_fours_dst(picked1[0]), by_fours_src(plain[:, :, half(0)]))
+        nc.vector.quantize_mx(out=w0_codes[1].bitcast(E4M3), scales=scales["w", 0][:, half(1)], in_=flat(picked0[1]))
         prepare_xm(0, 0)
         for q in range(2):
             scores(0, 0, q)

@@ -43,31 +43,31 @@ def tile_attend_gsl2_w_kernel(tc, xT, wT, y, wt, xm, offs, out):
         def half(h):
             return slice(h * HALF, (h + 1) * HALF)
 
-        pieces = [(b, h) for b in range(B) for h in range(2)]
+        A, Bp, C, Dp = pieces = [(b, h) for b in range(B) for h in range(2)]
         offsets = keep.tile([P, B * LIST_COLS], U16, name="offsets")
         planes = [tile([P, T], F32, f"plane{t}") for t in range(PACK)]
-        x0_raw = [tile_at([P, PACK, HALF], F32, "x0_raw0", 0), tile_at([P, PACK, HALF], F32, "x0_raw1", 4)]
-        x1_raw = tile([P, PACK, R], F32, "x1_raw")[:]
-        xm_raw = {bh: tile([P, PACK, HALF], F32, f"xm_raw{bh[0]}{bh[1]}")[:] for bh in pieces}
-        y_sb = {bh: tile([P, PACK, HALF], F32, f"y{bh[0]}{bh[1]}")[:] for bh in pieces}
+        x_raw = [tile_at([P, PACK, R], F32, "x_raw0", 36), tile([P, PACK, R], F32, "x_raw1")[:]]
+        xm0_raw = [tile([P, PACK, HALF], F32, f"xm0_raw{h}")[:] for h in range(2)]
+        xm1_raw = tile([P, PACK, D], F32, "xm1_raw")[:]
+        y0_sb = [tile([P, PACK, HALF], F32, f"y0{h}")[:] for h in range(2)]
+        y1_sb = tile([P, PACK, N], F32, "y1")[:]
+        xm_raw = {A: xm0_raw[0], Bp: xm0_raw[1], C: xm1_raw[:, :, half(0)]}
+        y_sb = {A: y0_sb[0], Bp: y0_sb[1], C: y1_sb[:, :, half(0)], Dp: y1_sb[:, :, half(1)]}
         wt_sb = tile([P, B, PACK], F32, "wt_sb")
 
         for t in range(PACK):
             nc.sync.dma_start(out=planes[t][:], in_=rows(wT)[:, t, :])
             if t == 0:
                 nc.sync.dma_start(offsets[:], offs)
-        for h in range(2):
-            nc.sync.dma_start(out=x0_raw[h], in_=rows(xT[0])[:, :, half(h)])
-        nc.sync.dma_start(out=xm_raw[0, 0], in_=rows(xm[0])[:, :, half(0)])
-        nc.sync.dma_start(out=y_sb[0, 0], in_=rows(y[0])[:, :, half(0)])
+        nc.sync.dma_start(out=x_raw[0], in_=rows(xT[0]))
+        nc.sync.dma_start(out=xm0_raw[0], in_=rows(xm[0])[:, :, half(0)])
+        nc.sync.dma_start(out=y0_sb[0], in_=rows(y[0])[:, :, half(0)])
         nc.sync.dma_start(out=wt_sb[:], in_=wt.rearrange("b (p t) o -> p b (t o)", t=PACK))
-        nc.sync.dma_start(out=x1_raw, in_=rows(xT[1]))
-        nc.sync.dma_start(out=y_sb[0, 1], in_=rows(y[0])[:, :, half(1)])
-        nc.sync.dma_start(out=y_sb[1, 0], in_=rows(y[1])[:, :, half(0)])
-        nc.sync.dma_start(out=xm_raw[0, 1], in_=rows(xm[0])[:, :, half(1)])
-        nc.sync.dma_start(out=y_sb[1, 1], in_=rows(y[1])[:, :, half(1)])
-        nc.sync.dma_start(out=xm_raw[1, 0], in_=rows(xm[1])[:, :, half(0)])
-        nc.sync.dma_start(out=xm_raw[1, 1], in_=rows(xm[1])[:, :, half(1)])
+        nc.sync.dma_start(out=x_raw[1], in_=rows(xT[1]))
+        nc.sync.dma_start(out=y0_sb[1], in_=rows(y[0])[:, :, half(1)])
+        nc.sync.dma_start(out=xm0_raw[1], in_=rows(xm[0])[:, :, half(1)])
+        nc.sync.dma_start(out=xm1_raw, in_=rows(xm[1]))
+        nc.sync.dma_start(out=y1_sb, in_=rows(y[1]))
 
         zero = tile([P, 1], F32, "zero")
         centre = tile([P, 1], F32, "centre")
@@ -81,29 +81,35 @@ def tile_attend_gsl2_w_kernel(tc, xT, wT, y, wt, xm, offs, out):
         codes, scales = {}, {}
         for b in range(B):
             for kind in ("w", "x", "xm", "g"):
-                if (kind, b) != ("w", 0):
+                if (kind, b) == ("w", 1):
+                    codes[kind, b] = tile_at([P, 512], U32, "w_codes1", 40)
+                else:
                     codes[kind, b] = tile([P, 512], U32, f"{kind}_codes{b}")[:]
                 scales[kind, b] = tile([P, 512], U8, f"{kind}_scales{b}")[:]
 
         picked0 = [tile([P, HALF, PACK], BF16, f"picked0{h}")[:] for h in range(2)]
-        w0_codes = [tile([P, HALF], U32, "w0_codes0")[:], tile_at([P, HALF], U32, "w0_codes1", 4)]
-        picked1 = [tile_at([P, HALF, PACK], BF16, "picked10", 0), tile_at([P, HALF, PACK], BF16, "picked11", 20)]
+        picked1 = [tile([P, HALF, PACK], BF16, "picked10")[:], tile_at([P, HALF, PACK], BF16, "picked11", 36)]
         plain = tile([P, PACK, N], BF16, "plain")
-        x_bf = [tile([P, R * PACK], BF16, "x_bf0")[:], tile_at([P, R * PACK], BF16, "x_bf1", 8)]
-        xm_bf = {bh: tile([P, HALF, PACK], BF16, f"xm_bf{bh[0]}{bh[1]}")[:] for bh in pieces}
-        prob = {bh: tile([P, PACK, HALF], F32, f"prob{bh[0]}{bh[1]}")[:] for bh in pieces[1:]}
-        prob[0, 0] = tile_at([P, PACK, HALF], F32, "prob00", 20)
-        sq = {bh: tile([P, PACK, HALF], F32, f"sq{bh[0]}{bh[1]}")[:] for bh in pieces}
-        g_bf = {bh: tile([P, HALF, PACK], BF16, f"g_bf{bh[0]}{bh[1]}")[:] for bh in pieces[1:3]}
-        g_bf[1, 1] = tile_at([P, HALF, PACK], BF16, "g_bf11", 14)
-        err = dict(y_sb)
-        g_bf[0, 0] = tile_at([P, HALF, PACK], BF16, "g_bf00", 8)
-        early = {bh: tile([P, HALF], F32, f"early{bh[0]}{bh[1]}")[:] for bh in pieces}
-        late30 = tile_at([P, N + P], F32, "late30", 12)
-        late10 = tile([P, N], F32, "late10")[:]
-        late11 = tile([P, N], F32, "late11")[:]
-        late31 = tile([P, N - P], F32, "late31")[:]
-        late2 = tile_at([P, B * N], F32, "late2", 15)
+        x0_bf = [tile([P, 2 * P * PACK], BF16, "x0_bf0")[:], tile_at([P, 2 * P * PACK], BF16, "x0_bf1", 44)]
+        x1_bf = tile_at([P, R * PACK], BF16, "x1_bf", 0)
+        big = [P, PACK, HALF]
+        packed = [P, HALF, PACK]
+        prob = {bh: tile(big, F32, f"prob{bh[0]}{bh[1]}")[:] for bh in pieces}
+        sq = {A: tile_at(big, F32, "sqA", 0), Bp: tile_at(big, F32, "sqB", 4), C: tile_at(big, F32, "sqC", 28), Dp: tile(big, F32, "sqD")[:]}
+        slope = {A: tile(big, F32, "slopeA")[:], Bp: tile(big, F32, "slopeB")[:], C: tile_at(big, F32, "slopeC", 18.5), Dp: tile_at(big, F32, "slopeD", 28)}
+        err = {A: y_sb[A], Bp: tile_at(big, F32, "errB", 8), C: tile_at(big, F32, "errC", 14.5), Dp: tile_at(big, F32, "errD", 22.5)}
+        g_bf = {A: tile_at(packed, BF16, "g_bfA", 8), Bp: tile_at(packed, BF16, "g_bfB", 13), C: tile(packed, BF16, "g_bfC")[:], Dp: tile_at(packed, BF16, "g_bfD", 33)}
+        xm_bf = {A: tile_at(packed, BF16, "xm_bfA", 44), Bp: tile_at(packed, BF16, "xm_bfB", 4), C: tile_at(packed, BF16, "xm_bfC", 11.5)}
+        early = {bh: tile([P, 2, HALF], F32, f"early{bh[0]}{bh[1]}")[:] for bh in (A, Bp)}
+        early[C] = tile([P, 1, HALF], F32, "earlyC")[:]
+        early[Dp] = tile([P, 2, HALF], F32, "earlyD")[:]
+        staged03 = [tile_at([P, HALF], F32, "staged03a", 13.5), tile_at([P, HALF], F32, "staged03b", 22)]
+        xm_bf13 = tile_at([P, P, PACK], BF16, "xm_bf13", 25)
+        xm_bf12 = tile_at([P, P, PACK], BF16, "xm_bf12", 25)
+        staged11 = tile_at([P, HALF], F32, "staged11", 33)
+        staged02 = tile_at([P, N], F32, "staged02", 25)
+        staged12 = tile([P, N], F32, "staged12")[:]
+        staged13 = tile([P, N], F32, "staged13")[:]
 
         def slots(lo, hi):
             return offsets[:, lo // 16 : hi // 16]
@@ -117,17 +123,23 @@ def tile_attend_gsl2_w_kernel(tc, xT, wT, y, wt, xm, offs, out):
         def quantise(kind, b, src, lo, hi, fmt):
             nc.vector.quantize_mx(out=codes[kind, b][:, lo:hi].bitcast(fmt), scales=scales[kind, b][:, lo:hi], in_=src)
 
-        def cast_x(b, raw, lo, hi, copy):
+        def cast_x(b, dst, u, lo, hi, copy):
             copy(
-                x_bf[b].rearrange("p (u e m j) -> p u m j e", u=2, e=2, j=PACK)[:, :, lo:hi],
-                raw.rearrange("p j (m u e) -> p u m j e", u=2, e=2),
+                dst.rearrange("p (e m j) -> p m j e", e=2, j=PACK)[:, lo:hi],
+                x_raw[b].rearrange("p j (m u e) -> p u m j e", u=2, e=2)[:, u, lo:hi],
             )
 
-        def prepare_xm(b, h):
-            nc.vector.tensor_copy(by_fours_dst(xm_bf[b, h]), by_fours_src(xm_raw[b, h]))
-            quantise("xm", b, flat(xm_bf[b, h]), h * HALF, (h + 1) * HALF, E4M3)
+        def cast_xm(bh):
+            nc.vector.tensor_copy(by_fours_dst(xm_bf[bh]), by_fours_src(xm_raw[bh]))
 
-        def scores(b, h, q):
+        def cast_aside(dst, src):
+            nc.gpsimd.tensor_scalar(dst, src.rearrange("p j c -> p c j"), 1.0, 0.0, ALU.mult, ALU.add)
+
+        def quantise_xm(bh):
+            quantise("xm", bh[0], flat(xm_bf[bh]), bh[1] * HALF, (bh[1] + 1) * HALF, E4M3)
+
+        def scores(bh, q):
+            b, h = bh
             bank = psum.tile([P, PACK, P], F32, name=f"score{h}{q}")
             cols = slice(h * HALF + q * P, h * HALF + (q + 1) * P)
             for t in range(PACK):
@@ -135,35 +147,30 @@ def tile_attend_gsl2_w_kernel(tc, xT, wT, y, wt, xm, offs, out):
                     out=bank[:, t, :],
                     lhsT=codes["x", b][:, t * P : (t + 1) * P].bitcast(E4M3),
                     lhsT_scale=scales["x", b][:, t * P : (t + 1) * P],
-                    rhs=(w0_codes[h][:, q * P : (q + 1) * P] if b == 0 else codes["w", b][:, cols]).bitcast(E4M3),
+                    rhs=codes["w", b][:, cols].bitcast(E4M3),
                     rhs_scale=scales["w", b][:, cols],
                     start=True,
                     stop=True,
                 )
-            nc.scalar.activation(prob[b, h][:, :, q * P : (q + 1) * P], bank[:], ACT.Sigmoid)
+            nc.scalar.activation(prob[bh][:, :, q * P : (q + 1) * P], bank[:], ACT.Sigmoid)
 
-        def square(b, h, lo, hi):
-            nc.scalar.activation(sq[b, h][:, :, lo:hi], prob[b, h][:, :, lo:hi], ACT.Square, bias=centre[:], scale=-1.0)
+        def square(bh, lo, hi):
+            nc.scalar.activation(sq[bh][:, :, lo:hi], prob[bh][:, :, lo:hi], ACT.Square, bias=centre[:], scale=-1.0)
 
-        def error(b, h, lo, hi, engine=nc.vector):
-            engine.tensor_tensor(err[b, h][:, :, lo:hi], y_sb[b, h][:, :, lo:hi], prob[b, h][:, :, lo:hi], ALU.subtract)
+        def error(bh, engine):
+            engine.tensor_tensor(err[bh], y_sb[bh], prob[bh], ALU.subtract)
 
-        def slope(b, h, lo, hi):
+        def weigh(bh):
             for t in range(PACK):
                 nc.vector.tensor_scalar(
-                    sq[b, h][:, t, lo:hi], sq[b, h][:, t, lo:hi], 0.25, wt_sb[:, b, t : t + 1], ALU.subtract, ALU.mult
+                    slope[bh][:, t, :], sq[bh][:, t, :], 0.25, wt_sb[:, bh[0], t : t + 1], ALU.subtract, ALU.mult
                 )
 
-        def gradient(b, h, lo, hi):
-            nc.vector.tensor_tensor(
-                by_fours_dst(g_bf[b, h][:, lo:hi, :]),
-                by_fours_src(sq[b, h][:, :, lo:hi]),
-                by_fours_src(err[b, h][:, :, lo:hi]),
-                ALU.mult,
-            )
+        def gradient(bh):
+            nc.vector.tensor_tensor(by_fours_dst(g_bf[bh]), by_fours_src(slope[bh]), by_fours_src(err[bh]), ALU.mult)
 
-        def quantise_g(b, h):
-            quantise("g", b, flat(g_bf[b, h]), h * HALF, (h + 1) * HALF, E5M2)
+        def quantise_g(bh):
+            quantise("g", bh[0], flat(g_bf[bh]), bh[1] * HALF, (bh[1] + 1) * HALF, E5M2)
 
         def product(dst, b, c, lo, hi):
             nc.tensor.matmul_mx(
@@ -185,80 +192,100 @@ def tile_attend_gsl2_w_kernel(tc, xT, wT, y, wt, xm, offs, out):
         def store(c):
             nc.sync.dma_start(out=out[c * P : (c + 1) * P, :], in_=windows[c][:])
 
-        def early_blocks(b, h):
-            bank = psum.tile([P, HALF], F32, name=f"grad{h}")
-            product(bank[:], b, 0, h * HALF, (h + 1) * HALF)
-            nc.scalar.copy(early[b, h], bank[:])
-            scatter_act(0, b * N + h * HALF, b * N + (h + 1) * HALF, early[b, h])
+        def early_blocks(bh, blocks):
+            b, h = bh
+            bank = psum.tile([P, blocks, HALF], F32, name=f"grad{h}")
+            for c in range(blocks):
+                product(bank[:, c, :], b, c, h * HALF, (h + 1) * HALF)
+            nc.scalar.copy(early[bh], bank[:])
+            for c in range(blocks):
+                scatter_act(c, b * N + h * HALF, b * N + (h + 1) * HALF, early[bh][:, c, :])
 
-        def late_block(b, c, name, dst, copy):
+        def block(b, c, name):
             bank = psum.tile([P, N], F32, name=name)
             product(bank[:], b, c, 0, N)
-            copy(dst, bank[:])
+            return bank
 
         for t in range(PACK):
             for h in range(2):
                 nc.vector.tensor_copy(picked0[h][:, :, t], planes[t][:].indirect(slots(h * HALF, (h + 1) * HALF)))
             nc.scalar.activation(plain[:, t, :], planes[t][:].indirect(slots(N, 2 * N)), ACT.Copy)
-        nc.vector.quantize_mx(out=w0_codes[0].bitcast(E4M3), scales=scales["w", 0][:, half(0)], in_=flat(picked0[0]))
-        cast_x(0, x0_raw[0], 0, 64, nc.scalar.copy)
-        cast_x(0, x0_raw[1], 64, 128, nc.vector.tensor_copy)
-        for u in range(2):
-            quantise("x", 0, x_bf[0][:, u * 1024 : (u + 1) * 1024], u * 256, (u + 1) * 256, E4M3)
+        for h in range(2):
+            quantise("w", 0, flat(picked0[h]), h * HALF, (h + 1) * HALF, E4M3)
         nc.scalar.copy(by_fours_dst(picked1[0]), by_fours_src(plain[:, :, half(0)]))
-        nc.vector.quantize_mx(out=w0_codes[1].bitcast(E4M3), scales=scales["w", 0][:, half(1)], in_=flat(picked0[1]))
-        prepare_xm(0, 0)
-        for q in range(2):
-            scores(0, 0, q)
-            square(0, 0, q * P, (q + 1) * P)
-            error(0, 0, q * P, (q + 1) * P)
-            slope(0, 0, q * P, (q + 1) * P)
-            gradient(0, 0, q * P, (q + 1) * P)
-        for q in range(2):
-            scores(0, 1, q)
-        square(0, 1, 0, HALF)
+        cast_x(0, x0_bf[0], 0, 0, P, nc.vector.tensor_copy)
+        cast_x(0, x0_bf[1], 1, 0, 80, nc.scalar.copy)
+        cast_x(0, x0_bf[1], 1, 80, P, nc.vector.tensor_copy)
+        for u in range(2):
+            quantise("x", 0, x0_bf[u], u * 256, (u + 1) * 256, E4M3)
         nc.scalar.copy(by_fours_dst(picked1[1]), by_fours_src(plain[:, :, half(1)]))
-        quantise_g(0, 0)
+        cast_xm(A)
+        quantise_xm(A)
+        for q in range(2):
+            scores(A, q)
+        for q in range(2):
+            square(A, q * P, (q + 1) * P)
         for h in range(2):
             quantise("w", 1, flat(picked1[h]), h * HALF, (h + 1) * HALF, E4M3)
-        for h in range(2):
-            cast_x(1, x1_raw[:, :, half(h)], 64 * h, 64 * (h + 1), nc.vector.tensor_copy)
-        early_blocks(0, 0)
-        error(0, 1, 0, HALF)
-        quantise("x", 1, x_bf[1], 0, R, E4M3)
-        for h in range(2):
+        error(A, nc.vector)
+        weigh(A)
+        gradient(A)
+        quantise_g(A)
+        for q in range(2):
+            scores(Bp, q)
+        square(Bp, 0, HALF)
+        cast_x(1, x1_bf[:, :1024], 0, 0, P, nc.vector.tensor_copy)
+        cast_x(1, x1_bf[:, 1024:], 1, 0, P, nc.scalar.copy)
+        early_blocks(A, 2)
+        quantise("x", 1, x1_bf, 0, R, E4M3)
+        error(Bp, nc.vector)
+        weigh(Bp)
+        for bh in (C, Dp):
             for q in range(2):
-                scores(1, h, q)
-            square(1, h, 0, HALF)
-        slope(0, 1, 0, HALF)
-        gradient(0, 1, 0, HALF)
-        quantise_g(0, 1)
-        early_blocks(0, 1)
-        late_block(0, 1, "grad2", late10, nc.scalar.copy)
+                scores(bh, q)
+            square(bh, 0, HALF)
+        gradient(Bp)
+        cast_xm(Bp)
+        quantise_xm(Bp)
+        quantise_g(Bp)
+        early_blocks(Bp, 2)
+
+        bank03 = [psum.tile([P, HALF], F32, name=f"late{h}") for h in range(2)]
         for h in range(2):
-            scatter_act(1, h * HALF, (h + 1) * HALF, late10[:, half(h)])
-        prepare_xm(1, 0)
-        for h in range(2):
-            error(1, h, 0, HALF)
-            slope(1, h, 0, HALF)
-            gradient(1, h, 0, HALF)
-            quantise_g(1, h)
-            early_blocks(1, h)
-            prepare_xm(h, 1)
+            product(bank03[h][:], 0, 3, h * HALF, (h + 1) * HALF)
+            nc.vector.tensor_copy(staged03[h], bank03[h][:])
+            scatter_vec(3, h * HALF, (h + 1) * HALF, staged03[h])
+        cast_aside(xm_bf[C], xm_raw[C])
+        error(C, nc.gpsimd)
+        bank02 = block(0, 2, "late0")
+
+        weigh(C)
+        gradient(C)
+        quantise_xm(C)
+        quantise_g(C)
+        early_blocks(C, 1)
+        bank11 = psum.tile([P, HALF], F32, name="score00")
+        product(bank11[:], 1, 1, 0, HALF)
+        error(Dp, nc.vector)
+        weigh(Dp)
+        gradient(Dp)
+        quantise_g(Dp)
+        nc.vector.tensor_copy(by_fours_dst(xm_bf13), by_fours_src(xm1_raw[:, :, 3 * P :]))
+        quantise("xm", 1, flat(xm_bf13), 3 * P, 4 * P, E4M3)
+        cast_aside(xm_bf12, xm1_raw[:, :, 2 * P : 3 * P])
+        nc.vector.tensor_copy(staged11, bank11[:])
+        scatter_vec(1, N, N + HALF, staged11)
+        early_blocks(Dp, 2)
         store(0)
-        late_block(1, 1, "grad2", late11, nc.scalar.copy)
-        for h in range(2):
-            scatter_act(1, N + h * HALF, N + (h + 1) * HALF, late11[:, half(h)])
         store(1)
-        late_block(0, 3, "grad3", late30[:, :N], nc.vector.tensor_copy)
-        bank31 = psum.tile([P, N], F32, name="score00")
-        product(bank31[:], 1, 3, 0, N)
-        nc.vector.tensor_copy(late30[:, N:], bank31[:, :P])
-        late_block(0, 2, "score01", late2[:, :N], nc.vector.tensor_copy)
-        scatter_vec(3, 0, N + P, late30)
-        late_block(1, 2, "score10", late2[:, N:], nc.vector.tensor_copy)
-        nc.scalar.copy(late31, bank31[:, P:])
-        scatter_act(3, N + P, 2 * N, late31)
+
+        nc.scalar.copy(staged13, block(1, 3, "score10")[:])
+        for h in range(2):
+            scatter_act(3, N + h * HALF, N + (h + 1) * HALF, staged13[:, half(h)])
         store(3)
-        scatter_vec(2, 0, 2 * N, late2)
+        quantise("xm", 1, flat(xm_bf12), 2 * P, 3 * P, E4M3)
+        nc.vector.tensor_copy(staged02, bank02[:])
+        scatter_vec(2, 0, N, staged02)
+        nc.vector.tensor_copy(staged12, block(1, 2, "score11")[:])
+        scatter_vec(2, N, 2 * N, staged12)
         store(2)

@@ -46,7 +46,7 @@ def tile_attend_gsl2_w_kernel(tc, xT, wT, y, wt, xm, offs, out):
         A, Bp, C, Dp = pieces = [(b, h) for b in range(B) for h in range(2)]
         offsets = keep.tile([P, B * LIST_COLS], U16, name="offsets")
         planes = [tile([P, T], F32, f"plane{t}") for t in range(PACK)]
-        x_raw = [tile_at([P, PACK, R], F32, "x_raw0", 36), tile([P, PACK, R], F32, "x_raw1")[:]]
+        x_raw = [tile_at([P, PACK, R], F32, "x_raw0", 0), tile_at([P, PACK, R], F32, "x_raw1", 44)]
         xm0_raw = [tile([P, PACK, HALF], F32, f"xm0_raw{h}")[:] for h in range(2)]
         xm1_raw = tile([P, PACK, D], F32, "xm1_raw")[:]
         y0_sb = [tile([P, PACK, HALF], F32, f"y0{h}")[:] for h in range(2)]
@@ -81,35 +81,38 @@ def tile_attend_gsl2_w_kernel(tc, xT, wT, y, wt, xm, offs, out):
         codes, scales = {}, {}
         for b in range(B):
             for kind in ("w", "x", "xm", "g"):
-                if (kind, b) == ("w", 1):
-                    codes[kind, b] = tile_at([P, 512], U32, "w_codes1", 40)
-                else:
+                if (kind, b) != ("w", 1):
                     codes[kind, b] = tile([P, 512], U32, f"{kind}_codes{b}")[:]
                 scales[kind, b] = tile([P, 512], U8, f"{kind}_scales{b}")[:]
+        w_codes = {A: codes["w", 0][:, half(0)], Bp: codes["w", 0][:, half(1)]}
+        w_codes[C] = tile_at([P, HALF], U32, "w_codesC", 2)
+        w_codes[Dp] = tile([P, HALF], U32, "w_codesD")[:]
 
-        picked0 = [tile([P, HALF, PACK], BF16, f"picked0{h}")[:] for h in range(2)]
-        picked1 = [tile([P, HALF, PACK], BF16, "picked10")[:], tile_at([P, HALF, PACK], BF16, "picked11", 36)]
-        plain = tile([P, PACK, N], BF16, "plain")
-        x0_bf = [tile([P, 2 * P * PACK], BF16, "x0_bf0")[:], tile_at([P, 2 * P * PACK], BF16, "x0_bf1", 44)]
-        x1_bf = tile_at([P, R * PACK], BF16, "x1_bf", 0)
         big = [P, PACK, HALF]
+        wide = [P, PACK, N]
         packed = [P, HALF, PACK]
-        prob = {bh: tile(big, F32, f"prob{bh[0]}{bh[1]}")[:] for bh in pieces}
-        sq = {A: tile_at(big, F32, "sqA", 0), Bp: tile_at(big, F32, "sqB", 4), C: tile_at(big, F32, "sqC", 28), Dp: tile(big, F32, "sqD")[:]}
-        slope = {A: tile(big, F32, "slopeA")[:], Bp: tile(big, F32, "slopeB")[:], C: tile_at(big, F32, "slopeC", 18.5), Dp: tile_at(big, F32, "slopeD", 28)}
-        err = {A: y_sb[A], Bp: tile_at(big, F32, "errB", 8), C: tile_at(big, F32, "errC", 14.5), Dp: tile_at(big, F32, "errD", 22.5)}
-        g_bf = {A: tile_at(packed, BF16, "g_bfA", 8), Bp: tile_at(packed, BF16, "g_bfB", 13), C: tile(packed, BF16, "g_bfC")[:], Dp: tile_at(packed, BF16, "g_bfD", 33)}
-        xm_bf = {A: tile_at(packed, BF16, "xm_bfA", 44), Bp: tile_at(packed, BF16, "xm_bfB", 4), C: tile_at(packed, BF16, "xm_bfC", 11.5)}
-        early = {bh: tile([P, 2, HALF], F32, f"early{bh[0]}{bh[1]}")[:] for bh in (A, Bp)}
-        early[C] = tile([P, 1, HALF], F32, "earlyC")[:]
-        early[Dp] = tile([P, 2, HALF], F32, "earlyD")[:]
-        staged03 = [tile_at([P, HALF], F32, "staged03a", 13.5), tile_at([P, HALF], F32, "staged03b", 22)]
-        xm_bf13 = tile_at([P, P, PACK], BF16, "xm_bf13", 25)
-        xm_bf12 = tile_at([P, P, PACK], BF16, "xm_bf12", 25)
-        staged11 = tile_at([P, HALF], F32, "staged11", 33)
-        staged02 = tile_at([P, N], F32, "staged02", 25)
+        picked = {bh: tile(packed, BF16, f"picked{bh[0]}{bh[1]}")[:] for bh in (A, Bp, C)}
+        picked[Dp] = tile_at(packed, BF16, "pickedD", 0)
+        plain = tile([P, PACK, N], BF16, "plain")
+        x0_bf = [tile([P, 2 * P * PACK], BF16, "x0_bf0")[:], tile_at([P, 2 * P * PACK], BF16, "x0_bf1", 8)]
+        x1_bf = tile_at([P, R * PACK], BF16, "x1_bf", 10)
+        prob1, sq1 = tile(wide, F32, "prob1")[:], tile(wide, F32, "sq1")[:]
+        work1 = tile_at([P, 13 * HALF], F32, "work1", 16)
+        slope1 = work1[:, : 8 * HALF].rearrange("p (j c) -> p j c", j=PACK)
+        g0_bf = tile_at([P, N, PACK], BF16, "g0_bf", 28.75)
+        prob = {A: tile(big, F32, "probA")[:], Bp: tile(big, F32, "probB")[:], C: prob1[:, :, half(0)], Dp: prob1[:, :, half(1)]}
+        sq = {A: tile_at(big, F32, "sqA", 12), Bp: tile(big, F32, "sqB")[:], C: sq1[:, :, half(0)], Dp: sq1[:, :, half(1)]}
+        slope = {A: tile(big, F32, "slopeA")[:], Bp: sq[Bp], C: slope1[:, :, half(0)], Dp: slope1[:, :, half(1)]}
+        err = {A: y_sb[A], Bp: tile_at(big, F32, "errB", 44), C: tile_at(big, F32, "errC", 32.5), Dp: work1[:, 8 * HALF : 12 * HALF].rearrange("p (j c) -> p j c", j=PACK)}
+        g_bf = {A: g0_bf[:, half(0), :], Bp: g0_bf[:, half(1), :], C: tile(packed, BF16, "g_bfC")[:], Dp: tile_at(packed, BF16, "g_bfD", 38)}
+        xm_bf = {A: tile_at(packed, BF16, "xm_bfA", 8), Bp: tile_at(packed, BF16, "xm_bfB", 48), C: tile_at(packed, BF16, "xm_bfC", 30.5)}
+        xm_bf13 = work1[:, 12 * HALF :].bitcast(BF16).rearrange("p (c j) -> p c j", j=PACK)
+        early = {bh: tile([P, 1 if bh == C else 2, HALF], F32, f"early{bh[0]}{bh[1]}")[:] for bh in pieces}
+        staged_a = {3: tile_at([P, HALF], F32, "staged_a3", 28.5), 2: tile_at([P, HALF], F32, "staged_a2", 29.5)}
+        xm_bf12 = tile_at([P, P, PACK], BF16, "xm_bf12", 38.5)
+        staged11 = tile_at([P, HALF], F32, "staged11", 37.5)
+        staged_b = tile_at([P, 2 * N], F32, "staged_b", 39.5)
         staged12 = tile([P, N], F32, "staged12")[:]
-        staged13 = tile([P, N], F32, "staged13")[:]
 
         def slots(lo, hi):
             return offsets[:, lo // 16 : hi // 16]
@@ -147,7 +150,7 @@ def tile_attend_gsl2_w_kernel(tc, xT, wT, y, wt, xm, offs, out):
                     out=bank[:, t, :],
                     lhsT=codes["x", b][:, t * P : (t + 1) * P].bitcast(E4M3),
                     lhsT_scale=scales["x", b][:, t * P : (t + 1) * P],
-                    rhs=codes["w", b][:, cols].bitcast(E4M3),
+                    rhs=w_codes[bh][:, q * P : (q + 1) * P].bitcast(E4M3),
                     rhs_scale=scales["w", b][:, cols],
                     start=True,
                     stop=True,
@@ -155,19 +158,25 @@ def tile_attend_gsl2_w_kernel(tc, xT, wT, y, wt, xm, offs, out):
             nc.scalar.activation(prob[bh][:, :, q * P : (q + 1) * P], bank[:], ACT.Sigmoid)
 
         def square(bh, lo, hi):
-            nc.scalar.activation(sq[bh][:, :, lo:hi], prob[bh][:, :, lo:hi], ACT.Square, bias=centre[:], scale=-1.0)
+            nc.scalar.activation(sq[bh][:, :, lo:hi], prob[bh][:, :, lo:hi], ACT.Square, bias=centre[:] if bh == Bp else 0.5, scale=-1.0)
 
-        def error(bh, engine):
-            engine.tensor_tensor(err[bh], y_sb[bh], prob[bh], ALU.subtract)
+        def error(bh, engine, cols=slice(0, HALF)):
+            engine.tensor_tensor(err[bh][:, :, cols], y_sb[bh][:, :, cols], prob[bh][:, :, cols], ALU.subtract)
 
-        def weigh(bh):
+        def weigh(b, dst, src):
             for t in range(PACK):
-                nc.vector.tensor_scalar(
-                    slope[bh][:, t, :], sq[bh][:, t, :], 0.25, wt_sb[:, bh[0], t : t + 1], ALU.subtract, ALU.mult
-                )
+                nc.vector.tensor_scalar(dst[:, t, :], src[:, t, :], 0.25, wt_sb[:, b, t : t + 1], ALU.subtract, ALU.mult)
 
-        def gradient(bh):
-            nc.vector.tensor_tensor(by_fours_dst(g_bf[bh]), by_fours_src(slope[bh]), by_fours_src(err[bh]), ALU.mult)
+        def quantise_w(bh):
+            nc.vector.quantize_mx(out=w_codes[bh].bitcast(E4M3), scales=scales["w", bh[0]][:, half(bh[1])], in_=flat(picked[bh]))
+
+        def weave(bh):
+            nc.scalar.copy(by_fours_dst(picked[bh]), by_fours_src(plain[:, :, half(bh[1])]))
+
+        def gradient(bh, cols=slice(0, HALF)):
+            nc.vector.tensor_tensor(
+                by_fours_dst(g_bf[bh][:, cols, :]), by_fours_src(slope[bh][:, :, cols]), by_fours_src(err[bh][:, :, cols]), ALU.mult
+            )
 
         def quantise_g(bh):
             quantise("g", bh[0], flat(g_bf[bh]), bh[1] * HALF, (bh[1] + 1) * HALF, E5M2)
@@ -207,28 +216,28 @@ def tile_attend_gsl2_w_kernel(tc, xT, wT, y, wt, xm, offs, out):
             return bank
 
         for t in range(PACK):
-            for h in range(2):
-                nc.vector.tensor_copy(picked0[h][:, :, t], planes[t][:].indirect(slots(h * HALF, (h + 1) * HALF)))
+            for bh in (A, Bp):
+                nc.vector.tensor_copy(picked[bh][:, :, t], planes[t][:].indirect(slots(bh[1] * HALF, (bh[1] + 1) * HALF)))
             nc.scalar.activation(plain[:, t, :], planes[t][:].indirect(slots(N, 2 * N)), ACT.Copy)
-        for h in range(2):
-            quantise("w", 0, flat(picked0[h]), h * HALF, (h + 1) * HALF, E4M3)
-        nc.scalar.copy(by_fours_dst(picked1[0]), by_fours_src(plain[:, :, half(0)]))
+        quantise_w(A)
+        quantise_w(Bp)
+        weave(C)
         cast_x(0, x0_bf[0], 0, 0, P, nc.vector.tensor_copy)
         cast_x(0, x0_bf[1], 1, 0, 80, nc.scalar.copy)
         cast_x(0, x0_bf[1], 1, 80, P, nc.vector.tensor_copy)
         for u in range(2):
             quantise("x", 0, x0_bf[u], u * 256, (u + 1) * 256, E4M3)
-        nc.scalar.copy(by_fours_dst(picked1[1]), by_fours_src(plain[:, :, half(1)]))
+        weave(Dp)
         cast_xm(A)
         quantise_xm(A)
+        quantise_w(C)
+        quantise_w(Dp)
         for q in range(2):
             scores(A, q)
         for q in range(2):
             square(A, q * P, (q + 1) * P)
-        for h in range(2):
-            quantise("w", 1, flat(picked1[h]), h * HALF, (h + 1) * HALF, E4M3)
         error(A, nc.vector)
-        weigh(A)
+        weigh(0, slope[A], sq[A])
         gradient(A)
         quantise_g(A)
         for q in range(2):
@@ -239,53 +248,56 @@ def tile_attend_gsl2_w_kernel(tc, xT, wT, y, wt, xm, offs, out):
         early_blocks(A, 2)
         quantise("x", 1, x1_bf, 0, R, E4M3)
         error(Bp, nc.vector)
-        weigh(Bp)
+        weigh(0, slope[Bp], sq[Bp])
+        gradient(Bp)
+        quantise_g(Bp)
+        cast_xm(Bp)
+        quantise_xm(Bp)
         for bh in (C, Dp):
             for q in range(2):
                 scores(bh, q)
             square(bh, 0, HALF)
-        gradient(Bp)
-        cast_xm(Bp)
-        quantise_xm(Bp)
-        quantise_g(Bp)
         early_blocks(Bp, 2)
 
-        bank03 = [psum.tile([P, HALF], F32, name=f"late{h}") for h in range(2)]
-        for h in range(2):
-            product(bank03[h][:], 0, 3, h * HALF, (h + 1) * HALF)
-            nc.vector.tensor_copy(staged03[h], bank03[h][:])
-            scatter_vec(3, h * HALF, (h + 1) * HALF, staged03[h])
+        late = {}
+        for bh in (A, Bp):
+            late[bh] = psum.tile([P, 2, HALF], F32, name=f"late{bh[1]}")
+            for k, c in enumerate((2, 3)):
+                product(late[bh][:, k, :], 0, c, bh[1] * HALF, (bh[1] + 1) * HALF)
+        for c in (3, 2):
+            nc.vector.tensor_copy(staged_a[c], late[A][:, c - 2, :])
+        for c in (3, 2):
+            scatter_vec(c, 0, HALF, staged_a[c])
         cast_aside(xm_bf[C], xm_raw[C])
         error(C, nc.gpsimd)
-        bank02 = block(0, 2, "late0")
 
-        weigh(C)
+        weigh(1, slope[C], sq[C])
         gradient(C)
-        quantise_xm(C)
         quantise_g(C)
+        quantise_xm(C)
+        nc.vector.tensor_copy(by_fours_dst(xm_bf13), by_fours_src(xm1_raw[:, :, 3 * P :]))
         early_blocks(C, 1)
         bank11 = psum.tile([P, HALF], F32, name="score00")
         product(bank11[:], 1, 1, 0, HALF)
         error(Dp, nc.vector)
-        weigh(Dp)
+        weigh(1, slope[Dp], sq[Dp])
         gradient(Dp)
         quantise_g(Dp)
-        nc.vector.tensor_copy(by_fours_dst(xm_bf13), by_fours_src(xm1_raw[:, :, 3 * P :]))
         quantise("xm", 1, flat(xm_bf13), 3 * P, 4 * P, E4M3)
         cast_aside(xm_bf12, xm1_raw[:, :, 2 * P : 3 * P])
         nc.vector.tensor_copy(staged11, bank11[:])
         scatter_vec(1, N, N + HALF, staged11)
+        nc.scalar.copy(staged_b[:, :N], late[Bp][:].rearrange("p k c -> p (k c)"))
         early_blocks(Dp, 2)
         store(0)
         store(1)
 
-        nc.scalar.copy(staged13, block(1, 3, "score10")[:])
-        for h in range(2):
-            scatter_act(3, N + h * HALF, N + (h + 1) * HALF, staged13[:, half(h)])
-        store(3)
+        nc.scalar.copy(staged_b[:, N:], block(1, 3, "score10")[:])
         quantise("xm", 1, flat(xm_bf12), 2 * P, 3 * P, E4M3)
-        nc.vector.tensor_copy(staged02, bank02[:])
-        scatter_vec(2, 0, N, staged02)
+        scatter_act(3, HALF, N + P, staged_b[:, HALF : N + P])
+        scatter_act(3, N + P, 2 * N, staged_b[:, N + P :])
+        scatter_vec(2, HALF, N, staged_b[:, :HALF])
         nc.vector.tensor_copy(staged12, block(1, 2, "score11")[:])
         scatter_vec(2, N, 2 * N, staged12)
         store(2)
+        store(3)

@@ -49,9 +49,9 @@ def tile_attend_gsl2_w_kernel(tc, xT, wT, y, wt, xm, offs, out):
         x_raw = [tile_at([P, PACK, R], F32, "x_raw0", 0), tile_at([P, PACK, R], F32, "x_raw1", 44)]
         xm0_raw = [tile([P, PACK, HALF], F32, f"xm0_raw{h}")[:] for h in range(2)]
         xm1_raw = tile([P, PACK, D], F32, "xm1_raw")[:]
-        y0_sb = [tile([P, PACK, HALF], F32, f"y0{h}")[:] for h in range(2)]
+        y0_sb = [tile([P, PACK, HALF], F32, "y00")[:], tile_at([P, PACK, HALF], F32, "y01", 28.5)]
         y1_sb = tile([P, PACK, N], F32, "y1")[:]
-        xm_raw = {A: xm0_raw[0], Bp: xm0_raw[1], C: xm1_raw[:, :, half(0)]}
+        xm_raw = {A: xm0_raw[0], Bp: xm0_raw[1]}
         y_sb = {A: y0_sb[0], Bp: y0_sb[1], C: y1_sb[:, :, half(0)], Dp: y1_sb[:, :, half(1)]}
         wt_sb = tile([P, B, PACK], F32, "wt_sb")
 
@@ -63,9 +63,9 @@ def tile_attend_gsl2_w_kernel(tc, xT, wT, y, wt, xm, offs, out):
         nc.sync.dma_start(out=xm0_raw[0], in_=rows(xm[0])[:, :, half(0)])
         nc.sync.dma_start(out=y0_sb[0], in_=rows(y[0])[:, :, half(0)])
         nc.sync.dma_start(out=wt_sb[:], in_=wt.rearrange("b (p t) o -> p b (t o)", t=PACK))
+        nc.sync.dma_start(out=xm0_raw[1], in_=rows(xm[0])[:, :, half(1)])
         nc.sync.dma_start(out=x_raw[1], in_=rows(xT[1]))
         nc.sync.dma_start(out=y0_sb[1], in_=rows(y[0])[:, :, half(1)])
-        nc.sync.dma_start(out=xm0_raw[1], in_=rows(xm[0])[:, :, half(1)])
         nc.sync.dma_start(out=xm1_raw, in_=rows(xm[1]))
         nc.sync.dma_start(out=y1_sb, in_=rows(y[1]))
 
@@ -96,21 +96,23 @@ def tile_attend_gsl2_w_kernel(tc, xT, wT, y, wt, xm, offs, out):
         plain = tile([P, PACK, N], BF16, "plain")
         x0_bf = [tile([P, 2 * P * PACK], BF16, "x0_bf0")[:], tile_at([P, 2 * P * PACK], BF16, "x0_bf1", 8)]
         x1_bf = tile_at([P, R * PACK], BF16, "x1_bf", 10)
-        prob1, sq1 = tile(wide, F32, "prob1")[:], tile(wide, F32, "sq1")[:]
+        prob1, sq1 = tile(wide, F32, "prob1")[:], tile_at(wide, F32, "sq1", 52)
         work1 = tile_at([P, 13 * HALF], F32, "work1", 16)
         slope1 = work1[:, : 8 * HALF].rearrange("p (j c) -> p j c", j=PACK)
-        g0_bf = tile_at([P, N, PACK], BF16, "g0_bf", 28.75)
+        g0_bf = tile_at([P, N, PACK], BF16, "g0_bf", 33)
         prob = {A: tile(big, F32, "probA")[:], Bp: tile(big, F32, "probB")[:], C: prob1[:, :, half(0)], Dp: prob1[:, :, half(1)]}
         sq = {A: tile_at(big, F32, "sqA", 12), Bp: tile(big, F32, "sqB")[:], C: sq1[:, :, half(0)], Dp: sq1[:, :, half(1)]}
         slope = {A: tile(big, F32, "slopeA")[:], Bp: sq[Bp], C: slope1[:, :, half(0)], Dp: slope1[:, :, half(1)]}
-        err = {A: y_sb[A], Bp: tile_at(big, F32, "errB", 44), C: tile_at(big, F32, "errC", 32.5), Dp: work1[:, 8 * HALF : 12 * HALF].rearrange("p (j c) -> p j c", j=PACK)}
+        err = {A: y_sb[A], Bp: tile_at(big, F32, "errB", 44), C: tile_at(big, F32, "errC", 36.5), Dp: work1[:, 8 * HALF : 12 * HALF].rearrange("p (j c) -> p j c", j=PACK)}
         g_bf = {A: g0_bf[:, half(0), :], Bp: g0_bf[:, half(1), :], C: tile(packed, BF16, "g_bfC")[:], Dp: tile_at(packed, BF16, "g_bfD", 38)}
-        xm_bf = {A: tile_at(packed, BF16, "xm_bfA", 8), Bp: tile_at(packed, BF16, "xm_bfB", 48), C: tile_at(packed, BF16, "xm_bfC", 30.5)}
-        xm_bf13 = work1[:, 12 * HALF :].bitcast(BF16).rearrange("p (c j) -> p c j", j=PACK)
+        xm_bf = {A: tile_at(packed, BF16, "xm_bfA", 8), Bp: tile(packed, BF16, "xm_bfB")[:]}
+        xm_bf10 = tile_at([P, P, PACK], BF16, "xm_bf10", 33)
+        xm_bf13 = tile_at([P, P, PACK], BF16, "xm_bf13", 37.5)
+        xm_bf11 = work1[:, 12 * HALF :].bitcast(BF16).rearrange("p (c j) -> p c j", j=PACK)
         early = {bh: tile([P, 1 if bh == C else 2, HALF], F32, f"early{bh[0]}{bh[1]}")[:] for bh in pieces}
         staged_a = {3: tile_at([P, HALF], F32, "staged_a3", 28.5), 2: tile_at([P, HALF], F32, "staged_a2", 29.5)}
         xm_bf12 = tile_at([P, P, PACK], BF16, "xm_bf12", 38.5)
-        staged11 = tile_at([P, HALF], F32, "staged11", 37.5)
+        staged11 = tile_at([P, HALF], F32, "staged11", 52)
         staged_b = tile_at([P, 2 * N], F32, "staged_b", 39.5)
         staged12 = tile([P, N], F32, "staged12")[:]
 
@@ -268,14 +270,15 @@ def tile_attend_gsl2_w_kernel(tc, xT, wT, y, wt, xm, offs, out):
             nc.vector.tensor_copy(staged_a[c], late[A][:, c - 2, :])
         for c in (3, 2):
             scatter_vec(c, 0, HALF, staged_a[c])
-        cast_aside(xm_bf[C], xm_raw[C])
+        cast_aside(xm_bf10, xm1_raw[:, :, :P])
         error(C, nc.gpsimd)
 
         weigh(1, slope[C], sq[C])
         gradient(C)
         quantise_g(C)
-        quantise_xm(C)
-        nc.vector.tensor_copy(by_fours_dst(xm_bf13), by_fours_src(xm1_raw[:, :, 3 * P :]))
+        nc.vector.tensor_copy(by_fours_dst(xm_bf11), by_fours_src(xm1_raw[:, :, P : 2 * P]))
+        quantise("xm", 1, flat(xm_bf10), 0, P, E4M3)
+        quantise("xm", 1, flat(xm_bf11), P, 2 * P, E4M3)
         early_blocks(C, 1)
         bank11 = psum.tile([P, HALF], F32, name="score00")
         product(bank11[:], 1, 1, 0, HALF)
@@ -283,8 +286,8 @@ def tile_attend_gsl2_w_kernel(tc, xT, wT, y, wt, xm, offs, out):
         weigh(1, slope[Dp], sq[Dp])
         gradient(Dp)
         quantise_g(Dp)
-        quantise("xm", 1, flat(xm_bf13), 3 * P, 4 * P, E4M3)
         cast_aside(xm_bf12, xm1_raw[:, :, 2 * P : 3 * P])
+        cast_aside(xm_bf13, xm1_raw[:, :, 3 * P :])
         nc.vector.tensor_copy(staged11, bank11[:])
         scatter_vec(1, N, N + HALF, staged11)
         nc.scalar.copy(staged_b[:, :N], late[Bp][:].rearrange("p k c -> p (k c)"))
@@ -292,12 +295,13 @@ def tile_attend_gsl2_w_kernel(tc, xT, wT, y, wt, xm, offs, out):
         store(0)
         store(1)
 
-        nc.scalar.copy(staged_b[:, N:], block(1, 3, "score10")[:])
         quantise("xm", 1, flat(xm_bf12), 2 * P, 3 * P, E4M3)
-        scatter_act(3, HALF, N + P, staged_b[:, HALF : N + P])
-        scatter_act(3, N + P, 2 * N, staged_b[:, N + P :])
+        quantise("xm", 1, flat(xm_bf13), 3 * P, 4 * P, E4M3)
         scatter_vec(2, HALF, N, staged_b[:, :HALF])
         nc.vector.tensor_copy(staged12, block(1, 2, "score11")[:])
+        nc.vector.tensor_copy(staged_b[:, N:], block(1, 3, "score10")[:])
+        scatter_act(3, HALF, N + P, staged_b[:, HALF : N + P])
+        scatter_act(3, N + P, 2 * N, staged_b[:, N + P :])
         scatter_vec(2, N, 2 * N, staged12)
         store(2)
         store(3)

@@ -109,7 +109,8 @@ def tile_attend_gsl2_w_kernel(tc, xT, wT, y, wt, xm, offs, out):
         xm_bf10 = tile_at([P, P, PACK], BF16, "xm_bf10", 33)
         xm_bf13 = tile_at([P, P, PACK], BF16, "xm_bf13", 37.5)
         xm_bf11 = work1[:, 12 * HALF :].bitcast(BF16).rearrange("p (c j) -> p c j", j=PACK)
-        early = {bh: tile([P, 1 if bh == C else 2, HALF], F32, f"early{bh[0]}{bh[1]}")[:] for bh in pieces}
+        early = {bh: tile([P, 1 + bh[1], HALF], F32, f"early{bh[0]}{bh[1]}")[:] for bh in pieces}
+        staged01 = tile([P, HALF], F32, "staged01")[:]
         staged_a = {3: tile_at([P, HALF], F32, "staged_a3", 28.5), 2: tile_at([P, HALF], F32, "staged_a2", 29.5)}
         xm_bf12 = tile_at([P, P, PACK], BF16, "xm_bf12", 38.5)
         staged11 = tile_at([P, HALF], F32, "staged11", 52)
@@ -247,7 +248,7 @@ def tile_attend_gsl2_w_kernel(tc, xT, wT, y, wt, xm, offs, out):
         square(Bp, 0, HALF)
         cast_x(1, x1_bf[:, :1024], 0, 0, P, nc.vector.tensor_copy)
         cast_x(1, x1_bf[:, 1024:], 1, 0, P, nc.scalar.copy)
-        early_blocks(A, 2)
+        early_blocks(A, 1)
         quantise("x", 1, x1_bf, 0, R, E4M3)
         error(Bp, nc.vector)
         weigh(0, slope[Bp], sq[Bp])
@@ -259,6 +260,10 @@ def tile_attend_gsl2_w_kernel(tc, xT, wT, y, wt, xm, offs, out):
             for q in range(2):
                 scores(bh, q)
             square(bh, 0, HALF)
+        bank01 = psum.tile([P, HALF], F32, name="score01")
+        product(bank01[:], 0, 1, 0, HALF)
+        nc.scalar.copy(staged01, bank01[:])
+        scatter_act(1, 0, HALF, staged01)
         early_blocks(Bp, 2)
 
         late = {}

@@ -48,11 +48,11 @@ def tile_attend_gsl2_w_kernel(tc, xT, wT, y, wt, xm, offs, out):
         planes = [tile([P, T], F32, f"plane{t}") for t in range(PACK)]
         x_raw = [tile_at([P, PACK, R], F32, "x_raw0", 0), tile_at([P, PACK, R], F32, "x_raw1", 44)]
         xm0_raw = [tile([P, PACK, HALF], F32, f"xm0_raw{h}")[:] for h in range(2)]
-        xm1_raw = tile([P, PACK, D], F32, "xm1_raw")[:]
+        xm1_raw = [tile([P, PACK, HALF], F32, f"xm1_raw{h}")[:] for h in range(2)]
         y0_sb = [tile([P, PACK, HALF], F32, "y00")[:], tile_at([P, PACK, HALF], F32, "y01", 28.5)]
-        y1_sb = tile([P, PACK, N], F32, "y1")[:]
-        xm_raw = {A: xm0_raw[0], Bp: xm0_raw[1]}
-        y_sb = {A: y0_sb[0], Bp: y0_sb[1], C: y1_sb[:, :, half(0)], Dp: y1_sb[:, :, half(1)]}
+        y1_sb = [tile([P, PACK, HALF], F32, f"y1{h}")[:] for h in range(2)]
+        xm_raw = {A: xm0_raw[0], Bp: xm0_raw[1], C: xm1_raw[0], Dp: xm1_raw[1]}
+        y_sb = {A: y0_sb[0], Bp: y0_sb[1], C: y1_sb[0], Dp: y1_sb[1]}
         wt_sb = tile([P, B, PACK], F32, "wt_sb")
 
         for t in range(PACK):
@@ -66,8 +66,9 @@ def tile_attend_gsl2_w_kernel(tc, xT, wT, y, wt, xm, offs, out):
         nc.sync.dma_start(out=xm0_raw[1], in_=rows(xm[0])[:, :, half(1)])
         nc.sync.dma_start(out=x_raw[1], in_=rows(xT[1]))
         nc.sync.dma_start(out=y0_sb[1], in_=rows(y[0])[:, :, half(1)])
-        nc.sync.dma_start(out=xm1_raw, in_=rows(xm[1]))
-        nc.sync.dma_start(out=y1_sb, in_=rows(y[1]))
+        for h in range(2):
+            nc.sync.dma_start(out=y1_sb[h], in_=rows(y[1])[:, :, half(h)])
+            nc.sync.dma_start(out=xm1_raw[h], in_=rows(xm[1])[:, :, half(h)])
 
         zero = tile([P, 1], F32, "zero")
         centre = tile([P, 1], F32, "centre")
@@ -89,32 +90,30 @@ def tile_attend_gsl2_w_kernel(tc, xT, wT, y, wt, xm, offs, out):
         w_codes[Dp] = tile([P, HALF], U32, "w_codesD")[:]
 
         big = [P, PACK, HALF]
-        wide = [P, PACK, N]
         packed = [P, HALF, PACK]
         picked = {bh: tile(packed, BF16, f"picked{bh[0]}{bh[1]}")[:] for bh in (A, Bp, C)}
         picked[Dp] = tile_at(packed, BF16, "pickedD", 0)
         plain = tile([P, PACK, N], BF16, "plain")
         x0_bf = [tile([P, 2 * P * PACK], BF16, "x0_bf0")[:], tile_at([P, 2 * P * PACK], BF16, "x0_bf1", 8)]
         x1_bf = tile_at([P, R * PACK], BF16, "x1_bf", 10)
-        prob1, sq1 = tile(wide, F32, "prob1")[:], tile_at(wide, F32, "sq1", 52)
-        work1 = tile_at([P, 13 * HALF], F32, "work1", 16)
-        slope1 = work1[:, : 8 * HALF].rearrange("p (j c) -> p j c", j=PACK)
-        g0_bf = tile_at([P, N, PACK], BF16, "g0_bf", 33)
-        prob = {A: tile(big, F32, "probA")[:], Bp: tile(big, F32, "probB")[:], C: prob1[:, :, half(0)], Dp: prob1[:, :, half(1)]}
-        sq = {A: tile_at(big, F32, "sqA", 12), Bp: tile(big, F32, "sqB")[:], C: sq1[:, :, half(0)], Dp: sq1[:, :, half(1)]}
-        slope = {A: tile(big, F32, "slopeA")[:], Bp: sq[Bp], C: slope1[:, :, half(0)], Dp: slope1[:, :, half(1)]}
-        err = {A: y_sb[A], Bp: tile_at(big, F32, "errB", 44), C: tile_at(big, F32, "errC", 36.5), Dp: work1[:, 8 * HALF : 12 * HALF].rearrange("p (j c) -> p j c", j=PACK)}
-        g_bf = {A: g0_bf[:, half(0), :], Bp: g0_bf[:, half(1), :], C: tile(packed, BF16, "g_bfC")[:], Dp: tile_at(packed, BF16, "g_bfD", 38)}
+        work1 = tile_at([P, 11 * HALF], F32, "work1", 18)
+        g0_bf = tile_at([P, N, PACK], BF16, "g0_bf", 37)
+        shift = tile([P, PACK], F32, "shift")
+        prob = {bh: tile(big, F32, f"prob{bh[0]}{bh[1]}")[:] for bh in pieces}
+        sq = {A: tile_at(big, F32, "sqA", 12), Bp: tile(big, F32, "sqB")[:], C: tile(big, F32, "sqC")[:], Dp: tile_at(big, F32, "sqD", 52)}
+        slope = {A: tile(big, F32, "slopeA")[:], Bp: sq[Bp], C: tile_at(big, F32, "slopeC", 33.5), Dp: work1[:, : 4 * HALF].rearrange("p (j c) -> p j c", j=PACK)}
+        err = {A: y_sb[A], Bp: tile_at(big, F32, "errB", 44), C: tile_at(big, F32, "errC", 40.5), Dp: work1[:, 4 * HALF : 8 * HALF].rearrange("p (j c) -> p j c", j=PACK)}
+        g_bf = {A: g0_bf[:, half(0), :], Bp: g0_bf[:, half(1), :], C: tile(packed, BF16, "g_bfC")[:], Dp: tile_at(packed, BF16, "g_bfD", 16)}
         xm_bf = {A: tile_at(packed, BF16, "xm_bfA", 8), Bp: tile(packed, BF16, "xm_bfB")[:]}
-        xm_bf10 = tile_at([P, P, PACK], BF16, "xm_bf10", 33)
-        xm_bf13 = tile_at([P, P, PACK], BF16, "xm_bf13", 37.5)
-        xm_bf11 = work1[:, 12 * HALF :].bitcast(BF16).rearrange("p (c j) -> p c j", j=PACK)
+        xm_bf13 = work1[:, 10 * HALF :].bitcast(BF16).rearrange("p (c j) -> p c j", j=PACK)
+        xm_bf[C] = work1[:, 8 * HALF : 10 * HALF].bitcast(BF16).rearrange("p (c j) -> p c j", j=PACK)
         early = {bh: tile([P, 1 + bh[1], HALF], F32, f"early{bh[0]}{bh[1]}")[:] for bh in pieces}
         staged01 = tile([P, HALF], F32, "staged01")[:]
         staged_a = {3: tile_at([P, HALF], F32, "staged_a3", 28.5), 2: tile_at([P, HALF], F32, "staged_a2", 29.5)}
-        xm_bf12 = tile_at([P, P, PACK], BF16, "xm_bf12", 38.5)
+        xm_bf12 = tile_at([P, P, PACK], BF16, "xm_bf12", 17.5)
         staged11 = tile_at([P, HALF], F32, "staged11", 52)
-        staged_b = tile_at([P, 2 * N], F32, "staged_b", 39.5)
+        staged02 = tile_at([P, HALF], F32, "staged02", 16.5)
+        staged3 = tile_at([P, HALF + N], F32, "staged3", 13.5)
         staged12 = tile([P, N], F32, "staged12")[:]
 
         def slots(lo, hi):
@@ -166,8 +165,8 @@ def tile_attend_gsl2_w_kernel(tc, xT, wT, y, wt, xm, offs, out):
         def error(bh, engine, cols=slice(0, HALF)):
             engine.tensor_tensor(err[bh][:, :, cols], y_sb[bh][:, :, cols], prob[bh][:, :, cols], ALU.subtract)
 
-        def weigh(b, dst, src):
-            for t in range(PACK):
+        def weigh(b, dst, src, places=range(PACK)):
+            for t in places:
                 nc.vector.tensor_scalar(dst[:, t, :], src[:, t, :], 0.25, wt_sb[:, b, t : t + 1], ALU.subtract, ALU.mult)
 
         def quantise_w(bh):
@@ -235,6 +234,7 @@ def tile_attend_gsl2_w_kernel(tc, xT, wT, y, wt, xm, offs, out):
         quantise_xm(A)
         quantise_w(C)
         quantise_w(Dp)
+        nc.vector.tensor_scalar(shift[:], wt_sb[:, 1, :], -0.25, None, ALU.mult)
         for q in range(2):
             scores(A, q)
         for q in range(2):
@@ -275,15 +275,17 @@ def tile_attend_gsl2_w_kernel(tc, xT, wT, y, wt, xm, offs, out):
             nc.vector.tensor_copy(staged_a[c], late[A][:, c - 2, :])
         for c in (3, 2):
             scatter_vec(c, 0, HALF, staged_a[c])
-        cast_aside(xm_bf10, xm1_raw[:, :, :P])
         error(C, nc.gpsimd)
+        for t in range(2):
+            nc.gpsimd.tensor_scalar(
+                slope[C][:, t, :], sq[C][:, t, :], wt_sb[:, 1, t : t + 1], shift[:, t : t + 1], ALU.mult, ALU.add
+            )
 
-        weigh(1, slope[C], sq[C])
+        weigh(1, slope[C], sq[C], range(2, PACK))
         gradient(C)
         quantise_g(C)
-        nc.vector.tensor_copy(by_fours_dst(xm_bf11), by_fours_src(xm1_raw[:, :, P : 2 * P]))
-        quantise("xm", 1, flat(xm_bf10), 0, P, E4M3)
-        quantise("xm", 1, flat(xm_bf11), P, 2 * P, E4M3)
+        cast_xm(C)
+        quantise_xm(C)
         early_blocks(C, 1)
         bank11 = psum.tile([P, HALF], F32, name="score00")
         product(bank11[:], 1, 1, 0, HALF)
@@ -291,22 +293,23 @@ def tile_attend_gsl2_w_kernel(tc, xT, wT, y, wt, xm, offs, out):
         weigh(1, slope[Dp], sq[Dp])
         gradient(Dp)
         quantise_g(Dp)
-        cast_aside(xm_bf12, xm1_raw[:, :, 2 * P : 3 * P])
-        cast_aside(xm_bf13, xm1_raw[:, :, 3 * P :])
+        cast_aside(xm_bf12, xm_raw[Dp][:, :, :P])
+        nc.vector.tensor_copy(by_fours_dst(xm_bf13), by_fours_src(xm_raw[Dp][:, :, P:]))
+        quantise("xm", 1, flat(xm_bf13), 3 * P, 4 * P, E4M3)
         nc.vector.tensor_copy(staged11, bank11[:])
         scatter_vec(1, N, N + HALF, staged11)
-        nc.scalar.copy(staged_b[:, :N], late[Bp][:].rearrange("p k c -> p (k c)"))
+        nc.scalar.copy(staged3[:, :HALF], late[Bp][:, 1, :])
         early_blocks(Dp, 2)
         store(0)
         store(1)
 
+        nc.vector.tensor_copy(staged02, late[Bp][:, 0, :])
+        nc.vector.tensor_copy(staged3[:, HALF:], block(1, 3, "score10")[:])
         quantise("xm", 1, flat(xm_bf12), 2 * P, 3 * P, E4M3)
-        quantise("xm", 1, flat(xm_bf13), 3 * P, 4 * P, E4M3)
-        scatter_vec(2, HALF, N, staged_b[:, :HALF])
+        scatter_vec(2, HALF, N, staged02)
         nc.vector.tensor_copy(staged12, block(1, 2, "score11")[:])
-        nc.vector.tensor_copy(staged_b[:, N:], block(1, 3, "score10")[:])
-        scatter_act(3, HALF, N + P, staged_b[:, HALF : N + P])
-        scatter_act(3, N + P, 2 * N, staged_b[:, N + P :])
+        scatter_act(3, HALF, N + P, staged3[:, : HALF + P])
+        scatter_act(3, N + P, 2 * N, staged3[:, HALF + P :])
         scatter_vec(2, N, 2 * N, staged12)
         store(2)
         store(3)

@@ -49,7 +49,7 @@ def tile_attend_gsl2_w_kernel(tc, xT, wT, y, wt, xm, offs, out):
         x_raw = [tile_at([P, PACK, R], F32, "x_raw0", 0), tile_at([P, PACK, R], F32, "x_raw1", 44)]
         xm0_raw = [tile([P, PACK, HALF], F32, f"xm0_raw{h}")[:] for h in range(2)]
         xm1_raw = [tile([P, PACK, HALF], F32, f"xm1_raw{h}")[:] for h in range(2)]
-        y0_sb = [tile([P, PACK, HALF], F32, "y00")[:], tile_at([P, PACK, HALF], F32, "y01", 28.5)]
+        y0_sb = [tile([P, PACK, HALF], F32, "y00")[:], tile_at([P, PACK, HALF], F32, "y01", 31.5)]
         y1_sb = [tile([P, PACK, HALF], F32, f"y1{h}")[:] for h in range(2)]
         xm_raw = {A: xm0_raw[0], Bp: xm0_raw[1], C: xm1_raw[0], Dp: xm1_raw[1]}
         y_sb = {A: y0_sb[0], Bp: y0_sb[1], C: y1_sb[0], Dp: y1_sb[1]}
@@ -96,20 +96,20 @@ def tile_attend_gsl2_w_kernel(tc, xT, wT, y, wt, xm, offs, out):
         plain = tile([P, PACK, N], BF16, "plain")
         x0_bf = [tile([P, 2 * P * PACK], BF16, "x0_bf0")[:], tile_at([P, 2 * P * PACK], BF16, "x0_bf1", 8)]
         x1_bf = tile_at([P, R * PACK], BF16, "x1_bf", 10)
-        work1 = tile_at([P, 11 * HALF], F32, "work1", 18)
+        work1 = tile_at([P, 14 * HALF], F32, "work1", 18)
         g0_bf = tile_at([P, N, PACK], BF16, "g0_bf", 37)
-        shift = tile([P, PACK], F32, "shift")
         prob = {bh: tile(big, F32, f"prob{bh[0]}{bh[1]}")[:] for bh in pieces}
         sq = {A: tile_at(big, F32, "sqA", 12), Bp: tile(big, F32, "sqB")[:], C: tile(big, F32, "sqC")[:], Dp: tile_at(big, F32, "sqD", 52)}
-        slope = {A: tile(big, F32, "slopeA")[:], Bp: sq[Bp], C: tile_at(big, F32, "slopeC", 33.5), Dp: work1[:, : 4 * HALF].rearrange("p (j c) -> p j c", j=PACK)}
+        slope = {A: tile(big, F32, "slopeA")[:], Bp: sq[Bp], C: work1[:, 10 * HALF :].rearrange("p (j c) -> p j c", j=PACK), Dp: work1[:, : 4 * HALF].rearrange("p (j c) -> p j c", j=PACK)}
         err = {A: y_sb[A], Bp: tile_at(big, F32, "errB", 44), C: tile_at(big, F32, "errC", 40.5), Dp: work1[:, 4 * HALF : 8 * HALF].rearrange("p (j c) -> p j c", j=PACK)}
         g_bf = {A: g0_bf[:, half(0), :], Bp: g0_bf[:, half(1), :], C: tile(packed, BF16, "g_bfC")[:], Dp: tile_at(packed, BF16, "g_bfD", 16)}
         xm_bf = {A: tile_at(packed, BF16, "xm_bfA", 8), Bp: tile(packed, BF16, "xm_bfB")[:]}
-        xm_bf13 = work1[:, 10 * HALF :].bitcast(BF16).rearrange("p (c j) -> p c j", j=PACK)
-        xm_bf[C] = work1[:, 8 * HALF : 10 * HALF].bitcast(BF16).rearrange("p (c j) -> p c j", j=PACK)
+        xm_bf13 = work1[:, 9 * HALF : 10 * HALF].bitcast(BF16).rearrange("p (c j) -> p c j", j=PACK)
+        xm_bf10 = tile_at([P, P, PACK], BF16, "xm_bf10", 37)
+        xm_bf11 = work1[:, 8 * HALF : 9 * HALF].bitcast(BF16).rearrange("p (c j) -> p c j", j=PACK)
         early = {bh: tile([P, 1 + bh[1], HALF], F32, f"early{bh[0]}{bh[1]}")[:] for bh in pieces}
         staged01 = tile([P, HALF], F32, "staged01")[:]
-        staged_a = {3: tile_at([P, HALF], F32, "staged_a3", 28.5), 2: tile_at([P, HALF], F32, "staged_a2", 29.5)}
+        staged_a = {3: tile_at([P, HALF], F32, "staged_a3", 31.5), 2: tile_at([P, HALF], F32, "staged_a2", 32.5)}
         xm_bf12 = tile_at([P, P, PACK], BF16, "xm_bf12", 17.5)
         staged11 = tile_at([P, HALF], F32, "staged11", 52)
         staged02 = tile_at([P, HALF], F32, "staged02", 16.5)
@@ -165,8 +165,8 @@ def tile_attend_gsl2_w_kernel(tc, xT, wT, y, wt, xm, offs, out):
         def error(bh, engine, cols=slice(0, HALF)):
             engine.tensor_tensor(err[bh][:, :, cols], y_sb[bh][:, :, cols], prob[bh][:, :, cols], ALU.subtract)
 
-        def weigh(b, dst, src, places=range(PACK)):
-            for t in places:
+        def weigh(b, dst, src):
+            for t in range(PACK):
                 nc.vector.tensor_scalar(dst[:, t, :], src[:, t, :], 0.25, wt_sb[:, b, t : t + 1], ALU.subtract, ALU.mult)
 
         def quantise_w(bh):
@@ -234,7 +234,6 @@ def tile_attend_gsl2_w_kernel(tc, xT, wT, y, wt, xm, offs, out):
         quantise_xm(A)
         quantise_w(C)
         quantise_w(Dp)
-        nc.vector.tensor_scalar(shift[:], wt_sb[:, 1, :], -0.25, None, ALU.mult)
         for q in range(2):
             scores(A, q)
         for q in range(2):
@@ -276,16 +275,14 @@ def tile_attend_gsl2_w_kernel(tc, xT, wT, y, wt, xm, offs, out):
         for c in (3, 2):
             scatter_vec(c, 0, HALF, staged_a[c])
         error(C, nc.gpsimd)
-        for t in range(2):
-            nc.gpsimd.tensor_scalar(
-                slope[C][:, t, :], sq[C][:, t, :], wt_sb[:, 1, t : t + 1], shift[:, t : t + 1], ALU.mult, ALU.add
-            )
+        cast_aside(xm_bf10, xm_raw[C][:, :, :P])
 
-        weigh(1, slope[C], sq[C], range(2, PACK))
+        weigh(1, slope[C], sq[C])
         gradient(C)
         quantise_g(C)
-        cast_xm(C)
-        quantise_xm(C)
+        nc.vector.tensor_copy(by_fours_dst(xm_bf11), by_fours_src(xm_raw[C][:, :, P:]))
+        quantise("xm", 1, flat(xm_bf10), 0, P, E4M3)
+        quantise("xm", 1, flat(xm_bf11), P, 2 * P, E4M3)
         early_blocks(C, 1)
         bank11 = psum.tile([P, HALF], F32, name="score00")
         product(bank11[:], 1, 1, 0, HALF)

@@ -67,8 +67,8 @@ def tile_attend_gsl2_w_kernel(tc, xT, wT, y, wt, xm, offs, out):
         nc.sync.dma_start(out=x_raw[1], in_=rows(xT[1]))
         nc.sync.dma_start(out=y0_sb[1], in_=rows(y[0])[:, :, half(1)])
         for h in range(2):
-            nc.sync.dma_start(out=y1_sb[h], in_=rows(y[1])[:, :, half(h)])
             nc.sync.dma_start(out=xm1_raw[h], in_=rows(xm[1])[:, :, half(h)])
+            nc.sync.dma_start(out=y1_sb[h], in_=rows(y[1])[:, :, half(h)])
 
         zero = tile([P, 1], F32, "zero")
         centre = tile([P, 1], F32, "centre")
@@ -274,8 +274,8 @@ def tile_attend_gsl2_w_kernel(tc, xT, wT, y, wt, xm, offs, out):
             nc.vector.tensor_copy(staged_a[c], late[A][:, c - 2, :])
         for c in (3, 2):
             scatter_vec(c, 0, HALF, staged_a[c])
-        error(C, nc.gpsimd)
         cast_aside(xm_bf10, xm_raw[C][:, :, :P])
+        error(C, nc.gpsimd)
 
         weigh(1, slope[C], sq[C])
         gradient(C)

@@ -60,11 +60,11 @@ def tile_attend_gsl2_w_kernel(tc, xT, wT, y, wt, xm, offs, out):
             if t == 0:
                 nc.sync.dma_start(offsets[:], offs)
         nc.sync.dma_start(out=x_raw[0], in_=rows(xT[0]))
-        nc.sync.dma_start(out=xm0_raw[0], in_=rows(xm[0])[:, :, half(0)])
+        nc.sync.dma_start(out=x_raw[1], in_=rows(xT[1]))
         nc.sync.dma_start(out=y0_sb[0], in_=rows(y[0])[:, :, half(0)])
         nc.sync.dma_start(out=wt_sb[:], in_=wt.rearrange("b (p t) o -> p b (t o)", t=PACK))
+        nc.sync.dma_start(out=xm0_raw[0], in_=rows(xm[0])[:, :, half(0)])
         nc.sync.dma_start(out=xm0_raw[1], in_=rows(xm[0])[:, :, half(1)])
-        nc.sync.dma_start(out=x_raw[1], in_=rows(xT[1]))
         nc.sync.dma_start(out=y0_sb[1], in_=rows(y[0])[:, :, half(1)])
         for h in range(2):
             nc.sync.dma_start(out=xm1_raw[h], in_=rows(xm[1])[:, :, half(h)])
@@ -82,7 +82,7 @@ def tile_attend_gsl2_w_kernel(tc, xT, wT, y, wt, xm, offs, out):
         codes, scales = {}, {}
         for b in range(B):
             for kind in ("w", "x", "xm", "g"):
-                if (kind, b) != ("w", 1):
+                if (kind, b) not in (("w", 1), ("x", 1)):
                     codes[kind, b] = tile([P, 512], U32, f"{kind}_codes{b}")[:]
                 scales[kind, b] = tile([P, 512], U8, f"{kind}_scales{b}")[:]
         w_codes = {A: codes["w", 0][:, half(0)], Bp: codes["w", 0][:, half(1)]}
@@ -98,9 +98,11 @@ def tile_attend_gsl2_w_kernel(tc, xT, wT, y, wt, xm, offs, out):
         x1_bf = tile_at([P, R * PACK], BF16, "x1_bf", 10)
         work1 = tile_at([P, 14 * HALF], F32, "work1", 18)
         g0_bf = tile_at([P, N, PACK], BF16, "g0_bf", 37)
-        prob = {bh: tile(big, F32, f"prob{bh[0]}{bh[1]}")[:] for bh in pieces}
-        sq = {A: tile_at(big, F32, "sqA", 12), Bp: tile(big, F32, "sqB")[:], C: tile(big, F32, "sqC")[:], Dp: tile_at(big, F32, "sqD", 52)}
-        slope = {A: tile(big, F32, "slopeA")[:], Bp: sq[Bp], C: work1[:, 10 * HALF :].rearrange("p (j c) -> p j c", j=PACK), Dp: work1[:, : 4 * HALF].rearrange("p (j c) -> p j c", j=PACK)}
+        prob = {bh: tile(big, F32, f"prob{bh[0]}{bh[1]}")[:] for bh in (Bp, C, Dp)}
+        prob[A] = tile_at(big, F32, "probA", 56)
+        codes["x", 1] = tile_at([P, 512], U32, "x_codes1", 56)
+        sq = {A: tile(big, F32, "sqA")[:], Bp: tile(big, F32, "sqB")[:], C: tile(big, F32, "sqC")[:], Dp: tile_at(big, F32, "sqD", 52)}
+        slope = {A: sq[A], Bp: sq[Bp], C: work1[:, 10 * HALF :].rearrange("p (j c) -> p j c", j=PACK), Dp: work1[:, : 4 * HALF].rearrange("p (j c) -> p j c", j=PACK)}
         err = {A: y_sb[A], Bp: tile_at(big, F32, "errB", 44), C: tile_at(big, F32, "errC", 40.5), Dp: work1[:, 4 * HALF : 8 * HALF].rearrange("p (j c) -> p j c", j=PACK)}
         g_bf = {A: g0_bf[:, half(0), :], Bp: g0_bf[:, half(1), :], C: tile(packed, BF16, "g_bfC")[:], Dp: tile_at(packed, BF16, "g_bfD", 16)}
         xm_bf = {A: tile_at(packed, BF16, "xm_bfA", 8), Bp: tile(packed, BF16, "xm_bfB")[:]}
@@ -134,8 +136,8 @@ def tile_attend_gsl2_w_kernel(tc, xT, wT, y, wt, xm, offs, out):
                 x_raw[b].rearrange("p j (m u e) -> p u m j e", u=2, e=2)[:, u, lo:hi],
             )
 
-        def cast_xm(bh):
-            nc.vector.tensor_copy(by_fours_dst(xm_bf[bh]), by_fours_src(xm_raw[bh]))
+        def cast_xm(bh, copy):
+            copy(by_fours_dst(xm_bf[bh]), by_fours_src(xm_raw[bh]))
 
         def cast_aside(dst, src):
             nc.gpsimd.tensor_scalar(dst, src.rearrange("p j c -> p c j"), 1.0, 0.0, ALU.mult, ALU.add)
@@ -230,35 +232,37 @@ def tile_attend_gsl2_w_kernel(tc, xT, wT, y, wt, xm, offs, out):
         for u in range(2):
             quantise("x", 0, x0_bf[u], u * 256, (u + 1) * 256, E4M3)
         weave(Dp)
-        cast_xm(A)
-        quantise_xm(A)
         quantise_w(C)
         quantise_w(Dp)
+        for u in range(2):
+            cast_x(1, x1_bf[:, u * 1024 : (u + 1) * 1024], u, 0, P, nc.vector.tensor_copy)
         for q in range(2):
             scores(A, q)
         for q in range(2):
             square(A, q * P, (q + 1) * P)
         error(A, nc.vector)
         weigh(0, slope[A], sq[A])
-        gradient(A)
-        quantise_g(A)
+        quantise("x", 1, x1_bf, 0, R, E4M3)
         for q in range(2):
             scores(Bp, q)
+        cast_xm(A, nc.scalar.copy)
+        gradient(A)
+        quantise_xm(A)
+        quantise_g(A)
         square(Bp, 0, HALF)
-        cast_x(1, x1_bf[:, :1024], 0, 0, P, nc.vector.tensor_copy)
-        cast_x(1, x1_bf[:, 1024:], 1, 0, P, nc.scalar.copy)
+        for q in range(2):
+            scores(C, q)
+        cast_xm(Bp, nc.vector.tensor_copy)
         early_blocks(A, 1)
-        quantise("x", 1, x1_bf, 0, R, E4M3)
         error(Bp, nc.vector)
         weigh(0, slope[Bp], sq[Bp])
+        quantise_xm(Bp)
         gradient(Bp)
         quantise_g(Bp)
-        cast_xm(Bp)
-        quantise_xm(Bp)
-        for bh in (C, Dp):
-            for q in range(2):
-                scores(bh, q)
-            square(bh, 0, HALF)
+        square(C, 0, HALF)
+        for q in range(2):
+            scores(Dp, q)
+        square(Dp, 0, HALF)
         bank01 = psum.tile([P, HALF], F32, name="score01")
         product(bank01[:], 0, 1, 0, HALF)
         nc.scalar.copy(staged01, bank01[:])

@@ -76,8 +76,9 @@ def tile_attend_gsl2_w_kernel(tc, xT, wT, y, wt, xm, offs, out):
         nc.scalar.activation(centre[:], zero[:], ACT.Sigmoid)
 
         windows = [tile([P, T], F32, f"window{c}") for c in range(D // P)]
-        for window in windows:
-            nc.gpsimd.memset(window[:], 0.0)
+        nc.gpsimd.memset(windows[0][:], 0.0)
+        for window in windows[1:]:
+            nc.vector.memset(window[:].bitcast(mybir.dt.int32), 0)
 
         codes, scales = {}, {}
         for b in range(B):

from contextlib import ExitStack

import concourse.mybir as mybir

B, N, T, D, R = 2, 512, 2048, 512, 512
FLOPS = 2 * 2 * B * R * D * N

F32 = mybir.dt.float32
BF16 = mybir.dt.bfloat16
U32 = mybir.dt.uint32
U16 = mybir.dt.uint16
U8 = mybir.dt.uint8
E4M3 = mybir.dt.float8_e4m3fn_x4
E5M2 = mybir.dt.float8_e5m2_x4
ACT = mybir.ActivationFunctionType
ALU = mybir.AluOpType

P = 128
PACK = 4
HALF = N // 2
LIST_COLS = N // 16


def tile_attend_gsl2_w_kernel(tc, xT, wT, y, wt, xm, offs, out):
    nc = tc.nc
    with ExitStack() as ctx:
        keep = ctx.enter_context(tc.tile_pool(name="keep", bufs=1))
        reuse = ctx.enter_context(tc.tile_pool(name="reuse", bufs=1))
        psum = ctx.enter_context(tc.psum_pool(name="psum", bufs=1))

        def tile(shape, dtype, name):
            return keep.tile(shape, dtype, name=name, align_bytes=64)

        def tile_at(shape, dtype, name, kib):
            return reuse.tile(shape, dtype, name=name, align_bytes=64, offset=int(1024 * kib))[:]

        def flat(ap):
            return ap.rearrange("p c j -> p (c j)")

        def rows(src):
            return src.rearrange("(p j) w -> p j w", j=PACK)

        def half(h):
            return slice(h * HALF, (h + 1) * HALF)

        A, Bp, C, Dp = pieces = [(b, h) for b in range(B) for h in range(2)]
        offsets = keep.tile([P, B * LIST_COLS], U16, name="offsets")
        planes = [tile([P, T], F32, f"plane{t}") for t in range(PACK)]
        x_raw = [tile_at([P, PACK, R], F32, "x_raw0", 0), tile_at([P, PACK, R], F32, "x_raw1", 44)]
        xm0_raw = [tile([P, PACK, HALF], F32, f"xm0_raw{h}")[:] for h in range(2)]
        xm1_raw = [tile([P, PACK, HALF], F32, f"xm1_raw{h}")[:] for h in range(2)]
        y0_sb = [tile([P, PACK, HALF], F32, "y00")[:], tile_at([P, PACK, HALF], F32, "y01", 31.5)]
        y1_sb = [tile([P, PACK, HALF], F32, f"y1{h}")[:] for h in range(2)]
        xm_raw = {A: xm0_raw[0], Bp: xm0_raw[1], C: xm1_raw[0], Dp: xm1_raw[1]}
        y_sb = {A: y0_sb[0], Bp: y0_sb[1], C: y1_sb[0], Dp: y1_sb[1]}
        wt_sb = tile([P, B, PACK], F32, "wt_sb")

        for t in range(PACK):
            nc.sync.dma_start(out=planes[t][:], in_=rows(wT)[:, t, :])
            if t == 0:
                nc.sync.dma_start(offsets[:], offs)
        nc.sync.dma_start(out=x_raw[0], in_=rows(xT[0]))
        nc.sync.dma_start(out=x_raw[1], in_=rows(xT[1]))
        nc.sync.dma_start(out=y0_sb[0], in_=rows(y[0])[:, :, half(0)])
        nc.sync.dma_start(out=wt_sb[:], in_=wt.rearrange("b (p t) o -> p b (t o)", t=PACK))
        nc.sync.dma_start(out=xm0_raw[0], in_=rows(xm[0])[:, :, half(0)])
        nc.sync.dma_start(out=xm0_raw[1], in_=rows(xm[0])[:, :, half(1)])
        nc.sync.dma_start(out=y0_sb[1], in_=rows(y[0])[:, :, half(1)])
        for h in range(2):
            nc.sync.dma_start(out=xm1_raw[h], in_=rows(xm[1])[:, :, half(h)])
            nc.sync.dma_start(out=y1_sb[h], in_=rows(y[1])[:, :, half(h)])

        zero = tile([P, 1], F32, "zero")
        centre = tile([P, 1], F32, "centre")
        nc.gpsimd.memset(zero[:], 0.0)
        nc.scalar.activation(centre[:], zero[:], ACT.Sigmoid)

        windows = [tile([P, T], F32, f"window{c}") for c in range(D // P)]
        nc.gpsimd.memset(windows[0][:], 0.0)
        for window in windows[1:]:
            nc.vector.memset(window[:].bitcast(mybir.dt.int32), 0)

        codes, scales = {}, {}
        for b in range(B):
            for kind in ("w", "x", "xm", "g"):
                if (kind, b) not in (("w", 1), ("x", 1)):
                    codes[kind, b] = tile([P, 512], U32, f"{kind}_codes{b}")[:]
                scales[kind, b] = tile([P, 512], U8, f"{kind}_scales{b}")[:]
        w_codes = {A: codes["w", 0][:, half(0)], Bp: codes["w", 0][:, half(1)]}
        w_codes[C] = tile_at([P, HALF], U32, "w_codesC", 2)
        w_codes[Dp] = tile([P, HALF], U32, "w_codesD")[:]

        big = [P, PACK, HALF]
        packed = [P, HALF, PACK]
        picked = {bh: tile(packed, BF16, f"picked{bh[0]}{bh[1]}")[:] for bh in (A, Bp, C)}
        picked[Dp] = tile_at(packed, BF16, "pickedD", 0)
        plain = tile([P, PACK, N], BF16, "plain")
        x0_bf = [tile([P, 2 * P * PACK], BF16, "x0_bf0")[:], tile_at([P, 2 * P * PACK], BF16, "x0_bf1", 8)]
        x1_bf = tile_at([P, R * PACK], BF16, "x1_bf", 10)
        work1 = tile_at([P, 14 * HALF], F32, "work1", 18)
        g0_bf = tile_at([P, N, PACK], BF16, "g0_bf", 37)
        prob = {bh: tile(big, F32, f"prob{bh[0]}{bh[1]}")[:] for bh in (Bp, C, Dp)}
        prob[A] = tile_at(big, F32, "probA", 56)
        codes["x", 1] = tile_at([P, 512], U32, "x_codes1", 56)
        sq = {A: tile(big, F32, "sqA")[:], Bp: tile(big, F32, "sqB")[:], C: tile(big, F32, "sqC")[:], Dp: tile_at(big, F32, "sqD", 52)}
        slope = {A: sq[A], Bp: sq[Bp], C: work1[:, 10 * HALF :].rearrange("p (j c) -> p j c", j=PACK), Dp: work1[:, : 4 * HALF].rearrange("p (j c) -> p j c", j=PACK)}
        err = {A: y_sb[A], Bp: tile_at(big, F32, "errB", 44), C: tile_at(big, F32, "errC", 40.5), Dp: work1[:, 4 * HALF : 8 * HALF].rearrange("p (j c) -> p j c", j=PACK)}
        g_bf = {A: g0_bf[:, half(0), :], Bp: g0_bf[:, half(1), :], C: tile(packed, BF16, "g_bfC")[:], Dp: tile_at(packed, BF16, "g_bfD", 16)}
        xm_bf = {A: tile_at(packed, BF16, "xm_bfA", 8), Bp: tile(packed, BF16, "xm_bfB")[:]}
        xm_bf13 = work1[:, 9 * HALF : 10 * HALF].bitcast(BF16).rearrange("p (c j) -> p c j", j=PACK)
        xm_bf10 = tile_at([P, P, PACK], BF16, "xm_bf10", 37)
        xm_bf11 = work1[:, 8 * HALF : 9 * HALF].bitcast(BF16).rearrange("p (c j) -> p c j", j=PACK)
        early = {bh: tile([P, 1 + bh[1], HALF], F32, f"early{bh[0]}{bh[1]}")[:] for bh in pieces}
        staged01 = tile([P, HALF], F32, "staged01")[:]
        staged_a = {3: tile_at([P, HALF], F32, "staged_a3", 31.5), 2: tile_at([P, HALF], F32, "staged_a2", 32.5)}
        xm_bf12 = tile_at([P, P, PACK], BF16, "xm_bf12", 17.5)
        staged11 = tile_at([P, HALF], F32, "staged11", 52)
        staged02 = tile_at([P, HALF], F32, "staged02", 16.5)
        staged3 = tile_at([P, HALF + N], F32, "staged3", 13.5)
        staged12 = tile([P, N], F32, "staged12")[:]

        def slots(lo, hi):
            return offsets[:, lo // 16 : hi // 16]

        def by_fours_src(ap):
            return ap.rearrange("p j (c i) -> p c j i", i=4)

        def by_fours_dst(ap):
            return ap.rearrange("p (c i) j -> p c j i", i=4)

        def quantise(kind, b, src, lo, hi, fmt):
            nc.vector.quantize_mx(out=codes[kind, b][:, lo:hi].bitcast(fmt), scales=scales[kind, b][:, lo:hi], in_=src)

        def cast_x(b, dst, u, lo, hi, copy):
            copy(
                dst.rearrange("p (e m j) -> p m j e", e=2, j=PACK)[:, lo:hi],
                x_raw[b].rearrange("p j (m u e) -> p u m j e", u=2, e=2)[:, u, lo:hi],
            )

        def cast_xm(bh, copy):
            copy(by_fours_dst(xm_bf[bh]), by_fours_src(xm_raw[bh]))

        def cast_aside(dst, src):
            nc.gpsimd.tensor_scalar(dst, src.rearrange("p j c -> p c j"), 1.0, 0.0, ALU.mult, ALU.add)

        def quantise_xm(bh):
            quantise("xm", bh[0], flat(xm_bf[bh]), bh[1] * HALF, (bh[1] + 1) * HALF, E4M3)

        def scores(bh, q):
            b, h = bh
            bank = psum.tile([P, PACK, P], F32, name=f"score{h}{q}")
            cols = slice(h * HALF + q * P, h * HALF + (q + 1) * P)
            for t in range(PACK):
                nc.tensor.matmul_mx(
                    out=bank[:, t, :],
                    lhsT=codes["x", b][:, t * P : (t + 1) * P].bitcast(E4M3),
                    lhsT_scale=scales["x", b][:, t * P : (t + 1) * P],
                    rhs=w_codes[bh][:, q * P : (q + 1) * P].bitcast(E4M3),
                    rhs_scale=scales["w", b][:, cols],
                    start=True,
                    stop=True,
                )
            nc.scalar.activation(prob[bh][:, :, q * P : (q + 1) * P], bank[:], ACT.Sigmoid)

        def square(bh, lo, hi):
            nc.scalar.activation(sq[bh][:, :, lo:hi], prob[bh][:, :, lo:hi], ACT.Square, bias=centre[:] if bh == Bp else 0.5, scale=-1.0)

        def error(bh, engine, cols=slice(0, HALF)):
            engine.tensor_tensor(err[bh][:, :, cols], y_sb[bh][:, :, cols], prob[bh][:, :, cols], ALU.subtract)

        def weigh(b, dst, src):
            for t in range(PACK):
                nc.vector.tensor_scalar(dst[:, t, :], src[:, t, :], 0.25, wt_sb[:, b, t : t + 1], ALU.subtract, ALU.mult)

        def quantise_w(bh):
            nc.vector.quantize_mx(out=w_codes[bh].bitcast(E4M3), scales=scales["w", bh[0]][:, half(bh[1])], in_=flat(picked[bh]))

        def weave(bh):
            nc.scalar.copy(by_fours_dst(picked[bh]), by_fours_src(plain[:, :, half(bh[1])]))

        def gradient(bh, cols=slice(0, HALF)):
            nc.vector.tensor_tensor(
                by_fours_dst(g_bf[bh][:, cols, :]), by_fours_src(slope[bh][:, :, cols]), by_fours_src(err[bh][:, :, cols]), ALU.mult
            )

        def quantise_g(bh):
            quantise("g", bh[0], flat(g_bf[bh]), bh[1] * HALF, (bh[1] + 1) * HALF, E5M2)

        def product(dst, b, c, lo, hi):
            nc.tensor.matmul_mx(
                out=dst,
                lhsT=codes["xm", b][:, c * P : (c + 1) * P].bitcast(E4M3),
                lhsT_scale=scales["xm", b][:, c * P : (c + 1) * P],
                rhs=codes["g", b][:, lo:hi].bitcast(E5M2),
                rhs_scale=scales["g", b][:, lo:hi],
                start=True,
                stop=True,
            )

        def scatter_act(c, lo, hi, src):
            nc.scalar.activation(windows[c][:].indirect(slots(lo, hi)), src, ACT.Copy)

        def scatter_vec(c, lo, hi, src):
            nc.vector.tensor_copy(windows[c][:].indirect(slots(lo, hi)), src)

        def store(c):
            nc.sync.dma_start(out=out[c * P : (c + 1) * P, :], in_=windows[c][:])

        def early_blocks(bh, blocks):
            b, h = bh
            bank = psum.tile([P, blocks, HALF], F32, name=f"grad{h}")
            for c in range(blocks):
                product(bank[:, c, :], b, c, h * HALF, (h + 1) * HALF)
            nc.scalar.copy(early[bh], bank[:])
            for c in range(blocks):
                scatter_act(c, b * N + h * HALF, b * N + (h + 1) * HALF, early[bh][:, c, :])

        def block(b, c, name):
            bank = psum.tile([P, N], F32, name=name)
            product(bank[:], b, c, 0, N)
            return bank

        for t in range(PACK):
            for bh in (A, Bp):
                nc.vector.tensor_copy(picked[bh][:, :, t], planes[t][:].indirect(slots(bh[1] * HALF, (bh[1] + 1) * HALF)))
            nc.scalar.activation(plain[:, t, :], planes[t][:].indirect(slots(N, 2 * N)), ACT.Copy)
        quantise_w(A)
        quantise_w(Bp)
        weave(C)
        cast_x(0, x0_bf[0], 0, 0, P, nc.vector.tensor_copy)
        cast_x(0, x0_bf[1], 1, 0, 80, nc.scalar.copy)
        cast_x(0, x0_bf[1], 1, 80, P, nc.vector.tensor_copy)
        for u in range(2):
            quantise("x", 0, x0_bf[u], u * 256, (u + 1) * 256, E4M3)
        weave(Dp)
        quantise_w(C)
        quantise_w(Dp)
        for u in range(2):
            cast_x(1, x1_bf[:, u * 1024 : (u + 1) * 1024], u, 0, P, nc.vector.tensor_copy)
        for q in range(2):
            scores(A, q)
        for q in range(2):
            square(A, q * P, (q + 1) * P)
        error(A, nc.vector)
        weigh(0, slope[A], sq[A])
        quantise("x", 1, x1_bf, 0, R, E4M3)
        for q in range(2):
            scores(Bp, q)
        cast_xm(A, nc.scalar.copy)
        gradient(A)
        quantise_xm(A)
        quantise_g(A)
        square(Bp, 0, HALF)
        for q in range(2):
            scores(C, q)
        cast_xm(Bp, nc.vector.tensor_copy)
        early_blocks(A, 1)
        error(Bp, nc.vector)
        weigh(0, slope[Bp], sq[Bp])
        quantise_xm(Bp)
        gradient(Bp)
        quantise_g(Bp)
        square(C, 0, HALF)
        for q in range(2):
            scores(Dp, q)
        square(Dp, 0, HALF)
        bank01 = psum.tile([P, HALF], F32, name="score01")
        product(bank01[:], 0, 1, 0, HALF)
        nc.scalar.copy(staged01, bank01[:])
        scatter_act(1, 0, HALF, staged01)
        early_blocks(Bp, 2)

        late = {}
        for bh in (A, Bp):
            late[bh] = psum.tile([P, 2, HALF], F32, name=f"late{bh[1]}")
            for k, c in enumerate((2, 3)):
                product(late[bh][:, k, :], 0, c, bh[1] * HALF, (bh[1] + 1) * HALF)
        for c in (3, 2):
            nc.vector.tensor_copy(staged_a[c], late[A][:, c - 2, :])
        for c in (3, 2):
            scatter_vec(c, 0, HALF, staged_a[c])
        cast_aside(xm_bf10, xm_raw[C][:, :, :P])
        error(C, nc.gpsimd)

        weigh(1, slope[C], sq[C])
        gradient(C)
        quantise_g(C)
        nc.vector.tensor_copy(by_fours_dst(xm_bf11), by_fours_src(xm_raw[C][:, :, P:]))
        quantise("xm", 1, flat(xm_bf10), 0, P, E4M3)
        quantise("xm", 1, flat(xm_bf11), P, 2 * P, E4M3)
        early_blocks(C, 1)
        bank11 = psum.tile([P, HALF], F32, name="score00")
        product(bank11[:], 1, 1, 0, HALF)
        error(Dp, nc.vector)
        weigh(1, slope[Dp], sq[Dp])
        gradient(Dp)
        quantise_g(Dp)
        cast_aside(xm_bf12, xm_raw[Dp][:, :, :P])
        nc.vector.tensor_copy(by_fours_dst(xm_bf13), by_fours_src(xm_raw[Dp][:, :, P:]))
        quantise("xm", 1, flat(xm_bf13), 3 * P, 4 * P, E4M3)
        nc.vector.tensor_copy(staged11, bank11[:])
        scatter_vec(1, N, N + HALF, staged11)
        nc.scalar.copy(staged3[:, :HALF], late[Bp][:, 1, :])
        early_blocks(Dp, 2)
        store(0)
        store(1)

        nc.vector.tensor_copy(staged02, late[Bp][:, 0, :])
        nc.vector.tensor_copy(staged3[:, HALF:], block(1, 3, "score10")[:])
        quantise("xm", 1, flat(xm_bf12), 2 * P, 3 * P, E4M3)
        scatter_vec(2, HALF, N, staged02)
        nc.vector.tensor_copy(staged12, block(1, 2, "score11")[:])
        scatter_act(3, HALF, N + P, staged3[:, : HALF + P])
        scatter_act(3, N + P, 2 * N, staged3[:, HALF + P :])
        scatter_vec(2, N, 2 * N, staged12)
        store(2)
        store(3)
